import numpy as np
import ml_dtypes


def mxq(x, axis, fmt="e4m3"):
    dtype, down = {"e4m3": (ml_dtypes.float8_e4m3fn, 7), "e5m2": (ml_dtypes.float8_e5m2, 14)}[fmt]
    v = np.moveaxis(np.asarray(x, np.float32).astype(ml_dtypes.bfloat16).astype(np.float64), axis, -1)
    blocks = v.reshape(v.shape[:-1] + (-1, 32))
    amax = np.abs(blocks).max(-1, keepdims=True)
    byte = np.maximum(np.where(amax > 0, np.frexp(amax)[1] - 1 + 127, 0) - down, 1)
    scale = np.exp2(byte - 127.0)
    codes = (blocks / scale).astype(np.float32).astype(dtype).astype(np.float64)
    return np.moveaxis((codes * scale).reshape(v.shape), -1, axis)


WIDE = False


def mx_kscale(k):
    if not WIDE:
        return np.ones(k)
    levels = np.array([10, -10, 5, -5, 0])
    if k % 512:
        return np.exp2(np.random.permutation(np.resize(levels, k // 32))).repeat(32)
    a = np.empty((k // 512, 16))
    for p in range(k // 512):
        a[p, :8] = np.random.permutation(np.resize(levels, 8))
        for g in range(8):
            far = levels[np.abs(levels - a[p, g]) >= 10]
            a[p, g + 8] = far[np.random.randint(len(far))]
    return np.exp2(a.ravel()).repeat(32)


def f64(x):
    return np.asarray(x).astype(np.float64)


def striped(idx):
    return np.tile(idx.reshape(-1, 16).T, (8, 1)).astype(np.uint16)


def unstriped(offs):
    return offs[:16].T.reshape(-1).astype(np.int64)


E2M1 = np.array([0.0, 0.5, 1.0, 1.5, 2.0, 3.0, 4.0, 6.0, -0.0, -0.5, -1.0, -1.5, -2.0, -3.0, -4.0, -6.0])


def pack_weight(w, fmt):
    k, n = w.shape
    w = f64(np.asarray(w, np.float32).astype(ml_dtypes.bfloat16)).reshape(k // 32, 32, n)
    amax = np.abs(w).max(1)
    if fmt == "e4m3":
        byte = np.frexp(amax)[1] - 1 + 127 - 7
    else:
        mant, ex = np.frexp(amax / 6.0)
        byte = np.where(mant > 0.5, ex, ex - 1) + 127
    byte = np.clip(np.where(amax > 0, byte, 1), 1, 254)
    scaled = (w * np.exp2(127.0 - byte)[:, None, :]).reshape(k, n).astype(np.float32)
    by_word = np.ascontiguousarray(scaled.reshape(k // 512, 128, 4, n).transpose(0, 1, 3, 2))
    if fmt == "e4m3":
        words = by_word.astype(ml_dtypes.float8_e4m3fn).view(np.uint8)
    else:
        c = by_word.astype(ml_dtypes.float4_e2m1fn).view(np.uint8) & 0xF
        words = (c[..., 0::2] | (c[..., 1::2] << 4)).reshape(k // 512, 128, 2 * n)
    return np.ascontiguousarray(words), np.ascontiguousarray(byte.astype(np.uint8).reshape(k // 512, 16, n))


def unpack_weight(words, scales, fmt):
    g, _, n = scales.shape
    words = np.ascontiguousarray(words).reshape(g, 128, n, -1)
    if fmt == "e4m3":
        vals = words.view(ml_dtypes.float8_e4m3fn).astype(np.float64)
    else:
        nib = np.empty((g, 128, n, 4), np.uint8)
        nib[..., 0::2] = words & 0xF
        nib[..., 1::2] = words >> 4
        vals = E2M1[nib]
    vals = vals * np.repeat(np.exp2(scales.astype(np.float64) - 127.0), 8, axis=1)[..., None]
    return vals.transpose(0, 1, 3, 2).reshape(g * 512, n)


def gelu(v):
    return 0.5 * v * (1.0 + np.tanh(np.sqrt(2.0 / np.pi) * (v + 0.044715 * v**3)))


def striped8(idx):
    return np.concatenate([v.reshape(-1, 16).T for v in idx]).astype(np.uint16)


def unstriped8(offs):
    return np.stack([offs[16 * g:16 * g + 16].T.reshape(-1) for g in range(8)]).astype(np.int64)


def put_heads(h, wgs, idx8, t2):
    r = np.arange(h.shape[0])
    page = np.zeros((h.shape[0], t2))
    page[r[:, None], idx8[r % 512 // 64]] = wgs[r // 4 % 128] * h
    return page


K, T, S, H, T2, N = 1024, 2048, 512, 1024, 1024, 768

def setup_inputs():
    n = np.random.standard_normal
    s = mx_kscale(K)[:, None]
    u = mx_kscale(H)[:, None]
    tab_words, tab_scales = pack_weight(n((K, T)) * s, "e4m3")
    w4_words, w4_scales = pack_weight(n((K, H)) / np.sqrt(K) / s, "e2m1")
    w8_words, w8_scales = pack_weight(1.5 * n((H, N)) / np.sqrt(H) / u, "e4m3")
    return {
        "tab_words": tab_words, "tab_scales": tab_scales,
        "offs": striped(np.random.permutation(T)[:S]),
        "wg": (1.5 * n((K, H)) / np.sqrt(K) / s).astype(np.float32),
        "w4_words": w4_words, "w4_scales": w4_scales,
        "gain": (np.random.uniform(1.0, 3.0, H) * u[:, 0]).astype(np.float32),
        "wgs": np.repeat(np.random.uniform(0.5, 2.0, (8, S)), 16, axis=0).astype(np.float32),
        "offs2": striped8(np.stack([np.random.permutation(T2)[:S] for _ in range(8)])),
        "slot": (0.5 * n((H, T2)) * u).astype(np.float32),
        "w8_words": w8_words, "w8_scales": w8_scales,
        "wf": (1.5 * n((H, N)) / np.sqrt(H) / u).astype(np.float32),
    }

def reference(tab_words, tab_scales, offs, wg, w4_words, w4_scales, gain, wgs, offs2, slot, w8_words, w8_scales, wf):
    v = unpack_weight(tab_words, tab_scales, "e4m3")[:, unstriped(offs)]
    a = mxq(f64(wg), 0, "e4m3").T @ v
    b = unpack_weight(w4_words, w4_scales, "e2m1").T @ v
    h = f64(gain)[:, None] / (1.0 + np.exp(-a)) * np.tanh(b)
    page = put_heads(h, f64(wgs), unstriped8(offs2), T2)
    z = mxq(page + f64(slot), 0, "e4m3")
    val = unpack_weight(w8_words, w8_scales, "e4m3").T @ z
    sel = mxq(f64(wf), 0, "e4m3").T @ z
    return val * (sel / (1.0 + np.exp(-sel)))

@@ -1,0 +1,364 @@
+from contextlib import ExitStack
+
+import concourse.mybir as mybir
+from concourse.masks import make_identity
+
+K, T, S, H, T2, N = 1024, 2048, 512, 1024, 1024, 768
+FLOPS = 2 * (2 * K * H * S + 2 * H * N * T2)
+
+F32 = mybir.dt.float32
+BF16 = mybir.dt.bfloat16
+I32 = mybir.dt.int32
+U32 = mybir.dt.uint32
+U16 = mybir.dt.uint16
+U8 = mybir.dt.uint8
+FP8X4 = mybir.dt.float8_e4m3fn_x4
+FP4X4 = mybir.dt.float4_e2m1fn_x4
+ACT = mybir.ActivationFunctionType
+MULT = mybir.AluOpType.mult
+ADD = mybir.AluOpType.add
+
+P = 128
+PASS = 512
+BANK = 512
+AL = 64
+PAGES = 6
+
+
+def tile_list_feed_slot_ranking_kernel(
+    tc, tab_words, tab_scales, offs, wg, w4_words, w4_scales, gain, wgs, offs2, slot, w8_words, w8_scales, wf, out
+):
+    nc = tc.nc
+    with ExitStack() as ctx:
+        lists = ctx.enter_context(tc.tile_pool(name="lists", bufs=1))
+        sb = ctx.enter_context(tc.tile_pool(name="sb", bufs=1))
+        psum = ctx.enter_context(tc.psum_pool(name="psum", bufs=1))
+
+        def new(name, shape, dtype, tag=None):
+            return sb.tile(shape, dtype, name=name, tag=tag or name, align_bytes=AL)
+
+        banks = [psum.tile([P, BANK], F32, name=f"bank{i}") for i in range(8)]
+
+        idx = lists.tile([P, S // 16], U16, name="idx")
+        idx2 = lists.tile([P, S // 16], U16, name="idx2")
+
+        def load_scale_rows(plane, scales):
+            for q in range(4):
+                nc.sync.dma_start(
+                    out=plane[32 * q : 32 * q + 4].bitcast(I32),
+                    in_=scales.bitcast(I32)[:, 4 * q : 4 * q + 4, :].rearrange("a r n -> r a n"),
+                )
+
+        tab_s = new("tab_s", [P, 2, T], U8)
+        w4_s = new("w4_s", [P, 2, H], U8)
+        w8_s = new("w8_s", [P, 2, N], U8)
+        warm = new("warm", [P, 16], F32)
+        nc.vector.memset(tab_s[:].bitcast(I32), 0)
+        nc.vector.memset(w4_s[:].bitcast(I32), 0)
+        nc.vector.memset(w8_s[:].bitcast(I32), 0)
+        nc.vector.memset(warm[:, 0:8], 0.0)
+        nc.scalar.activation(warm[:, 8:16], warm[:, 0:8], ACT.Sigmoid)
+
+        ident = new("ident", [P, P], F32)
+        make_identity(nc, ident[:])
+        pages = [new(f"page{i}", [P, T2], F32) for i in range(PAGES)]
+        for page in pages:
+            nc.gpsimd.memset(page[:], 0.0)
+
+        def load_wg(b, a):
+            raw = new(f"wg_raw{b}{a}", [P, 4, PASS], F32, tag=f"raw{2 * b + a}")
+            nc.sync.dma_start(
+                out=raw[:],
+                in_=wg[PASS * a : PASS * (a + 1), PASS * b : PASS * (b + 1)].rearrange("(p j) c -> p j c", j=4),
+            )
+            return raw
+
+        def load_slot(b, u, tag):
+            raw = new(f"slot{b}{u}", [P, 2, T2], F32, tag=tag)
+            rows = slot[PASS * b : PASS * (b + 1), :].rearrange("(p i) m -> p i m", i=4)
+            nc.sync.dma_start(out=raw[:], in_=rows[:, 2 * u : 2 * u + 2, :])
+            return raw
+
+        def load_wf(b):
+            raw = new(f"wf_raw{b}", [P, 4, N], F32)
+            nc.sync.dma_start(out=raw[:], in_=wf[PASS * b : PASS * (b + 1), :].rearrange("(p j) c -> p j c", j=4))
+            return raw
+
+        def load_tab(a):
+            words = new(f"tab_w{a}", [P, T], U32)
+            nc.sync.dma_start(out=words[:].bitcast(I32), in_=tab_words[a].rearrange("p t i -> p (t i)").bitcast(I32))
+            return words
+
+        def load_w4(b):
+            words = new(f"w4_w{b}", [P, 2, 2 * PASS], U8)
+            part = w4_words.bitcast(I32)[:, :, PASS // 2 * b : PASS // 2 * (b + 1)]
+            nc.sync.dma_start(out=words[:].bitcast(I32), in_=part.rearrange("a p n -> p a n"))
+            return words
+
+        nc.sync.dma_start(idx[:], offs)
+        tab_w = [load_tab(0)]
+        load_scale_rows(tab_s, tab_scales)
+        w4_w = [load_w4(0)]
+        tab_w.append(load_tab(1))
+        load_scale_rows(w4_s, w4_scales)
+        wg_raw = {(0, a): load_wg(0, a) for a in range(2)}
+        wgs_sb = new("wgs_sb", [P, S], F32)
+        nc.sync.dma_start(out=wgs_sb[:], in_=wgs)
+        gain_sb = new("gain_sb", [P, 2, 4], F32)
+        nc.sync.dma_start(out=gain_sb[:], in_=gain.rearrange("(b p i) -> p b i", b=2, i=4))
+        nc.sync.dma_start(idx2[:], offs2)
+        w4_w.append(load_w4(1))
+        wg_raw[1, 0] = load_wg(1, 0)
+        wg_raw[1, 1] = load_wg(1, 1)
+        slot_sb = {(0, 0): load_slot(0, 0, "raw4")}
+        wf_raw = [load_wf(0), load_wf(1)]
+        slot_sb[0, 1] = load_slot(0, 1, "raw5")
+        w8_w = new("w8_w", [P, 2, N], U32)
+        nc.sync.dma_start(
+            out=w8_w[:].bitcast(I32), in_=w8_words.rearrange("a p n i -> p a (n i)").bitcast(I32)
+        )
+        load_scale_rows(w8_s, w8_scales)
+
+        v_w = [new(f"v_w{a}", [P, S], U32) for a in range(2)]
+        v_s = [new(f"v_s{a}", [P, S], U8) for a in range(2)]
+        nc.vector.tensor_copy(v_w[0][:], tab_w[0][:].indirect(idx[:]))
+        for a in range(2):
+            nc.vector.tensor_copy(v_s[a][:], tab_s[:, a, :].indirect(idx[:]))
+        nc.vector.tensor_copy(v_w[1][:], tab_w[1][:].indirect(idx[:]))
+
+        wg_w, wg_s = {}, {}
+
+        def round_wg(b, a, vector_from):
+            rounded = new(f"wg_bf{b}{a}", [P, 4 * PASS], BF16, tag=f"wg_bf{a}")
+            dst = rounded[:].rearrange("p (t m j) -> p m j t", t=4, j=4)
+            src = wg_raw[b, a][:].rearrange("p j (m t) -> p m j t", t=4)
+            if vector_from > 0:
+                nc.scalar.copy(dst[:, :vector_from], src[:, :vector_from])
+            if vector_from < P:
+                nc.vector.tensor_copy(dst[:, vector_from:], src[:, vector_from:])
+            return rounded
+
+        def quantize_wg(b, a, rounded, width):
+            wg_w[b, a] = new(f"wg_w{b}{a}", [P, PASS], U32)
+            wg_s[b, a] = new(f"wg_s{b}{a}", [P, PASS], U8)
+            for c in range(0, PASS, width):
+                nc.vector.quantize_mx(
+                    out=wg_w[b, a][:, c : c + width].bitcast(FP8X4),
+                    scales=wg_s[b, a][:, c : c + width],
+                    in_=rounded[:, 4 * c : 4 * (c + width)],
+                )
+
+        tanh_b, factor, gate = {}, {}, {}
+
+        def features(b):
+            cols = slice(PASS * b, PASS * (b + 1))
+            for a in range(2):
+                for jb in range(4):
+                    entries = slice(P * jb, P * (jb + 1))
+                    nc.tensor.matmul_mx(
+                        out=banks[4 + jb][:],
+                        lhsT=v_w[a][:, entries].bitcast(FP8X4),
+                        lhsT_scale=v_s[a][:, entries],
+                        rhs=w4_w[b][:, a, :].bitcast(FP4X4),
+                        rhs_scale=w4_s[:, a, cols],
+                        start=(a == 0),
+                        stop=(a == 1),
+                    )
+            for jb in range(4):
+                tanh_b[b, jb] = new(f"tanh{b}{jb}", [P, 4, P], F32, tag=f"tanh{jb}")
+                nc.scalar.activation(
+                    tanh_b[b, jb][:], banks[4 + jb][:].rearrange("j (m t) -> j t m", t=4), ACT.Tanh
+                )
+
+        def weigh(s, dst):
+            b, t = divmod(s, 4)
+            bank = banks[(0, 1, 0, 1, 1, 6, 7, 3)[s]]
+            for jb in range(4):
+                nc.tensor.transpose(bank[:, P * jb : P * (jb + 1)], tanh_b[b, jb][:, t, :], ident[:])
+            factor[s] = dst
+            nc.vector.scalar_tensor_tensor(dst, bank[:], gain_sb[:, b, t : t + 1], wgs_sb[:], MULT, MULT)
+
+        def row(name, tag=None):
+            return new(name, [P, S], F32, tag=tag)[:]
+
+        def sigmoid_gate(s, dst):
+            b, t = divmod(s, 4)
+            bank = banks[4 + s % (4 if b == 0 else 2)]
+            for a in range(2):
+                nc.tensor.matmul_mx(
+                    out=bank[:],
+                    lhsT=wg_w[b, a][:, P * t : P * (t + 1)].bitcast(FP8X4),
+                    lhsT_scale=wg_s[b, a][:, P * t : P * (t + 1)],
+                    rhs=v_w[a][:].bitcast(FP8X4),
+                    rhs_scale=v_s[a][:],
+                    start=(a == 0),
+                    stop=(a == 1),
+                )
+            gate[s] = dst
+            nc.scalar.activation(dst, bank[:], ACT.Sigmoid)
+
+        def scatter(s):
+            nc.vector.tensor_tensor(pages[s % PAGES][:].indirect(idx2[:]), gate[s], factor[s], MULT)
+
+        def add_slot_turned(b, u, use):
+            turned = new(f"turned{b}{u}", [P, 8, P, 2], BF16, tag=f"turned{u}")
+            for g in range(4):
+                bank = banks[use[g]]
+                for c2 in range(2):
+                    cols = slice(P * (2 * g + c2), P * (2 * g + c2 + 1))
+                    for e in range(2):
+                        dst = bank[:, P * (2 * c2 + e) : P * (2 * c2 + e + 1)]
+                        nc.tensor.matmul(
+                            dst, slot_sb[b, u][:, e, cols], ident[:], start=True, stop=False, is_transpose=True
+                        )
+                        nc.tensor.matmul(
+                            dst, pages[(4 * b + 2 * u + e) % PAGES][:, cols], ident[:], start=False, stop=True, is_transpose=True
+                        )
+                nc.scalar.copy(
+                    turned[:, 2 * g : 2 * g + 2], bank[:].rearrange("m (c e p) -> m c p e", c=2, e=2)
+                )
+            return turned[:].rearrange("m c p e -> m c (p e)").bitcast(F32)
+
+        wf_w = [new(f"wf_w{b}", [P, N], U32) for b in range(2)]
+        wf_s = [new(f"wf_s{b}", [P, N], U8) for b in range(2)]
+
+        def round_wf(b):
+            rounded = new(f"wf_bf{b}", [P, 4 * N], BF16)
+            dst = rounded[:].rearrange("p (c i j) -> p c j i", i=4, j=4)
+            src = wf_raw[b][:].rearrange("p j (c i) -> p c j i", i=4)
+            for c in range(0, N // 4, 64):
+                nc.scalar.copy(dst[:, c : c + 64], src[:, c : c + 64])
+            return rounded
+
+        def quantize_wf(b, rounded):
+            for c0, c1 in ((0, 512), (512, N)):
+                nc.vector.quantize_mx(
+                    out=wf_w[b][:, c0:c1].bitcast(FP8X4), scales=wf_s[b][:, c0:c1], in_=rounded[:, 4 * c0 : 4 * c1]
+                )
+
+        z_w = [new(f"z_w{b}", [P, T2], U32) for b in range(2)]
+        z_s = [new(f"z_s{b}", [P, T2], U8) for b in range(2)]
+
+        def quantize_z(b, z_bf, m0, m1):
+            nc.vector.quantize_mx(
+                out=z_w[b][:, m0:m1].bitcast(FP8X4), scales=z_s[b][:, m0:m1], in_=z_bf[:, 4 * m0 : 4 * m1]
+            )
+
+        quantize_wg(0, 0, round_wg(0, 0, 0), PASS)
+        features(0)
+        quantize_wg(0, 1, round_wg(0, 1, 32), P)
+        for s in range(2):
+            sigmoid_gate(s, row(f"gate{s}"))
+            weigh(s, row(f"factor{s}"))
+        for s in range(2, 4):
+            sigmoid_gate(s, row(f"gate{s}"))
+        for s in range(2):
+            scatter(s)
+        slot_sb[1, 0] = load_slot(1, 0, "raw0")
+        slot_sb[1, 1] = load_slot(1, 1, "raw1")
+        for a in range(2):
+            quantize_wg(1, a, round_wg(1, a, P), PASS)
+        late = new("factor23", [P, 2, S], F32, tag="wg_bf1")
+        for s in range(2, 4):
+            weigh(s, late[:, s - 2, :])
+        scatter(2)
+        features(1)
+        scatter(3)
+        turned0 = [add_slot_turned(0, 0, (2, 3, 2, 3))]
+        wf_bf = [round_wf(0)]
+        for s in range(4, 6):
+            sigmoid_gate(s, row(f"gate{s}"))
+            weigh(s, row(f"factor{s}"))
+            scatter(s)
+        wf_bf.append(round_wf(1))
+        sigmoid_gate(6, row("gate6"))
+        weigh(6, row("factor6"))
+        scatter(6)
+        for b in range(2):
+            quantize_wf(b, wf_bf[b])
+        turned0.append(add_slot_turned(0, 1, (2, 3, 0, 1)))
+        pairs = new("pairs", [P, 2, T2, 2], BF16, tag="raw3")
+        pair_words = pairs[:].rearrange("p u m e -> p u (m e)").bitcast(F32)
+
+        z_bf = new("z_bf0", [P, 4 * T2], BF16, tag="raw2")
+        for q in range(4):
+            bank = banks[q]
+            for u in range(2):
+                for c2 in range(2):
+                    nc.tensor.transpose(
+                        bank[:, P * (2 * u + c2) : P * (2 * u + c2 + 1)], turned0[u][:, 2 * q + c2, :], ident[:]
+                    )
+            nc.scalar.copy(
+                z_bf[:, 1024 * q : 1024 * (q + 1)].bitcast(F32).rearrange("p (m u) -> p m u", u=2),
+                bank[:].rearrange("p (u m) -> p m u", u=2),
+            )
+        for h in range(2):
+            quantize_z(0, z_bf, 512 * h, 512 * (h + 1))
+        sigmoid_gate(7, pair_words[:, 1, 0:S])
+        weigh(7, pair_words[:, 1, S : 2 * S])
+        scatter(7)
+
+        turned1 = add_slot_turned(1, 0, (0, 1, 2, 0))
+        for h in range(2):
+            bank = banks[6 + h]
+            for c in range(4):
+                nc.tensor.transpose(bank[:, P * c : P * (c + 1)], turned1[:, 4 * h + c, :], ident[:])
+            nc.scalar.copy(pair_words[:, 0, 512 * h : 512 * (h + 1)], bank[:])
+
+        nc.scalar.activation(warm[:, 8:16], pairs[:, 0, T2 - 8 :, 0], ACT.Silu)
+        units = [(h, n) for h in range(2) for n in range(N // P)]
+
+        def product(k, b, m0, m1, start, stop, which=(0, 1)):
+            h, n = units[k]
+            cols = slice(P * n, P * (n + 1))
+            moving = slice(512 * h + m0, 512 * h + m1)
+            weights = ((wf_w[b][:, cols], wf_s[b][:, cols]), (w8_w[:, b, cols], w8_s[:, b, cols]))
+            for i in which:
+                bank, (words, plane) = banks[2 * (k % 4) + i], weights[i]
+                nc.tensor.matmul_mx(
+                    out=bank[:, m0:m1],
+                    lhsT=words.bitcast(FP8X4),
+                    lhsT_scale=plane,
+                    rhs=z_w[b][:, moving].bitcast(FP8X4),
+                    rhs_scale=z_s[b][:, moving],
+                    start=start,
+                    stop=stop,
+                )
+
+        def finish(k):
+            h, n = units[k]
+            silu = new(f"silu{k}", [P, 512], F32, tag=f"gate{k % 4}")
+            nc.scalar.activation(silu[:], banks[2 * (k % 4)][:], ACT.Silu)
+            result = new(f"result{k}", [P, 512], F32, tag=f"tanh{k % 4}")
+            nc.vector.tensor_tensor(result[:], banks[2 * (k % 4) + 1][:], silu[:], MULT)
+            nc.sync.dma_start(out=out[P * n : P * (n + 1), 512 * h : 512 * (h + 1)], in_=result[:])
+
+        for k in range(4):
+            product(k, 0, 0, 512, True, False)
+
+        z_bf = new("z_bf1", [P, 4 * T2], BF16, tag="wf_raw0")
+
+        def last_pair(q):
+            cols = slice(256 * q, 256 * (q + 1))
+            for e in range(2):
+                nc.vector.tensor_tensor(pairs[:, 1, cols, e], pages[(6 + e) % PAGES][:, cols], slot_sb[1, 1][:, e, cols], ADD)
+            weave = nc.vector.tensor_copy if q < 2 else nc.scalar.copy
+            weave(
+                z_bf[:, 1024 * q : 1024 * (q + 1)].bitcast(F32).rearrange("p (m u) -> p m u", u=2),
+                pair_words[:, :, cols].rearrange("p u m -> p m u"),
+            )
+
+        for q in range(2):
+            last_pair(q)
+            quantize_z(1, z_bf, 256 * q, 256 * (q + 1))
+            for k in range(4):
+                product(k, 1, 256 * q, 256 * (q + 1), False, q == 1)
+        for q in range(2, 4):
+            last_pair(q)
+        quantize_z(1, z_bf, 512, 1024)
+        for k in range(len(units)):
+            if k >= 4:
+                for i in range(2):
+                    product(k, 0, 0, 512, True, False, (i,))
+                    product(k, 1, 0, 512, False, True, (i,))
+            finish(k)

@@ -22,7 +22,7 @@ P = 128
 PASS = 512
 BANK = 512
 AL = 64
-PAGES = 6
+PAGES = 4
 
 
 def tile_list_feed_slot_ranking_kernel(
@@ -63,7 +63,7 @@ def tile_list_feed_slot_ranking_kernel(
         make_identity(nc, ident[:])
         pages = [new(f"page{i}", [P, T2], F32) for i in range(PAGES)]
         for page in pages:
-            nc.gpsimd.memset(page[:], 0.0)
+            nc.vector.memset(page[:], 0.0)
 
         def load_wg(b, a):
             raw = new(f"wg_raw{b}{a}", [P, 4, PASS], F32, tag=f"raw{2 * b + a}")
@@ -100,8 +100,9 @@ def tile_list_feed_slot_ranking_kernel(
         load_scale_rows(tab_s, tab_scales)
         w4_w = [load_w4(0)]
         tab_w.append(load_tab(1))
+        wg_raw = {(0, 0): load_wg(0, 0)}
         load_scale_rows(w4_s, w4_scales)
-        wg_raw = {(0, a): load_wg(0, a) for a in range(2)}
+        wg_raw[0, 1] = load_wg(0, 1)
         wgs_sb = new("wgs_sb", [P, S], F32)
         nc.sync.dma_start(out=wgs_sb[:], in_=wgs)
         gain_sb = new("gain_sb", [P, 2, 4], F32)
@@ -172,7 +173,7 @@ def tile_list_feed_slot_ranking_kernel(
 
         def weigh(s, dst):
             b, t = divmod(s, 4)
-            bank = banks[(0, 1, 0, 1, 1, 6, 7, 3)[s]]
+            bank = banks[(0, 1, 0, 1, 1, 6, 7, 2)[s]]
             for jb in range(4):
                 nc.tensor.transpose(bank[:, P * jb : P * (jb + 1)], tanh_b[b, jb][:, t, :], ident[:])
             factor[s] = dst
@@ -236,17 +237,15 @@ def tile_list_feed_slot_ranking_kernel(
                     out=wf_w[b][:, c0:c1].bitcast(FP8X4), scales=wf_s[b][:, c0:c1], in_=rounded[:, 4 * c0 : 4 * c1]
                 )
 
-        z_w = [new(f"z_w{b}", [P, T2], U32) for b in range(2)]
+        z_w = {}
         z_s = [new(f"z_s{b}", [P, T2], U8) for b in range(2)]
 
-        def quantize_z(b, z_bf, m0, m1):
-            nc.vector.quantize_mx(
-                out=z_w[b][:, m0:m1].bitcast(FP8X4), scales=z_s[b][:, m0:m1], in_=z_bf[:, 4 * m0 : 4 * m1]
-            )
+        def quantize_z(b, woven, m0, m1):
+            nc.vector.quantize_mx(out=z_w[b][:, m0:m1].bitcast(FP8X4), scales=z_s[b][:, m0:m1], in_=woven)
 
-        quantize_wg(0, 0, round_wg(0, 0, 0), PASS)
+        quantize_wg(0, 0, round_wg(0, 0, 48), PASS)
         features(0)
-        quantize_wg(0, 1, round_wg(0, 1, 32), P)
+        quantize_wg(0, 1, round_wg(0, 1, 0), P)
         for s in range(2):
             sigmoid_gate(s, row(f"gate{s}"))
             weigh(s, row(f"factor{s}"))
@@ -264,7 +263,7 @@ def tile_list_feed_slot_ranking_kernel(
         scatter(2)
         features(1)
         scatter(3)
-        turned0 = [add_slot_turned(0, 0, (2, 3, 2, 3))]
+        turned0 = [add_slot_turned(0, 0, (2, 3, 6, 7))]
         wf_bf = [round_wf(0)]
         for s in range(4, 6):
             sigmoid_gate(s, row(f"gate{s}"))
@@ -273,14 +272,16 @@ def tile_list_feed_slot_ranking_kernel(
         wf_bf.append(round_wf(1))
         sigmoid_gate(6, row("gate6"))
         weigh(6, row("factor6"))
-        scatter(6)
         for b in range(2):
             quantize_wf(b, wf_bf[b])
         turned0.append(add_slot_turned(0, 1, (2, 3, 0, 1)))
+        scatter(6)
         pairs = new("pairs", [P, 2, T2, 2], BF16, tag="raw3")
         pair_words = pairs[:].rearrange("p u m e -> p u (m e)").bitcast(F32)
 
         z_bf = new("z_bf0", [P, 4 * T2], BF16, tag="raw2")
+        woven0 = [z_bf[:, 1024 * q : 1024 * (q + 1)] for q in range(4)]
+        woven0[0] = pairs[:, 1, 512:1024, :].rearrange("p m e -> p (m e)")
         for q in range(4):
             bank = banks[q]
             for u in range(2):
@@ -289,16 +290,19 @@ def tile_list_feed_slot_ranking_kernel(
                         bank[:, P * (2 * u + c2) : P * (2 * u + c2 + 1)], turned0[u][:, 2 * q + c2, :], ident[:]
                     )
             nc.scalar.copy(
-                z_bf[:, 1024 * q : 1024 * (q + 1)].bitcast(F32).rearrange("p (m u) -> p m u", u=2),
+                woven0[q].bitcast(F32).rearrange("p (m u) -> p m u", u=2),
                 bank[:].rearrange("p (u m) -> p m u", u=2),
             )
-        for h in range(2):
-            quantize_z(0, z_bf, 512 * h, 512 * (h + 1))
         sigmoid_gate(7, pair_words[:, 1, 0:S])
-        weigh(7, pair_words[:, 1, S : 2 * S])
+        turned1 = add_slot_turned(1, 0, (0, 1, 2, 3))
+        weigh(7, row("factor7", "z_w0"))
         scatter(7)
+        z_w[0] = new("z_w0", [P, T2], U32)
+        z_w[1] = new("z_w1", [P, T2], U32)
+        for q in range(2):
+            quantize_z(0, woven0[q], 256 * q, 256 * (q + 1))
+        z_rest = z_bf[:, 2048:]
 
-        turned1 = add_slot_turned(1, 0, (0, 1, 2, 0))
         for h in range(2):
             bank = banks[6 + h]
             for c in range(4):
@@ -350,12 +354,13 @@ def tile_list_feed_slot_ranking_kernel(
 
         for q in range(2):
             last_pair(q)
-            quantize_z(1, z_bf, 256 * q, 256 * (q + 1))
+            quantize_z(1, z_bf[:, 1024 * q : 1024 * (q + 1)], 256 * q, 256 * (q + 1))
             for k in range(4):
                 product(k, 1, 256 * q, 256 * (q + 1), False, q == 1)
         for q in range(2, 4):
             last_pair(q)
-        quantize_z(1, z_bf, 512, 1024)
+        quantize_z(0, z_rest, 512, 1024)
+        quantize_z(1, z_bf[:, 2048:], 512, 1024)
         for k in range(len(units)):
             if k >= 4:
                 for i in range(2):

@@ -173,7 +173,7 @@ def tile_list_feed_slot_ranking_kernel(
 
         def weigh(s, dst):
             b, t = divmod(s, 4)
-            bank = banks[(0, 1, 0, 1, 1, 6, 7, 2)[s]]
+            bank = banks[(0, 1, 0, 1, 1, 6, 7, 4)[s]]
             for jb in range(4):
                 nc.tensor.transpose(bank[:, P * jb : P * (jb + 1)], tanh_b[b, jb][:, t, :], ident[:])
             factor[s] = dst
@@ -203,39 +203,37 @@ def tile_list_feed_slot_ranking_kernel(
 
         def add_slot_turned(b, u, use):
             turned = new(f"turned{b}{u}", [P, 8, P, 2], BF16, tag=f"turned{u}")
+            for e in range(2):
+                for c in range(8):
+                    cols = slice(P * c, P * (c + 1))
+                    place = 2 * (c % 2) + e
+                    dst = banks[use[c // 2]][:, P * place : P * (place + 1)]
+                    page = pages[(4 * b + 2 * u + e) % PAGES]
+                    nc.tensor.matmul(
+                        dst, slot_sb[b, u][:, e, cols], ident[:], start=True, stop=False, is_transpose=True
+                    )
+                    nc.tensor.matmul(dst, page[:, cols], ident[:], start=False, stop=True, is_transpose=True)
             for g in range(4):
-                bank = banks[use[g]]
-                for c2 in range(2):
-                    cols = slice(P * (2 * g + c2), P * (2 * g + c2 + 1))
-                    for e in range(2):
-                        dst = bank[:, P * (2 * c2 + e) : P * (2 * c2 + e + 1)]
-                        nc.tensor.matmul(
-                            dst, slot_sb[b, u][:, e, cols], ident[:], start=True, stop=False, is_transpose=True
-                        )
-                        nc.tensor.matmul(
-                            dst, pages[(4 * b + 2 * u + e) % PAGES][:, cols], ident[:], start=False, stop=True, is_transpose=True
-                        )
                 nc.scalar.copy(
-                    turned[:, 2 * g : 2 * g + 2], bank[:].rearrange("m (c e p) -> m c p e", c=2, e=2)
+                    turned[:, 2 * g : 2 * g + 2], banks[use[g]][:].rearrange("m (c e p) -> m c p e", c=2, e=2)
                 )
             return turned[:].rearrange("m c p e -> m c (p e)").bitcast(F32)
 
         wf_w = [new(f"wf_w{b}", [P, N], U32) for b in range(2)]
         wf_s = [new(f"wf_s{b}", [P, N], U8) for b in range(2)]
 
-        def round_wf(b):
-            rounded = new(f"wf_bf{b}", [P, 4 * N], BF16)
-            dst = rounded[:].rearrange("p (c i j) -> p c j i", i=4, j=4)
-            src = wf_raw[b][:].rearrange("p j (c i) -> p c j i", i=4)
-            for c in range(0, N // 4, 64):
-                nc.scalar.copy(dst[:, c : c + 64], src[:, c : c + 64])
-            return rounded
+        wf_bf = [new(f"wf_bf{b}", [P, 4 * N], BF16) for b in range(2)]
 
-        def quantize_wf(b, rounded):
-            for c0, c1 in ((0, 512), (512, N)):
-                nc.vector.quantize_mx(
-                    out=wf_w[b][:, c0:c1].bitcast(FP8X4), scales=wf_s[b][:, c0:c1], in_=rounded[:, 4 * c0 : 4 * c1]
-                )
+        def round_wf(b, c0, c1):
+            dst = wf_bf[b][:].rearrange("p (c i j) -> p c j i", i=4, j=4)
+            src = wf_raw[b][:].rearrange("p j (c i) -> p c j i", i=4)
+            for c in range(c0 // 4, c1 // 4, 64):
+                nc.scalar.copy(dst[:, c : c + 64], src[:, c : c + 64])
+
+        def quantize_wf(b, c0, c1):
+            nc.vector.quantize_mx(
+                out=wf_w[b][:, c0:c1].bitcast(FP8X4), scales=wf_s[b][:, c0:c1], in_=wf_bf[b][:, 4 * c0 : 4 * c1]
+            )
 
         z_w = {}
         z_s = [new(f"z_s{b}", [P, T2], U8) for b in range(2)]
@@ -264,16 +262,16 @@ def tile_list_feed_slot_ranking_kernel(
         features(1)
         scatter(3)
         turned0 = [add_slot_turned(0, 0, (2, 3, 6, 7))]
-        wf_bf = [round_wf(0)]
+        round_wf(0, 0, 512)
         for s in range(4, 6):
             sigmoid_gate(s, row(f"gate{s}"))
             weigh(s, row(f"factor{s}"))
             scatter(s)
-        wf_bf.append(round_wf(1))
+        round_wf(1, 0, 512)
         sigmoid_gate(6, row("gate6"))
         weigh(6, row("factor6"))
         for b in range(2):
-            quantize_wf(b, wf_bf[b])
+            quantize_wf(b, 0, 512)
         turned0.append(add_slot_turned(0, 1, (2, 3, 0, 1)))
         scatter(6)
         pairs = new("pairs", [P, 2, T2, 2], BF16, tag="raw3")
@@ -282,8 +280,8 @@ def tile_list_feed_slot_ranking_kernel(
         z_bf = new("z_bf0", [P, 4 * T2], BF16, tag="raw2")
         woven0 = [z_bf[:, 1024 * q : 1024 * (q + 1)] for q in range(4)]
         woven0[0] = pairs[:, 1, 512:1024, :].rearrange("p m e -> p (m e)")
-        for q in range(4):
-            bank = banks[q]
+
+        def weave_first(q, bank):
             for u in range(2):
                 for c2 in range(2):
                     nc.tensor.transpose(
@@ -293,6 +291,11 @@ def tile_list_feed_slot_ranking_kernel(
                 woven0[q].bitcast(F32).rearrange("p (m u) -> p m u", u=2),
                 bank[:].rearrange("p (u m) -> p m u", u=2),
             )
+
+        for q in range(4):
+            weave_first(q, banks[q])
+        for b in range(2):
+            round_wf(b, 512, N)
         sigmoid_gate(7, pair_words[:, 1, 0:S])
         turned1 = add_slot_turned(1, 0, (0, 1, 2, 3))
         weigh(7, row("factor7", "z_w0"))
@@ -303,14 +306,13 @@ def tile_list_feed_slot_ranking_kernel(
             quantize_z(0, woven0[q], 256 * q, 256 * (q + 1))
         z_rest = z_bf[:, 2048:]
 
-        for h in range(2):
-            bank = banks[6 + h]
-            for c in range(4):
-                nc.tensor.transpose(bank[:, P * c : P * (c + 1)], turned1[:, 4 * h + c, :], ident[:])
-            nc.scalar.copy(pair_words[:, 0, 512 * h : 512 * (h + 1)], bank[:])
+        for q, bank in enumerate(banks[4:]):
+            for c in range(2):
+                nc.tensor.transpose(bank[:, P * c : P * (c + 1)], turned1[:, 2 * q + c, :], ident[:])
+            nc.scalar.copy(pair_words[:, 0, 256 * q : 256 * (q + 1)], bank[:, 0:256])
 
         nc.scalar.activation(warm[:, 8:16], pairs[:, 0, T2 - 8 :, 0], ACT.Silu)
-        units = [(h, n) for h in range(2) for n in range(N // P)]
+        units = [(h, n) for first, last in ((0, 4), (4, 6)) for h in range(2) for n in range(first, last)]
 
         def product(k, b, m0, m1, start, stop, which=(0, 1)):
             h, n = units[k]
@@ -334,13 +336,18 @@ def tile_list_feed_slot_ranking_kernel(
             silu = new(f"silu{k}", [P, 512], F32, tag=f"gate{k % 4}")
             nc.scalar.activation(silu[:], banks[2 * (k % 4)][:], ACT.Silu)
             result = new(f"result{k}", [P, 512], F32, tag=f"tanh{k % 4}")
-            nc.vector.tensor_tensor(result[:], banks[2 * (k % 4) + 1][:], silu[:], MULT)
-            nc.sync.dma_start(out=out[P * n : P * (n + 1), 512 * h : 512 * (h + 1)], in_=result[:])
+            width = 256 if k == len(units) - 1 else 512
+            for c in range(0, 512, width):
+                cols = slice(c, c + width)
+                nc.vector.tensor_tensor(result[:, cols], banks[2 * (k % 4) + 1][:, cols], silu[:, cols], MULT)
+                nc.sync.dma_start(
+                    out=out[P * n : P * (n + 1), 512 * h + c : 512 * h + c + width], in_=result[:, cols]
+                )
 
         for k in range(4):
             product(k, 0, 0, 512, True, False)
 
-        z_bf = new("z_bf1", [P, 4 * T2], BF16, tag="wf_raw0")
+        z_bf = new("z_bf1", [P, 4 * T2], BF16, tag="raw4")
 
         def last_pair(q):
             cols = slice(256 * q, 256 * (q + 1))
@@ -361,6 +368,8 @@ def tile_list_feed_slot_ranking_kernel(
             last_pair(q)
         quantize_z(0, z_rest, 512, 1024)
         quantize_z(1, z_bf[:, 2048:], 512, 1024)
+        for b in range(2):
+            quantize_wf(b, 512, N)
         for k in range(len(units)):
             if k >= 4:
                 for i in range(2):

@@ -22,7 +22,12 @@ P = 128
 PASS = 512
 BANK = 512
 AL = 64
-PAGES = 4
+PAGE_OF = (0, 1, 2, 2, 0, 1, 2, 0)
+HALF = T2 // 2
+QUARTER = T2 // 4
+GATE_BANK = (6, 7, 0, 1, 4, 5, 6, 7)
+FIRST_CUTS = (0, 128, 256, 512)
+WF_FRONT = 512
 
 
 def tile_list_feed_slot_ranking_kernel(
@@ -42,9 +47,9 @@ def tile_list_feed_slot_ranking_kernel(
         idx = lists.tile([P, S // 16], U16, name="idx")
         idx2 = lists.tile([P, S // 16], U16, name="idx2")
 
-        def load_scale_rows(plane, scales):
+        def load_scale_rows(queue, plane, scales):
             for q in range(4):
-                nc.sync.dma_start(
+                queue.dma_start(
                     out=plane[32 * q : 32 * q + 4].bitcast(I32),
                     in_=scales.bitcast(I32)[:, 4 * q : 4 * q + 4, :].rearrange("a r n -> r a n"),
                 )
@@ -55,29 +60,32 @@ def tile_list_feed_slot_ranking_kernel(
         warm = new("warm", [P, 16], F32)
         nc.vector.memset(tab_s[:].bitcast(I32), 0)
         nc.vector.memset(w4_s[:].bitcast(I32), 0)
-        nc.vector.memset(w8_s[:].bitcast(I32), 0)
         nc.vector.memset(warm[:, 0:8], 0.0)
-        nc.scalar.activation(warm[:, 8:16], warm[:, 0:8], ACT.Sigmoid)
+        nc.vector.memset(w8_s[:].bitcast(I32), 0)
 
         ident = new("ident", [P, P], F32)
         make_identity(nc, ident[:])
-        pages = [new(f"page{i}", [P, T2], F32) for i in range(PAGES)]
+        pages = [new(f"page{i}", [P, T2], F32) for i in range(3)]
         for page in pages:
             nc.vector.memset(page[:], 0.0)
 
         def load_wg(b, a):
-            raw = new(f"wg_raw{b}{a}", [P, 4, PASS], F32, tag=f"raw{2 * b + a}")
+            raw = new(f"wg_raw{b}{a}", [P, 4, PASS], F32, tag=f"raw{b}{a}")
             nc.sync.dma_start(
                 out=raw[:],
                 in_=wg[PASS * a : PASS * (a + 1), PASS * b : PASS * (b + 1)].rearrange("(p j) c -> p j c", j=4),
             )
             return raw
 
-        def load_slot(b, u, tag):
-            raw = new(f"slot{b}{u}", [P, 2, T2], F32, tag=tag)
+        slot_sb = {}
+
+        def load_slot(s, tag=None):
+            b, t = divmod(s, 4)
+            whole = new(f"slot{s}", [P, T2], F32, tag=tag)
             rows = slot[PASS * b : PASS * (b + 1), :].rearrange("(p i) m -> p i m", i=4)
-            nc.sync.dma_start(out=raw[:], in_=rows[:, 2 * u : 2 * u + 2, :])
-            return raw
+            nc.sync.dma_start(out=whole[:], in_=rows[:, t, :])
+            for h in range(2):
+                slot_sb[s, h] = whole[:, HALF * h : HALF * (h + 1)]
 
         def load_wf(b):
             raw = new(f"wf_raw{b}", [P, 4, N], F32)
@@ -97,28 +105,27 @@ def tile_list_feed_slot_ranking_kernel(
 
         nc.sync.dma_start(idx[:], offs)
         tab_w = [load_tab(0)]
-        load_scale_rows(tab_s, tab_scales)
+        load_scale_rows(nc.sync, tab_s, tab_scales)
         w4_w = [load_w4(0)]
         tab_w.append(load_tab(1))
+        load_scale_rows(nc.sync, w4_s, w4_scales)
+        nc.scalar.activation(warm[:, 8:16], warm[:, 0:8], ACT.Sigmoid)
         wg_raw = {(0, 0): load_wg(0, 0)}
-        load_scale_rows(w4_s, w4_scales)
         wg_raw[0, 1] = load_wg(0, 1)
         wgs_sb = new("wgs_sb", [P, S], F32)
         nc.sync.dma_start(out=wgs_sb[:], in_=wgs)
         gain_sb = new("gain_sb", [P, 2, 4], F32)
         nc.sync.dma_start(out=gain_sb[:], in_=gain.rearrange("(b p i) -> p b i", b=2, i=4))
         nc.sync.dma_start(idx2[:], offs2)
-        w4_w.append(load_w4(1))
         wg_raw[1, 0] = load_wg(1, 0)
         wg_raw[1, 1] = load_wg(1, 1)
-        slot_sb = {(0, 0): load_slot(0, 0, "raw4")}
+        w4_w.append(load_w4(1))
+        for s in range(4):
+            load_slot(s)
         wf_raw = [load_wf(0), load_wf(1)]
-        slot_sb[0, 1] = load_slot(0, 1, "raw5")
         w8_w = new("w8_w", [P, 2, N], U32)
-        nc.sync.dma_start(
-            out=w8_w[:].bitcast(I32), in_=w8_words.rearrange("a p n i -> p a (n i)").bitcast(I32)
-        )
-        load_scale_rows(w8_s, w8_scales)
+        nc.sync.dma_start(out=w8_w[:].bitcast(I32), in_=w8_words.rearrange("a p n i -> p a (n i)").bitcast(I32))
+        load_scale_rows(nc.sync, w8_s, w8_scales)
 
         v_w = [new(f"v_w{a}", [P, S], U32) for a in range(2)]
         v_s = [new(f"v_s{a}", [P, S], U8) for a in range(2)]
@@ -127,252 +134,240 @@ def tile_list_feed_slot_ranking_kernel(
             nc.vector.tensor_copy(v_s[a][:], tab_s[:, a, :].indirect(idx[:]))
         nc.vector.tensor_copy(v_w[1][:], tab_w[1][:].indirect(idx[:]))
 
-        wg_w, wg_s = {}, {}
-
-        def round_wg(b, a, vector_from):
-            rounded = new(f"wg_bf{b}{a}", [P, 4 * PASS], BF16, tag=f"wg_bf{a}")
-            dst = rounded[:].rearrange("p (t m j) -> p m j t", t=4, j=4)
-            src = wg_raw[b, a][:].rearrange("p j (m t) -> p m j t", t=4)
+        def round_wg(raw, rounded, vector_from):
+            dst = rounded.rearrange("p (t m j) -> p m j t", t=4, j=4)
+            src = raw[:].rearrange("p j (m t) -> p m j t", t=4)
             if vector_from > 0:
                 nc.scalar.copy(dst[:, :vector_from], src[:, :vector_from])
             if vector_from < P:
                 nc.vector.tensor_copy(dst[:, vector_from:], src[:, vector_from:])
-            return rounded
 
-        def quantize_wg(b, a, rounded, width):
-            wg_w[b, a] = new(f"wg_w{b}{a}", [P, PASS], U32)
-            wg_s[b, a] = new(f"wg_s{b}{a}", [P, PASS], U8)
-            for c in range(0, PASS, width):
-                nc.vector.quantize_mx(
-                    out=wg_w[b, a][:, c : c + width].bitcast(FP8X4),
-                    scales=wg_s[b, a][:, c : c + width],
-                    in_=rounded[:, 4 * c : 4 * (c + width)],
-                )
+        def quantize(words, plane, rounded):
+            nc.vector.quantize_mx(out=words.bitcast(FP8X4), scales=plane, in_=rounded)
 
+        def mx(bank, lhs_w, lhs_s, rhs, rhs_s, start, stop):
+            nc.tensor.matmul_mx(
+                out=bank, lhsT=lhs_w.bitcast(FP8X4), lhsT_scale=lhs_s, rhs=rhs, rhs_scale=rhs_s, start=start, stop=stop
+            )
+
+        wg_w = [new(f"wg_w{b}", [P, 2 * PASS], U32) for b in range(2)]
+        wg_s = [new(f"wg_s{b}", [P, 2 * PASS], U8) for b in range(2)]
         tanh_b, factor, gate = {}, {}, {}
 
         def features(b):
-            cols = slice(PASS * b, PASS * (b + 1))
             for a in range(2):
                 for jb in range(4):
                     entries = slice(P * jb, P * (jb + 1))
-                    nc.tensor.matmul_mx(
-                        out=banks[4 + jb][:],
-                        lhsT=v_w[a][:, entries].bitcast(FP8X4),
-                        lhsT_scale=v_s[a][:, entries],
-                        rhs=w4_w[b][:, a, :].bitcast(FP4X4),
-                        rhs_scale=w4_s[:, a, cols],
-                        start=(a == 0),
-                        stop=(a == 1),
+                    mx(
+                        banks[jb][:], v_w[a][:, entries], v_s[a][:, entries], w4_w[b][:, a, :].bitcast(FP4X4),
+                        w4_s[:, a, PASS * b : PASS * (b + 1)], a == 0, a == 1,
                     )
             for jb in range(4):
-                tanh_b[b, jb] = new(f"tanh{b}{jb}", [P, 4, P], F32, tag=f"tanh{jb}")
-                nc.scalar.activation(
-                    tanh_b[b, jb][:], banks[4 + jb][:].rearrange("j (m t) -> j t m", t=4), ACT.Tanh
-                )
+                if b == 1 and jb >= 2:
+                    tanh_b[jb] = pairs[0, jb - 2][:, HALF:].rearrange("j (t m) -> j t m", t=4)
+                else:
+                    tanh_b[jb] = new(f"tanh{b}{jb}", [P, 4, P], F32, tag=f"tanh{jb}")[:]
+                nc.scalar.activation(tanh_b[jb], banks[jb][:].rearrange("j (m t) -> j t m", t=4), ACT.Tanh)
 
-        def weigh(s, dst):
+        def weigh(s, dst, bank):
             b, t = divmod(s, 4)
-            bank = banks[(0, 1, 0, 1, 1, 6, 7, 4)[s]]
             for jb in range(4):
-                nc.tensor.transpose(bank[:, P * jb : P * (jb + 1)], tanh_b[b, jb][:, t, :], ident[:])
+                nc.tensor.transpose(bank[:, P * jb : P * (jb + 1)], tanh_b[jb][:, t, :], ident[:])
             factor[s] = dst
             nc.vector.scalar_tensor_tensor(dst, bank[:], gain_sb[:, b, t : t + 1], wgs_sb[:], MULT, MULT)
 
         def row(name, tag=None):
             return new(name, [P, S], F32, tag=tag)[:]
 
-        def sigmoid_gate(s, dst):
+        def gate_pass(s, a):
             b, t = divmod(s, 4)
-            bank = banks[4 + s % (4 if b == 0 else 2)]
-            for a in range(2):
-                nc.tensor.matmul_mx(
-                    out=bank[:],
-                    lhsT=wg_w[b, a][:, P * t : P * (t + 1)].bitcast(FP8X4),
-                    lhsT_scale=wg_s[b, a][:, P * t : P * (t + 1)],
-                    rhs=v_w[a][:].bitcast(FP8X4),
-                    rhs_scale=v_s[a][:],
-                    start=(a == 0),
-                    stop=(a == 1),
-                )
-            gate[s] = dst
-            nc.scalar.activation(dst, bank[:], ACT.Sigmoid)
+            cols = slice(PASS * a + P * t, PASS * a + P * (t + 1))
+            mx(banks[GATE_BANK[s]][:], wg_w[b][:, cols], wg_s[b][:, cols], v_w[a][:].bitcast(FP8X4), v_s[a][:], a == 0, a == 1)
+
+        def sigmoid(s):
+            gate[s] = row(f"gate{s}")
+            nc.scalar.activation(gate[s], banks[GATE_BANK[s]][:], ACT.Sigmoid)
+
+        def multiply(s, engine):
+            engine.tensor_tensor(gate[s], gate[s], factor[s], MULT)
 
         def scatter(s):
-            nc.vector.tensor_tensor(pages[s % PAGES][:].indirect(idx2[:]), gate[s], factor[s], MULT)
+            nc.vector.tensor_copy(pages[PAGE_OF[s]][:].indirect(idx2[:]), gate[s])
 
-        def add_slot_turned(b, u, use):
-            turned = new(f"turned{b}{u}", [P, 8, P, 2], BF16, tag=f"turned{u}")
-            for e in range(2):
-                for c in range(8):
-                    cols = slice(P * c, P * (c + 1))
-                    place = 2 * (c % 2) + e
-                    dst = banks[use[c // 2]][:, P * place : P * (place + 1)]
-                    page = pages[(4 * b + 2 * u + e) % PAGES]
-                    nc.tensor.matmul(
-                        dst, slot_sb[b, u][:, e, cols], ident[:], start=True, stop=False, is_transpose=True
-                    )
-                    nc.tensor.matmul(dst, page[:, cols], ident[:], start=False, stop=True, is_transpose=True)
-            for g in range(4):
-                nc.scalar.copy(
-                    turned[:, 2 * g : 2 * g + 2], banks[use[g]][:].rearrange("m (c e p) -> m c p e", c=2, e=2)
-                )
-            return turned[:].rearrange("m c p e -> m c (p e)").bitcast(F32)
+        pairs = {(b, h): new(f"pairs{b}{h}", [P, T2], F32) for b in range(2) for h in range(2)}
 
-        wf_w = [new(f"wf_w{b}", [P, N], U32) for b in range(2)]
-        wf_s = [new(f"wf_s{b}", [P, N], U8) for b in range(2)]
+        def add_slot(s, engine, m0, m1):
+            b, t = divmod(s, 4)
+            h = m0 // HALF
+            dst = pairs[b, h][:].bitcast(BF16).rearrange("p (u m e) -> p u m e", u=2, e=2)
+            cols = slice(m0 - HALF * h, m1 - HALF * h)
+            engine.tensor_tensor(dst[:, t // 2, cols, t % 2], pages[PAGE_OF[s]][:, m0:m1], slot_sb[s, h][:, cols], ADD)
 
-        wf_bf = [new(f"wf_bf{b}", [P, 4 * N], BF16) for b in range(2)]
+        def add_halves(s):
+            for h in range(2):
+                add_slot(s, nc.gpsimd, HALF * h, HALF * (h + 1))
 
-        def round_wf(b, c0, c1):
-            dst = wf_bf[b][:].rearrange("p (c i j) -> p c j i", i=4, j=4)
-            src = wf_raw[b][:].rearrange("p j (c i) -> p c j i", i=4)
-            for c in range(c0 // 4, c1 // 4, 64):
-                nc.scalar.copy(dst[:, c : c + 64], src[:, c : c + 64])
+        z_bf, z_w = {}, {}
+        z_s = {(b, h): new(f"z_s{b}{h}", [P, HALF], U8) for b in range(2) for h in range(2)}
 
-        def quantize_wf(b, c0, c1):
-            nc.vector.quantize_mx(
-                out=wf_w[b][:, c0:c1].bitcast(FP8X4), scales=wf_s[b][:, c0:c1], in_=wf_bf[b][:, 4 * c0 : 4 * c1]
-            )
-
-        z_w = {}
-        z_s = [new(f"z_s{b}", [P, T2], U8) for b in range(2)]
-
-        def quantize_z(b, woven, m0, m1):
-            nc.vector.quantize_mx(out=z_w[b][:, m0:m1].bitcast(FP8X4), scales=z_s[b][:, m0:m1], in_=woven)
-
-        quantize_wg(0, 0, round_wg(0, 0, 48), PASS)
-        features(0)
-        quantize_wg(0, 1, round_wg(0, 1, 0), P)
-        for s in range(2):
-            sigmoid_gate(s, row(f"gate{s}"))
-            weigh(s, row(f"factor{s}"))
-        for s in range(2, 4):
-            sigmoid_gate(s, row(f"gate{s}"))
-        for s in range(2):
-            scatter(s)
-        slot_sb[1, 0] = load_slot(1, 0, "raw0")
-        slot_sb[1, 1] = load_slot(1, 1, "raw1")
-        for a in range(2):
-            quantize_wg(1, a, round_wg(1, a, P), PASS)
-        late = new("factor23", [P, 2, S], F32, tag="wg_bf1")
-        for s in range(2, 4):
-            weigh(s, late[:, s - 2, :])
-        scatter(2)
-        features(1)
-        scatter(3)
-        turned0 = [add_slot_turned(0, 0, (2, 3, 6, 7))]
-        round_wf(0, 0, 512)
-        for s in range(4, 6):
-            sigmoid_gate(s, row(f"gate{s}"))
-            weigh(s, row(f"factor{s}"))
-            scatter(s)
-        round_wf(1, 0, 512)
-        sigmoid_gate(6, row("gate6"))
-        weigh(6, row("factor6"))
-        for b in range(2):
-            quantize_wf(b, 0, 512)
-        turned0.append(add_slot_turned(0, 1, (2, 3, 0, 1)))
-        scatter(6)
-        pairs = new("pairs", [P, 2, T2, 2], BF16, tag="raw3")
-        pair_words = pairs[:].rearrange("p u m e -> p u (m e)").bitcast(F32)
-
-        z_bf = new("z_bf0", [P, 4 * T2], BF16, tag="raw2")
-        woven0 = [z_bf[:, 1024 * q : 1024 * (q + 1)] for q in range(4)]
-        woven0[0] = pairs[:, 1, 512:1024, :].rearrange("p m e -> p (m e)")
-
-        def weave_first(q, bank):
-            for u in range(2):
-                for c2 in range(2):
-                    nc.tensor.transpose(
-                        bank[:, P * (2 * u + c2) : P * (2 * u + c2 + 1)], turned0[u][:, 2 * q + c2, :], ident[:]
-                    )
+        def weave(b, h, m0, m1):
             nc.scalar.copy(
-                woven0[q].bitcast(F32).rearrange("p (m u) -> p m u", u=2),
-                bank[:].rearrange("p (u m) -> p m u", u=2),
+                z_bf[b, h][:, 4 * m0 : 4 * m1].bitcast(F32).rearrange("p (m u) -> p m u", u=2),
+                pairs[b, h][:].rearrange("p (u m) -> p m u", u=2)[:, m0:m1],
             )
 
-        for q in range(4):
-            weave_first(q, banks[q])
+        def z_words(b, h, m0, m1):
+            if (b, h) == (0, 0):
+                q = m0 // QUARTER
+                return z_w[0, 0, q][:, m0 - QUARTER * q : m1 - QUARTER * q]
+            return z_w[b, h][:, m0:m1]
+
+        def quantize_z(b, h, m0, m1):
+            quantize(z_words(b, h, m0, m1), z_s[b, h][:, m0:m1], z_bf[b, h][:, 4 * m0 : 4 * m1])
+
+        widths = (WF_FRONT, N - WF_FRONT)
+        wf_bf = {}
+        wf_w = []
+        wf_s = [new(f"wf_s{part}", [P, 2 * widths[part]], U8) for part in range(2)]
+
+        def round_wf(b, part):
+            width = widths[part]
+            dst = wf_bf[part][:, 4 * width * b : 4 * width * (b + 1)].rearrange("p (c i j) -> p c j i", i=4, j=4)
+            src = wf_raw[b][:, :, WF_FRONT * part : WF_FRONT * part + width].rearrange("p j (c i) -> p c j i", i=4)
+            nc.scalar.copy(dst, src)
+
+        features(0)
+        rounded = [new(f"wg_bf0{a}", [P, 4 * PASS], BF16) for a in range(2)]
+        round_wg(wg_raw[0, 0], rounded[0][:], 0)
+        quantize(wg_w[0][:, :PASS], wg_s[0][:, :PASS], rounded[0][:])
+        for s in range(4):
+            gate_pass(s, 0)
+        round_wg(wg_raw[0, 1], rounded[1][:], 32)
+        quantize(wg_w[0][:, PASS : PASS + P], wg_s[0][:, PASS : PASS + P], rounded[1][:, :PASS])
+        quantize(wg_w[0][:, PASS + P : PASS + 2 * P], wg_s[0][:, PASS + P : PASS + 2 * P], rounded[1][:, PASS : 2 * PASS])
+        quantize(wg_w[0][:, PASS + 2 * P :], wg_s[0][:, PASS + 2 * P :], rounded[1][:, 2 * PASS :])
+        for s in range(4):
+            gate_pass(s, 1)
+            sigmoid(s)
+        early = new("early", [P, 2 * S], F32, tag="wg_bf01")
+        weigh(0, early[:, :S], banks[4])
+        weigh(1, early[:, S:], banks[5])
+        multiply(0, nc.vector)
+        for s in range(2, 4):
+            weigh(s, row(f"factor{s}"), banks[2 + s])
+        scatter(0)
+        for s in range(1, 4):
+            multiply(s, nc.gpsimd)
+        scatter(1)
+        scatter(2)
+        for s in range(2):
+            add_halves(s)
+        load_slot(4, "raw00")
+        load_slot(5, "raw01")
+        for h in range(2):
+            slot_sb[6, h] = pairs[1, h][:, HALF:]
+            rows = slot[PASS:, HALF * h : HALF * (h + 1)].rearrange("(p i) m -> p i m", i=4)
+            nc.sync.dma_start(out=slot_sb[6, h], in_=rows[:, 2, :])
+        load_slot(7, "wg_bf00")
+        rounded1 = new("wg_bf1", [P, 8 * PASS], BF16, tag="wg_bf01")
+        for a in range(2):
+            round_wg(wg_raw[1, a], rounded1[:, 4 * PASS * a : 4 * PASS * (a + 1)], P)
+        quantize(wg_w[1][:], wg_s[1][:], rounded1[:])
+        features(1)
+        for s in range(4, 8):
+            weigh(s, row(f"factor{s}"), banks[s])
+        for s in range(4, 8):
+            for a in range(2):
+                gate_pass(s, a)
+            sigmoid(s)
+        add_halves(2)
+        scatter(3)
+        for s in range(4, 8):
+            multiply(s, nc.gpsimd)
+        add_halves(3)
+        wf_bf[0] = new("wf_bf0", [P, 8 * WF_FRONT], BF16, tag="wg_w1")
         for b in range(2):
-            round_wf(b, 512, N)
-        sigmoid_gate(7, pair_words[:, 1, 0:S])
-        turned1 = add_slot_turned(1, 0, (0, 1, 2, 3))
-        weigh(7, row("factor7", "z_w0"))
+            round_wf(b, 0)
+        nc.scalar.activation(warm[:, 8:16], wf_bf[0][:, 8 * WF_FRONT - 8 :], ACT.Silu)
+        z_bf[0, 0] = new("z_bf00", [P, 4 * HALF], BF16, tag="raw10")
+        z_bf[0, 1] = new("z_bf01", [P, 4 * HALF], BF16, tag="raw11")
+        for h in range(2):
+            weave(0, h, 0, HALF)
+        wf_bf[1] = new("wf_bf1", [P, 8 * widths[1]], BF16, tag="pairs00")
+        for b in range(2):
+            round_wf(b, 1)
+        scatter(4)
+        scatter(5)
+        wf_w.append(new("wf_w0", [P, 2 * WF_FRONT], U32, tag="gate5")[:])
+        quantize(wf_w[0][:], wf_s[0][:], wf_bf[0][:])
+        scatter(6)
+        z_w[0, 0, 0] = new("z_w000", [P, QUARTER], U32, tag="gate6")[:]
+        quantize_z(0, 0, 0, QUARTER)
+        for s in range(4, 7):
+            add_halves(s)
         scatter(7)
-        z_w[0] = new("z_w0", [P, T2], U32)
-        z_w[1] = new("z_w1", [P, T2], U32)
-        for q in range(2):
-            quantize_z(0, woven0[q], 256 * q, 256 * (q + 1))
-        z_rest = z_bf[:, 2048:]
 
-        for q, bank in enumerate(banks[4:]):
-            for c in range(2):
-                nc.tensor.transpose(bank[:, P * c : P * (c + 1)], turned1[:, 2 * q + c, :], ident[:])
-            nc.scalar.copy(pair_words[:, 0, 256 * q : 256 * (q + 1)], bank[:, 0:256])
-
-        nc.scalar.activation(warm[:, 8:16], pairs[:, 0, T2 - 8 :, 0], ACT.Silu)
-        units = [(h, n) for first, last in ((0, 4), (4, 6)) for h in range(2) for n in range(first, last)]
+        units = [(h, n) for h in range(2) for n in range(N // P)]
 
         def product(k, b, m0, m1, start, stop, which=(0, 1)):
             h, n = units[k]
+            part, first = divmod(P * n, WF_FRONT)
+            wf_cols = slice(widths[part] * b + first, widths[part] * b + first + P)
             cols = slice(P * n, P * (n + 1))
-            moving = slice(512 * h + m0, 512 * h + m1)
-            weights = ((wf_w[b][:, cols], wf_s[b][:, cols]), (w8_w[:, b, cols], w8_s[:, b, cols]))
+            weights = ((wf_w[part][:, wf_cols], wf_s[part][:, wf_cols]), (w8_w[:, b, cols], w8_s[:, b, cols]))
             for i in which:
-                bank, (words, plane) = banks[2 * (k % 4) + i], weights[i]
-                nc.tensor.matmul_mx(
-                    out=bank[:, m0:m1],
-                    lhsT=words.bitcast(FP8X4),
-                    lhsT_scale=plane,
-                    rhs=z_w[b][:, moving].bitcast(FP8X4),
-                    rhs_scale=z_s[b][:, moving],
-                    start=start,
-                    stop=stop,
+                mx(
+                    banks[2 * (k % 4) + i][:, m0:m1], weights[i][0], weights[i][1],
+                    z_words(b, h, m0, m1).bitcast(FP8X4), z_s[b, h][:, m0:m1], start, stop,
                 )
 
         def finish(k):
             h, n = units[k]
-            silu = new(f"silu{k}", [P, 512], F32, tag=f"gate{k % 4}")
-            nc.scalar.activation(silu[:], banks[2 * (k % 4)][:], ACT.Silu)
-            result = new(f"result{k}", [P, 512], F32, tag=f"tanh{k % 4}")
-            width = 256 if k == len(units) - 1 else 512
-            for c in range(0, 512, width):
+            silu = row(f"silu{k}", f"gate{k % 4}")
+            nc.scalar.activation(silu, banks[2 * (k % 4)][:], ACT.Silu)
+            result = row(f"result{k}", f"tanh{k % 4}")
+            width = 256 if k == len(units) - 1 else HALF
+            for c in range(0, HALF, width):
                 cols = slice(c, c + width)
                 nc.vector.tensor_tensor(result[:, cols], banks[2 * (k % 4) + 1][:, cols], silu[:, cols], MULT)
-                nc.sync.dma_start(
-                    out=out[P * n : P * (n + 1), 512 * h + c : 512 * h + c + width], in_=result[:, cols]
-                )
+                nc.sync.dma_start(out=out[P * n : P * (n + 1), HALF * h + c : HALF * h + c + width], in_=result[:, cols])
 
         for k in range(4):
-            product(k, 0, 0, 512, True, False)
-
-        z_bf = new("z_bf1", [P, 4 * T2], BF16, tag="raw4")
-
-        def last_pair(q):
-            cols = slice(256 * q, 256 * (q + 1))
-            for e in range(2):
-                nc.vector.tensor_tensor(pairs[:, 1, cols, e], pages[(6 + e) % PAGES][:, cols], slot_sb[1, 1][:, e, cols], ADD)
-            weave = nc.vector.tensor_copy if q < 2 else nc.scalar.copy
-            weave(
-                z_bf[:, 1024 * q : 1024 * (q + 1)].bitcast(F32).rearrange("p (m u) -> p m u", u=2),
-                pair_words[:, :, cols].rearrange("p u m -> p m u"),
-            )
-
-        for q in range(2):
-            last_pair(q)
-            quantize_z(1, z_bf[:, 1024 * q : 1024 * (q + 1)], 256 * q, 256 * (q + 1))
+            product(k, 0, 0, QUARTER, True, False)
+        z_w[0, 0, 1] = new("z_w001", [P, QUARTER], U32, tag="gate7")[:]
+        quantize_z(0, 0, QUARTER, HALF)
+        for k in range(4):
+            product(k, 0, QUARTER, HALF, False, False)
+        z_bf[1, 0] = new("z_bf10", [P, 4 * HALF], BF16, tag="tab_w0")
+        z_bf[1, 1] = new("z_bf11", [P, 4 * HALF], BF16, tag="tab_w1")
+        z_w[1, 0] = new("z_w10", [P, HALF], U32)[:]
+        z_w[1, 1] = new("z_w11", [P, HALF], U32)[:]
+        cuts = list(zip(FIRST_CUTS, FIRST_CUTS[1:]))
+        for m0, m1 in cuts:
+            add_slot(7, nc.vector, m0, m1)
+            weave(1, 0, m0, m1)
+        for m0, m1 in cuts:
+            quantize_z(1, 0, m0, m1)
             for k in range(4):
-                product(k, 1, 256 * q, 256 * (q + 1), False, q == 1)
-        for q in range(2, 4):
-            last_pair(q)
-        quantize_z(0, z_rest, 512, 1024)
-        quantize_z(1, z_bf[:, 2048:], 512, 1024)
-        for b in range(2):
-            quantize_wf(b, 512, N)
-        for k in range(len(units)):
+                product(k, 1, m0, m1, False, m1 == HALF)
+        add_slot(7, nc.vector, HALF, T2)
+        tail_words = new("tail_words", [P, 2 * HALF], U32, tag="pairs10")
+        wf_w.append(tail_words[:, :HALF])
+        z_w[0, 1] = tail_words[:, HALF:]
+        quantize(wf_w[1][:], wf_s[1][:], wf_bf[1][:])
+        finish(0)
+        weave(1, 1, 0, QUARTER)
+        finish(1)
+        weave(1, 1, QUARTER, HALF)
+        quantize_z(0, 1, 0, HALF)
+        quantize_z(1, 1, 0, HALF)
+        for k in range(2, len(units)):
             if k >= 4:
                 for i in range(2):
-                    product(k, 0, 0, 512, True, False, (i,))
-                    product(k, 1, 0, 512, False, True, (i,))
+                    if units[k][0] == 0:
+                        product(k, 0, 0, QUARTER, True, False, (i,))
+                        product(k, 0, QUARTER, HALF, False, False, (i,))
+                    else:
+                        product(k, 0, 0, HALF, True, False, (i,))
+                    product(k, 1, 0, HALF, False, True, (i,))
             finish(k)

@@ -22,10 +22,10 @@ P = 128
 PASS = 512
 BANK = 512
 AL = 64
-PAGE_OF = (0, 1, 2, 2, 0, 1, 2, 0)
+PAGE_OF = (0, 1, 2, 3, 0, 1, 0, 1)
 HALF = T2 // 2
 QUARTER = T2 // 4
-GATE_BANK = (6, 7, 0, 1, 4, 5, 6, 7)
+GATE_BANK = (6, 7, 0, 1, 5, 6, 7, 5)
 FIRST_CUTS = (0, 128, 256, 512)
 WF_FRONT = 512
 
@@ -65,7 +65,7 @@ def tile_list_feed_slot_ranking_kernel(
 
         ident = new("ident", [P, P], F32)
         make_identity(nc, ident[:])
-        pages = [new(f"page{i}", [P, T2], F32) for i in range(3)]
+        pages = [new(f"page{i}", [P, T2], F32) for i in range(2)]
         for page in pages:
             nc.vector.memset(page[:], 0.0)
 
@@ -79,13 +79,16 @@ def tile_list_feed_slot_ranking_kernel(
 
         slot_sb = {}
 
-        def load_slot(s, tag=None):
+        def load_slot(s, dst, m0=0, m1=T2):
             b, t = divmod(s, 4)
-            whole = new(f"slot{s}", [P, T2], F32, tag=tag)
-            rows = slot[PASS * b : PASS * (b + 1), :].rearrange("(p i) m -> p i m", i=4)
-            nc.sync.dma_start(out=whole[:], in_=rows[:, t, :])
-            for h in range(2):
-                slot_sb[s, h] = whole[:, HALF * h : HALF * (h + 1)]
+            rows = slot[PASS * b : PASS * (b + 1), m0:m1].rearrange("(p i) m -> p i m", i=4)
+            nc.sync.dma_start(out=dst, in_=rows[:, t, :])
+            for h in range(m0 // HALF, m1 // HALF):
+                slot_sb[s, h] = dst[:, HALF * h - m0 : HALF * (h + 1) - m0]
+
+        def load_slots(first):
+            for s in range(first, first + 2):
+                load_slot(s, new(f"slot{s}", [P, T2], F32, tag=f"slot{s % 4}")[:])
 
         def load_wf(b):
             raw = new(f"wf_raw{b}", [P, 4, N], F32)
@@ -120,9 +123,10 @@ def tile_list_feed_slot_ranking_kernel(
         wg_raw[1, 0] = load_wg(1, 0)
         wg_raw[1, 1] = load_wg(1, 1)
         w4_w.append(load_w4(1))
-        for s in range(4):
-            load_slot(s)
-        wf_raw = [load_wf(0), load_wf(1)]
+        wf_raw = [load_wf(0)]
+        load_slots(0)
+        load_slots(2)
+        wf_raw.append(load_wf(1))
         w8_w = new("w8_w", [P, 2, N], U32)
         nc.sync.dma_start(out=w8_w[:].bitcast(I32), in_=w8_words.rearrange("a p n i -> p a (n i)").bitcast(I32))
         load_scale_rows(nc.sync, w8_s, w8_scales)
@@ -133,6 +137,10 @@ def tile_list_feed_slot_ranking_kernel(
         for a in range(2):
             nc.vector.tensor_copy(v_s[a][:], tab_s[:, a, :].indirect(idx[:]))
         nc.vector.tensor_copy(v_w[1][:], tab_w[1][:].indirect(idx[:]))
+
+        for tag in ("tab_w0", "tab_s"):
+            pages.append(new(f"page{len(pages)}", [P, T2], F32, tag=tag))
+            nc.gpsimd.memset(pages[-1][:], 0.0)
 
         def round_wg(raw, rounded, vector_from):
             dst = rounded.rearrange("p (t m j) -> p m j t", t=4, j=4)
@@ -152,7 +160,7 @@ def tile_list_feed_slot_ranking_kernel(
 
         wg_w = [new(f"wg_w{b}", [P, 2 * PASS], U32) for b in range(2)]
         wg_s = [new(f"wg_s{b}", [P, 2 * PASS], U8) for b in range(2)]
-        tanh_b, factor, gate = {}, {}, {}
+        tanh_b, factor, gate, weighted = {}, {}, {}, {}
 
         def features(b):
             for a in range(2):
@@ -163,16 +171,13 @@ def tile_list_feed_slot_ranking_kernel(
                         w4_s[:, a, PASS * b : PASS * (b + 1)], a == 0, a == 1,
                     )
             for jb in range(4):
-                if b == 1 and jb >= 2:
-                    tanh_b[jb] = pairs[0, jb - 2][:, HALF:].rearrange("j (t m) -> j t m", t=4)
-                else:
-                    tanh_b[jb] = new(f"tanh{b}{jb}", [P, 4, P], F32, tag=f"tanh{jb}")[:]
-                nc.scalar.activation(tanh_b[jb], banks[jb][:].rearrange("j (m t) -> j t m", t=4), ACT.Tanh)
+                tanh_b[b, jb] = new(f"tanh{b}{jb}", [P, 4, P], F32)[:]
+                nc.scalar.activation(tanh_b[b, jb], banks[jb][:].rearrange("j (m t) -> j t m", t=4), ACT.Tanh)
 
         def weigh(s, dst, bank):
             b, t = divmod(s, 4)
             for jb in range(4):
-                nc.tensor.transpose(bank[:, P * jb : P * (jb + 1)], tanh_b[jb][:, t, :], ident[:])
+                nc.tensor.transpose(bank[:, P * jb : P * (jb + 1)], tanh_b[b, jb][:, t, :], ident[:])
             factor[s] = dst
             nc.vector.scalar_tensor_tensor(dst, bank[:], gain_sb[:, b, t : t + 1], wgs_sb[:], MULT, MULT)
 
@@ -188,32 +193,54 @@ def tile_list_feed_slot_ranking_kernel(
             gate[s] = row(f"gate{s}")
             nc.scalar.activation(gate[s], banks[GATE_BANK[s]][:], ACT.Sigmoid)
 
-        def multiply(s, engine):
-            engine.tensor_tensor(gate[s], gate[s], factor[s], MULT)
-
         def scatter(s):
-            nc.vector.tensor_copy(pages[PAGE_OF[s]][:].indirect(idx2[:]), gate[s])
+            nc.vector.tensor_tensor(pages[PAGE_OF[s]][:].indirect(idx2[:]), gate[s], factor[s], MULT)
 
-        pairs = {(b, h): new(f"pairs{b}{h}", [P, T2], F32) for b in range(2) for h in range(2)}
+        def multiply(s, dst):
+            weighted[s] = dst
+            nc.gpsimd.tensor_tensor(dst, gate[s], factor[s], MULT)
 
-        def add_slot(s, engine, m0, m1):
-            b, t = divmod(s, 4)
-            h = m0 // HALF
-            dst = pairs[b, h][:].bitcast(BF16).rearrange("p (u m e) -> p u m e", u=2, e=2)
-            cols = slice(m0 - HALF * h, m1 - HALF * h)
-            engine.tensor_tensor(dst[:, t // 2, cols, t % 2], pages[PAGE_OF[s]][:, m0:m1], slot_sb[s, h][:, cols], ADD)
+        def place(s):
+            nc.vector.tensor_copy(pages[PAGE_OF[s]][:].indirect(idx2[:]), weighted[s])
+
+        def add_turned(first, tag, by_bank):
+            turned = new(f"turned{first}", [P, 8, P, 2], BF16, tag=tag)
+            steps = [(step, c) for step in range(4) for c in range(8)]
+            for step, c in sorted(steps, key=lambda sc: sc[1] // 2) if by_bank else steps:
+                s = first + step % 2
+                source = pages[PAGE_OF[s]][:, P * c : P * (c + 1)] if step < 2 else slot_sb[s, c // 4][:, P * (c % 4) : P * (c % 4 + 1)]
+                column = P * (2 * (c % 2) + step % 2)
+                nc.tensor.matmul(
+                    banks[4 + c // 2][:, column : column + P], source, ident[:],
+                    start=(step == 0 and c % 2 == 0), stop=(step == 3 and c % 2 == 1), is_transpose=True,
+                )
+            for g in range(4):
+                nc.scalar.copy(
+                    turned[:, 2 * g : 2 * g + 2], banks[4 + g][:].rearrange("m (c e p) -> m c p e", c=2, e=2)
+                )
+            return turned[:].rearrange("m c p e -> m c (p e)").bitcast(F32)
+
+        pairs = [new("pairs0", [P, T2], F32)[:], new("pairs1", [P, T2 + HALF], F32)[:]]
+
+        def pair_halves(h):
+            return pairs[h][:, :T2].bitcast(BF16).rearrange("p (u m e) -> p u m e", u=2, e=2)
 
         def add_halves(s):
             for h in range(2):
-                add_slot(s, nc.gpsimd, HALF * h, HALF * (h + 1))
+                nc.gpsimd.tensor_tensor(slot_sb[s, h], pages[PAGE_OF[s]][:, HALF * h : HALF * (h + 1)], slot_sb[s, h], ADD)
+
+        def add_last(m0, m1):
+            h = m0 // HALF
+            cols = slice(m0 - HALF * h, m1 - HALF * h)
+            nc.vector.tensor_tensor(pair_halves(h)[:, 1, cols, 1], pages[PAGE_OF[7]][:, m0:m1], slot_sb[7, h][:, cols], ADD)
 
         z_bf, z_w = {}, {}
         z_s = {(b, h): new(f"z_s{b}{h}", [P, HALF], U8) for b in range(2) for h in range(2)}
 
-        def weave(b, h, m0, m1):
+        def weave(h, m0, m1):
             nc.scalar.copy(
-                z_bf[b, h][:, 4 * m0 : 4 * m1].bitcast(F32).rearrange("p (m u) -> p m u", u=2),
-                pairs[b, h][:].rearrange("p (u m) -> p m u", u=2)[:, m0:m1],
+                z_bf[1, h][:, 4 * m0 : 4 * m1].bitcast(F32).rearrange("p (m u) -> p m u", u=2),
+                pairs[h][:, :T2].rearrange("p (u m) -> p m u", u=2)[:, m0:m1],
             )
 
         def z_words(b, h, m0, m1):
@@ -226,7 +253,7 @@ def tile_list_feed_slot_ranking_kernel(
             quantize(z_words(b, h, m0, m1), z_s[b, h][:, m0:m1], z_bf[b, h][:, 4 * m0 : 4 * m1])
 
         widths = (WF_FRONT, N - WF_FRONT)
-        wf_bf = {}
+        wf_bf = [new(f"wf_bf{part}", [P, 8 * widths[part]], BF16) for part in range(2)]
         wf_w = []
         wf_s = [new(f"wf_s{part}", [P, 2 * widths[part]], U8) for part in range(2)]
 
@@ -234,7 +261,8 @@ def tile_list_feed_slot_ranking_kernel(
             width = widths[part]
             dst = wf_bf[part][:, 4 * width * b : 4 * width * (b + 1)].rearrange("p (c i j) -> p c j i", i=4, j=4)
             src = wf_raw[b][:, :, WF_FRONT * part : WF_FRONT * part + width].rearrange("p j (c i) -> p c j i", i=4)
-            nc.scalar.copy(dst, src)
+            for c in range(0, width // 4, QUARTER // 4):
+                nc.scalar.copy(dst[:, c : c + QUARTER // 4], src[:, c : c + QUARTER // 4])
 
         features(0)
         rounded = [new(f"wg_bf0{a}", [P, 4 * PASS], BF16) for a in range(2)]
@@ -252,60 +280,65 @@ def tile_list_feed_slot_ranking_kernel(
         early = new("early", [P, 2 * S], F32, tag="wg_bf01")
         weigh(0, early[:, :S], banks[4])
         weigh(1, early[:, S:], banks[5])
-        multiply(0, nc.vector)
-        for s in range(2, 4):
-            weigh(s, row(f"factor{s}"), banks[2 + s])
         scatter(0)
-        for s in range(1, 4):
-            multiply(s, nc.gpsimd)
         scatter(1)
-        scatter(2)
-        for s in range(2):
-            add_halves(s)
-        load_slot(4, "raw00")
-        load_slot(5, "raw01")
-        for h in range(2):
-            slot_sb[6, h] = pairs[1, h][:, HALF:]
-            rows = slot[PASS:, HALF * h : HALF * (h + 1)].rearrange("(p i) m -> p i m", i=4)
-            nc.sync.dma_start(out=slot_sb[6, h], in_=rows[:, 2, :])
-        load_slot(7, "wg_bf00")
-        rounded1 = new("wg_bf1", [P, 8 * PASS], BF16, tag="wg_bf01")
+        rounded1 = new("wg_bf1", [P, 8 * PASS], BF16)
         for a in range(2):
             round_wg(wg_raw[1, a], rounded1[:, 4 * PASS * a : 4 * PASS * (a + 1)], P)
         quantize(wg_w[1][:], wg_s[1][:], rounded1[:])
+        weigh(2, row("factor2", "wg_bf1"), banks[4])
+        scatter(2)
+        weigh(3, gate[2], banks[4])
         features(1)
-        for s in range(4, 8):
-            weigh(s, row(f"factor{s}"), banks[s])
         for s in range(4, 8):
             for a in range(2):
                 gate_pass(s, a)
             sigmoid(s)
-        add_halves(2)
-        scatter(3)
         for s in range(4, 8):
-            multiply(s, nc.gpsimd)
-        add_halves(3)
-        wf_bf[0] = new("wf_bf0", [P, 8 * WF_FRONT], BF16, tag="wg_w1")
-        for b in range(2):
-            round_wf(b, 0)
-        nc.scalar.activation(warm[:, 8:16], wf_bf[0][:, 8 * WF_FRONT - 8 :], ACT.Silu)
-        z_bf[0, 0] = new("z_bf00", [P, 4 * HALF], BF16, tag="raw10")
-        z_bf[0, 1] = new("z_bf01", [P, 4 * HALF], BF16, tag="raw11")
-        for h in range(2):
-            weave(0, h, 0, HALF)
-        wf_bf[1] = new("wf_bf1", [P, 8 * widths[1]], BF16, tag="pairs00")
-        for b in range(2):
-            round_wf(b, 1)
-        scatter(4)
-        scatter(5)
+            weigh(s, row(f"factor{s}"), banks[7 - s])
+        multiply(3, row("weighted3", "tanh10"))
+        place(3)
+        for s in range(4, 8):
+            multiply(s, gate[s])
+        for part in range(2):
+            round_wf(0, part)
+        turned0 = [add_turned(0, "wf_raw0", False)]
+        place(4)
+        place(5)
+        for part in range(2):
+            round_wf(1, part)
+        turned0.append(add_turned(2, "wf_raw1", True))
+        slot45 = new("slot45", [P, 2, T2], F32, tag="raw00")
+        for s in range(4, 6):
+            load_slot(s, slot45[:, s - 4, :])
+        second = new("second", [P, 2, HALF], F32, tag="wg_bf00")
+        load_slot(6, pairs[0][:, HALF:], 0, HALF)
+        load_slot(7, row("first7"), 0, HALF)
+        for s in range(6, 8):
+            load_slot(s, second[:, s - 6, :], HALF, T2)
+        z_bf0 = new("z_bf0", [P, 4 * T2], BF16, tag="raw01")
+        woven0 = [z_bf0[:, 4 * QUARTER * q : 4 * QUARTER * (q + 1)] for q in range(4)]
+        for q in range(4):
+            for u in range(2):
+                for c in range(2):
+                    column = P * (2 * u + c)
+                    nc.tensor.transpose(banks[q][:, column : column + P], turned0[u][:, 2 * q + c, :], ident[:])
+            nc.scalar.copy(
+                woven0[q].bitcast(F32).rearrange("p (m u) -> p m u", u=2), banks[q][:].rearrange("p (u m) -> p m u", u=2)
+            )
+        nc.scalar.activation(warm[:, 8:16], woven0[2][:, 4 * QUARTER - 8 :], ACT.Silu)
         wf_w.append(new("wf_w0", [P, 2 * WF_FRONT], U32, tag="gate5")[:])
         quantize(wf_w[0][:], wf_s[0][:], wf_bf[0][:])
-        scatter(6)
+        add_halves(4)
+        place(6)
         z_w[0, 0, 0] = new("z_w000", [P, QUARTER], U32, tag="gate6")[:]
-        quantize_z(0, 0, 0, QUARTER)
-        for s in range(4, 7):
-            add_halves(s)
-        scatter(7)
+        quantize(z_w[0, 0, 0], z_s[0, 0][:, :QUARTER], woven0[0])
+        add_halves(5)
+        for h in range(2):
+            nc.scalar.copy(pair_halves(h)[:, 0], slot45[:, :, HALF * h : HALF * (h + 1)].rearrange("p e m -> p m e"))
+        nc.gpsimd.tensor_tensor(slot_sb[6, 0], pages[PAGE_OF[6]][:, :HALF], slot_sb[6, 0], ADD)
+        nc.scalar.copy(pair_halves(0)[:, 1, :, 0], slot_sb[6, 0])
+        place(7)
 
         units = [(h, n) for h in range(2) for n in range(N // P)]
 
@@ -323,9 +356,9 @@ def tile_list_feed_slot_ranking_kernel(
 
         def finish(k):
             h, n = units[k]
-            silu = row(f"silu{k}", f"gate{k % 4}")
+            silu = row(f"silu{k}", f"gate{k % 4}" if k else "factor4")
             nc.scalar.activation(silu, banks[2 * (k % 4)][:], ACT.Silu)
-            result = row(f"result{k}", f"tanh{k % 4}")
+            result = row(f"result{k}", f"tanh0{k % 4}")
             width = 256 if k == len(units) - 1 else HALF
             for c in range(0, HALF, width):
                 cols = slice(c, c + width)
@@ -335,31 +368,31 @@ def tile_list_feed_slot_ranking_kernel(
         for k in range(4):
             product(k, 0, 0, QUARTER, True, False)
         z_w[0, 0, 1] = new("z_w001", [P, QUARTER], U32, tag="gate7")[:]
-        quantize_z(0, 0, QUARTER, HALF)
+        quantize(z_w[0, 0, 1], z_s[0, 0][:, QUARTER:], woven0[1])
         for k in range(4):
             product(k, 0, QUARTER, HALF, False, False)
-        z_bf[1, 0] = new("z_bf10", [P, 4 * HALF], BF16, tag="tab_w0")
-        z_bf[1, 1] = new("z_bf11", [P, 4 * HALF], BF16, tag="tab_w1")
+        z_bf[1, 0] = pairs[1][:, HALF:].bitcast(BF16)
         z_w[1, 0] = new("z_w10", [P, HALF], U32)[:]
         z_w[1, 1] = new("z_w11", [P, HALF], U32)[:]
         cuts = list(zip(FIRST_CUTS, FIRST_CUTS[1:]))
         for m0, m1 in cuts:
-            add_slot(7, nc.vector, m0, m1)
-            weave(1, 0, m0, m1)
+            add_last(m0, m1)
+            weave(0, m0, m1)
+        wf_w.append(new("wf_w1", [P, 2 * widths[1]], U32, tag="first7")[:])
+        quantize(wf_w[1], wf_s[1][:], wf_bf[1][:])
         for m0, m1 in cuts:
             quantize_z(1, 0, m0, m1)
             for k in range(4):
                 product(k, 1, m0, m1, False, m1 == HALF)
-        add_slot(7, nc.vector, HALF, T2)
-        tail_words = new("tail_words", [P, 2 * HALF], U32, tag="pairs10")
-        wf_w.append(tail_words[:, :HALF])
-        z_w[0, 1] = tail_words[:, HALF:]
-        quantize(wf_w[1][:], wf_s[1][:], wf_bf[1][:])
+        nc.vector.tensor_tensor(pair_halves(1)[:, 1, :, 0], pages[PAGE_OF[6]][:, HALF:], slot_sb[6, 1], ADD)
+        add_last(HALF, T2)
+        z_w[0, 1] = new("z_w01", [P, HALF], U32, tag="wg_bf00")[:]
         finish(0)
-        weave(1, 1, 0, QUARTER)
         finish(1)
-        weave(1, 1, QUARTER, HALF)
-        quantize_z(0, 1, 0, HALF)
+        z_bf[1, 1] = new("z_bf11", [P, 4 * HALF], BF16, tag="factor4")
+        weave(1, 0, QUARTER)
+        weave(1, QUARTER, HALF)
+        quantize(z_w[0, 1], z_s[0, 1][:], z_bf0[:, 4 * HALF :])
         quantize_z(1, 1, 0, HALF)
         for k in range(2, len(units)):
             if k >= 4:

@@ -22,7 +22,8 @@ P = 128
 PASS = 512
 BANK = 512
 AL = 64
-PAGE_OF = (0, 1, 2, 3, 0, 1, 0, 1)
+PAGE_OF = (0, 1, 2, 3, 0, 1, 2, 0)
+ROW_OF = (0, 1, 2, 3, 2, 3, 0, 1)
 HALF = T2 // 2
 QUARTER = T2 // 4
 GATE_BANK = (6, 7, 0, 1, 5, 6, 7, 5)
@@ -80,7 +81,7 @@ def tile_list_feed_slot_ranking_kernel(
         slot_sb = {}
 
         def load_slot(s, dst, m0=0, m1=T2):
-            b, t = divmod(s, 4)
+            b, t = s // 4, ROW_OF[s]
             rows = slot[PASS * b : PASS * (b + 1), m0:m1].rearrange("(p i) m -> p i m", i=4)
             nc.sync.dma_start(out=dst, in_=rows[:, t, :])
             for h in range(m0 // HALF, m1 // HALF):
@@ -125,8 +126,8 @@ def tile_list_feed_slot_ranking_kernel(
         w4_w.append(load_w4(1))
         wf_raw = [load_wf(0)]
         load_slots(0)
-        load_slots(2)
         wf_raw.append(load_wf(1))
+        load_slots(2)
         w8_w = new("w8_w", [P, 2, N], U32)
         nc.sync.dma_start(out=w8_w[:].bitcast(I32), in_=w8_words.rearrange("a p n i -> p a (n i)").bitcast(I32))
         load_scale_rows(nc.sync, w8_s, w8_scales)
@@ -175,7 +176,7 @@ def tile_list_feed_slot_ranking_kernel(
                 nc.scalar.activation(tanh_b[b, jb], banks[jb][:].rearrange("j (m t) -> j t m", t=4), ACT.Tanh)
 
         def weigh(s, dst, bank):
-            b, t = divmod(s, 4)
+            b, t = s // 4, ROW_OF[s]
             for jb in range(4):
                 nc.tensor.transpose(bank[:, P * jb : P * (jb + 1)], tanh_b[b, jb][:, t, :], ident[:])
             factor[s] = dst
@@ -185,7 +186,7 @@ def tile_list_feed_slot_ranking_kernel(
             return new(name, [P, S], F32, tag=tag)[:]
 
         def gate_pass(s, a):
-            b, t = divmod(s, 4)
+            b, t = s // 4, ROW_OF[s]
             cols = slice(PASS * a + P * t, PASS * a + P * (t + 1))
             mx(banks[GATE_BANK[s]][:], wg_w[b][:, cols], wg_s[b][:, cols], v_w[a][:].bitcast(FP8X4), v_s[a][:], a == 0, a == 1)
 
@@ -208,7 +209,10 @@ def tile_list_feed_slot_ranking_kernel(
             steps = [(step, c) for step in range(4) for c in range(8)]
             for step, c in sorted(steps, key=lambda sc: sc[1] // 2) if by_bank else steps:
                 s = first + step % 2
-                source = pages[PAGE_OF[s]][:, P * c : P * (c + 1)] if step < 2 else slot_sb[s, c // 4][:, P * (c % 4) : P * (c % 4 + 1)]
+                if (step < 2) == by_bank:
+                    source = slot_sb[s, c // 4][:, P * (c % 4) : P * (c % 4 + 1)]
+                else:
+                    source = pages[PAGE_OF[s]][:, P * c : P * (c + 1)]
                 column = P * (2 * (c % 2) + step % 2)
                 nc.tensor.matmul(
                     banks[4 + c // 2][:, column : column + P], source, ident[:],
@@ -220,28 +224,20 @@ def tile_list_feed_slot_ranking_kernel(
                 )
             return turned[:].rearrange("m c p e -> m c (p e)").bitcast(F32)
 
-        pairs = [new("pairs0", [P, T2], F32)[:], new("pairs1", [P, T2 + HALF], F32)[:]]
+        sums0 = new("sums0", [P, 4 * HALF], F32)
+        sums = {0: sums0[:].rearrange("p (t m) -> p t m", t=4)}
 
-        def pair_halves(h):
-            return pairs[h][:, :T2].bitcast(BF16).rearrange("p (u m e) -> p u m e", u=2, e=2)
-
-        def add_halves(s):
-            for h in range(2):
-                nc.gpsimd.tensor_tensor(slot_sb[s, h], pages[PAGE_OF[s]][:, HALF * h : HALF * (h + 1)], slot_sb[s, h], ADD)
-
-        def add_last(m0, m1):
+        def add_slot(engine, s, m0, m1):
             h = m0 // HALF
             cols = slice(m0 - HALF * h, m1 - HALF * h)
-            nc.vector.tensor_tensor(pair_halves(h)[:, 1, cols, 1], pages[PAGE_OF[7]][:, m0:m1], slot_sb[7, h][:, cols], ADD)
+            engine.tensor_tensor(sums[h][:, ROW_OF[s], cols], pages[PAGE_OF[s]][:, m0:m1], slot_sb[s, h][:, cols], ADD)
 
         z_bf, z_w = {}, {}
         z_s = {(b, h): new(f"z_s{b}{h}", [P, HALF], U8) for b in range(2) for h in range(2)}
 
-        def weave(h, m0, m1):
-            nc.scalar.copy(
-                z_bf[1, h][:, 4 * m0 : 4 * m1].bitcast(F32).rearrange("p (m u) -> p m u", u=2),
-                pairs[h][:, :T2].rearrange("p (u m) -> p m u", u=2)[:, m0:m1],
-            )
+        def round_sums(copy, h, m0, m1):
+            dst = z_bf[1, h][:, 4 * m0 : 4 * m1].rearrange("p (c i j) -> p c j i", i=4, j=4)
+            copy(dst, sums[h][:, :, m0:m1].rearrange("p j (c i) -> p c j i", i=4))
 
         def z_words(b, h, m0, m1):
             if (b, h) == (0, 0):
@@ -308,16 +304,16 @@ def tile_list_feed_slot_ranking_kernel(
         for part in range(2):
             round_wf(1, part)
         turned0.append(add_turned(2, "wf_raw1", True))
-        slot45 = new("slot45", [P, 2, T2], F32, tag="raw00")
-        for s in range(4, 6):
-            load_slot(s, slot45[:, s - 4, :])
-        second = new("second", [P, 2, HALF], F32, tag="wg_bf00")
-        load_slot(6, pairs[0][:, HALF:], 0, HALF)
-        load_slot(7, row("first7"), 0, HALF)
-        for s in range(6, 8):
-            load_slot(s, second[:, s - 6, :], HALF, T2)
-        z_bf0 = new("z_bf0", [P, 4 * T2], BF16, tag="raw01")
-        woven0 = [z_bf0[:, 4 * QUARTER * q : 4 * QUARTER * (q + 1)] for q in range(4)]
+        second = new("second", [P, 4, HALF], F32, tag="raw10")
+        load_slot(6, row("first6"), 0, HALF)
+        load_slot(7, sums[0][:, ROW_OF[7], :], 0, HALF)
+        for s in range(4, 8):
+            if s < 6:
+                load_slot(s, sums[0][:, ROW_OF[s], :], 0, HALF)
+            load_slot(s, second[:, s - 4, :], HALF, T2)
+        z_bf0 = new("z_bf0", [P, 12 * QUARTER], BF16, tag="raw01")
+        woven0 = [z_bf0[:, 4 * QUARTER * q : 4 * QUARTER * (q + 1)] for q in range(3)]
+        woven0.insert(1, sums0[:, :HALF].bitcast(BF16))
         for q in range(4):
             for u in range(2):
                 for c in range(2):
@@ -329,15 +325,15 @@ def tile_list_feed_slot_ranking_kernel(
         nc.scalar.activation(warm[:, 8:16], woven0[2][:, 4 * QUARTER - 8 :], ACT.Silu)
         wf_w.append(new("wf_w0", [P, 2 * WF_FRONT], U32, tag="gate5")[:])
         quantize(wf_w[0][:], wf_s[0][:], wf_bf[0][:])
-        add_halves(4)
+        sums1 = new("sums1", [P, 4 * HALF], F32, tag="wf_bf0")
+        sums[1] = sums1[:].rearrange("p (t m) -> p t m", t=4)
+        for s, h in ((4, 0), (4, 1)):
+            add_slot(nc.gpsimd, s, HALF * h, HALF * (h + 1))
         place(6)
         z_w[0, 0, 0] = new("z_w000", [P, QUARTER], U32, tag="gate6")[:]
         quantize(z_w[0, 0, 0], z_s[0, 0][:, :QUARTER], woven0[0])
-        add_halves(5)
-        for h in range(2):
-            nc.scalar.copy(pair_halves(h)[:, 0], slot45[:, :, HALF * h : HALF * (h + 1)].rearrange("p e m -> p m e"))
-        nc.gpsimd.tensor_tensor(slot_sb[6, 0], pages[PAGE_OF[6]][:, :HALF], slot_sb[6, 0], ADD)
-        nc.scalar.copy(pair_halves(0)[:, 1, :, 0], slot_sb[6, 0])
+        for s, h in ((5, 0), (5, 1)):
+            add_slot(nc.gpsimd, s, HALF * h, HALF * (h + 1))
         place(7)
 
         units = [(h, n) for h in range(2) for n in range(N // P)]
@@ -356,7 +352,7 @@ def tile_list_feed_slot_ranking_kernel(
 
         def finish(k):
             h, n = units[k]
-            silu = row(f"silu{k}", f"gate{k % 4}" if k else "factor4")
+            silu = row(f"silu{k}", f"gate{k % 4}" if k else None)
             nc.scalar.activation(silu, banks[2 * (k % 4)][:], ACT.Silu)
             result = row(f"result{k}", f"tanh0{k % 4}")
             width = 256 if k == len(units) - 1 else HALF
@@ -371,28 +367,29 @@ def tile_list_feed_slot_ranking_kernel(
         quantize(z_w[0, 0, 1], z_s[0, 0][:, QUARTER:], woven0[1])
         for k in range(4):
             product(k, 0, QUARTER, HALF, False, False)
-        z_bf[1, 0] = pairs[1][:, HALF:].bitcast(BF16)
+        z_bf[1, 0] = sums1[:, : 2 * HALF].bitcast(BF16)
         z_w[1, 0] = new("z_w10", [P, HALF], U32)[:]
         z_w[1, 1] = new("z_w11", [P, HALF], U32)[:]
         cuts = list(zip(FIRST_CUTS, FIRST_CUTS[1:]))
         for m0, m1 in cuts:
-            add_last(m0, m1)
-            weave(0, m0, m1)
-        wf_w.append(new("wf_w1", [P, 2 * widths[1]], U32, tag="first7")[:])
+            for s in (6, 7):
+                add_slot(nc.vector, s, m0, m1)
+            round_sums(nc.scalar.copy, 0, m0, m1)
+        wf_w.append(new("wf_w1", [P, 2 * widths[1]], U32, tag="first6")[:])
         quantize(wf_w[1], wf_s[1][:], wf_bf[1][:])
         for m0, m1 in cuts:
             quantize_z(1, 0, m0, m1)
             for k in range(4):
                 product(k, 1, m0, m1, False, m1 == HALF)
-        nc.vector.tensor_tensor(pair_halves(1)[:, 1, :, 0], pages[PAGE_OF[6]][:, HALF:], slot_sb[6, 1], ADD)
-        add_last(HALF, T2)
-        z_w[0, 1] = new("z_w01", [P, HALF], U32, tag="wg_bf00")[:]
+        for s in (6, 7):
+            add_slot(nc.vector, s, HALF, T2)
+        z_bf[1, 1] = new("z_bf11", [P, 4 * HALF], BF16, tag="factor4")
+        round_sums(nc.vector.tensor_copy, 1, 0, QUARTER)
         finish(0)
         finish(1)
-        z_bf[1, 1] = new("z_bf11", [P, 4 * HALF], BF16, tag="factor4")
-        weave(1, 0, QUARTER)
-        weave(1, QUARTER, HALF)
-        quantize(z_w[0, 1], z_s[0, 1][:], z_bf0[:, 4 * HALF :])
+        round_sums(nc.scalar.copy, 1, QUARTER, HALF)
+        z_w[0, 1] = new("z_w01", [P, HALF], U32, tag="silu0")[:]
+        quantize(z_w[0, 1], z_s[0, 1][:], z_bf0[:, 4 * QUARTER :])
         quantize_z(1, 1, 0, HALF)
         for k in range(2, len(units)):
             if k >= 4:

@@ -338,6 +338,11 @@ def tile_list_feed_slot_ranking_kernel(
 
         units = [(h, n) for h in range(2) for n in range(N // P)]
 
+        def bank_of(k, i, m0):
+            if k == len(units) - 1 and m0 >= QUARTER:
+                return banks[i]
+            return banks[2 * (k % 4) + i]
+
         def product(k, b, m0, m1, start, stop, which=(0, 1)):
             h, n = units[k]
             part, first = divmod(P * n, WF_FRONT)
@@ -346,19 +351,20 @@ def tile_list_feed_slot_ranking_kernel(
             weights = ((wf_w[part][:, wf_cols], wf_s[part][:, wf_cols]), (w8_w[:, b, cols], w8_s[:, b, cols]))
             for i in which:
                 mx(
-                    banks[2 * (k % 4) + i][:, m0:m1], weights[i][0], weights[i][1],
+                    bank_of(k, i, m0)[:, m0:m1], weights[i][0], weights[i][1],
                     z_words(b, h, m0, m1).bitcast(FP8X4), z_s[b, h][:, m0:m1], start, stop,
                 )
 
         def finish(k):
             h, n = units[k]
             silu = row(f"silu{k}", f"gate{k % 4}" if k else None)
-            nc.scalar.activation(silu, banks[2 * (k % 4)][:], ACT.Silu)
-            result = row(f"result{k}", f"tanh0{k % 4}")
-            width = 256 if k == len(units) - 1 else HALF
+            result = row(f"result{k}", f"tanh{k // 4 % 2}{k % 4}")
+            width = QUARTER if k == len(units) - 1 else HALF
+            for c in range(0, HALF, width):
+                nc.scalar.activation(silu[:, c : c + width], bank_of(k, 0, c)[:, c : c + width], ACT.Silu)
             for c in range(0, HALF, width):
                 cols = slice(c, c + width)
-                nc.vector.tensor_tensor(result[:, cols], banks[2 * (k % 4) + 1][:, cols], silu[:, cols], MULT)
+                nc.vector.tensor_tensor(result[:, cols], bank_of(k, 1, c)[:, cols], silu[:, cols], MULT)
                 nc.sync.dma_start(out=out[P * n : P * (n + 1), HALF * h + c : HALF * h + c + width], in_=result[:, cols])
 
         for k in range(4):
@@ -394,6 +400,11 @@ def tile_list_feed_slot_ranking_kernel(
         for k in range(2, len(units)):
             if k >= 4:
                 for i in range(2):
+                    if k == len(units) - 1:
+                        for m0 in range(0, HALF, QUARTER):
+                            product(k, 0, m0, m0 + QUARTER, True, False, (i,))
+                            product(k, 1, m0, m0 + QUARTER, False, True, (i,))
+                        continue
                     if units[k][0] == 0:
                         product(k, 0, 0, QUARTER, True, False, (i,))
                         product(k, 0, QUARTER, HALF, False, False, (i,))

@@ -224,8 +224,8 @@ def tile_list_feed_slot_ranking_kernel(
                 )
             return turned[:].rearrange("m c p e -> m c (p e)").bitcast(F32)
 
-        sums0 = new("sums0", [P, 4 * HALF], F32)
-        sums = {0: sums0[:].rearrange("p (t m) -> p t m", t=4)}
+        sums0 = new("sums0", [P, 4 * HALF + QUARTER], F32)
+        sums = {0: sums0[:, : 4 * HALF].rearrange("p (t m) -> p t m", t=4)}
 
         def add_slot(engine, s, m0, m1):
             h = m0 // HALF
@@ -309,11 +309,11 @@ def tile_list_feed_slot_ranking_kernel(
         load_slot(7, sums[0][:, ROW_OF[7], :], 0, HALF)
         for s in range(4, 8):
             if s < 6:
-                load_slot(s, sums[0][:, ROW_OF[s], :], 0, HALF)
+                load_slot(s, sums[0][:, ROW_OF[s], :] if s == 4 else row("first5"), 0, HALF)
             load_slot(s, second[:, s - 4, :], HALF, T2)
-        z_bf0 = new("z_bf0", [P, 12 * QUARTER], BF16, tag="raw01")
-        woven0 = [z_bf0[:, 4 * QUARTER * q : 4 * QUARTER * (q + 1)] for q in range(3)]
-        woven0.insert(1, sums0[:, :HALF].bitcast(BF16))
+        z_bf0 = new("z_bf0", [P, 4 * HALF], BF16, tag="raw01")
+        woven0 = [sums0[:, 4 * HALF - QUARTER :].bitcast(BF16), sums0[:, :HALF].bitcast(BF16)]
+        woven0 += [z_bf0[:, 4 * QUARTER * q : 4 * QUARTER * (q + 1)] for q in range(2)]
         for q in range(4):
             for u in range(2):
                 for c in range(2):
@@ -332,8 +332,8 @@ def tile_list_feed_slot_ranking_kernel(
         place(6)
         z_w[0, 0, 0] = new("z_w000", [P, QUARTER], U32, tag="gate6")[:]
         quantize(z_w[0, 0, 0], z_s[0, 0][:, :QUARTER], woven0[0])
-        for s, h in ((5, 0), (5, 1)):
-            add_slot(nc.gpsimd, s, HALF * h, HALF * (h + 1))
+        for m0, m1 in ((0, QUARTER), (QUARTER, HALF), (HALF, T2)):
+            add_slot(nc.gpsimd, 5, m0, m1)
         place(7)
 
         units = [(h, n) for h in range(2) for n in range(N // P)]
@@ -395,7 +395,7 @@ def tile_list_feed_slot_ranking_kernel(
         finish(1)
         round_sums(nc.scalar.copy, 1, QUARTER, HALF)
         z_w[0, 1] = new("z_w01", [P, HALF], U32, tag="silu0")[:]
-        quantize(z_w[0, 1], z_s[0, 1][:], z_bf0[:, 4 * QUARTER :])
+        quantize(z_w[0, 1], z_s[0, 1][:], z_bf0[:])
         quantize_z(1, 1, 0, HALF)
         for k in range(2, len(units)):
             if k >= 4:

@@ -23,12 +23,10 @@ PASS = 512
 BANK = 512
 AL = 64
 PAGE_OF = (0, 1, 2, 3, 0, 1, 2, 0)
-ROW_OF = (0, 1, 2, 3, 2, 3, 0, 1)
 HALF = T2 // 2
 QUARTER = T2 // 4
+STRIP = T2 + QUARTER
 GATE_BANK = (6, 7, 0, 1, 5, 6, 7, 5)
-FIRST_CUTS = (0, 128, 256, 512)
-WF_FRONT = 512
 
 
 def tile_list_feed_slot_ranking_kernel(
@@ -78,18 +76,16 @@ def tile_list_feed_slot_ranking_kernel(
             )
             return raw
 
-        slot_sb = {}
-
         def load_slot(s, dst, m0=0, m1=T2):
-            b, t = s // 4, ROW_OF[s]
-            rows = slot[PASS * b : PASS * (b + 1), m0:m1].rearrange("(p i) m -> p i m", i=4)
-            nc.sync.dma_start(out=dst, in_=rows[:, t, :])
-            for h in range(m0 // HALF, m1 // HALF):
-                slot_sb[s, h] = dst[:, HALF * h - m0 : HALF * (h + 1) - m0]
+            rows = slot[PASS * (s // 4) : PASS * (s // 4 + 1), m0:m1].rearrange("(p i) m -> p i m", i=4)
+            nc.sync.dma_start(out=dst, in_=rows[:, s % 4, :])
+
+        slot_sb = {}
 
         def load_slots(first):
             for s in range(first, first + 2):
-                load_slot(s, new(f"slot{s}", [P, T2], F32, tag=f"slot{s % 4}")[:])
+                slot_sb[s] = new(f"slot{s}", [P, T2], F32)
+                load_slot(s, slot_sb[s][:])
 
         def load_wf(b):
             raw = new(f"wf_raw{b}", [P, 4, N], F32)
@@ -130,7 +126,6 @@ def tile_list_feed_slot_ranking_kernel(
         load_slots(2)
         w8_w = new("w8_w", [P, 2, N], U32)
         nc.sync.dma_start(out=w8_w[:].bitcast(I32), in_=w8_words.rearrange("a p n i -> p a (n i)").bitcast(I32))
-        load_scale_rows(nc.sync, w8_s, w8_scales)
 
         v_w = [new(f"v_w{a}", [P, S], U32) for a in range(2)]
         v_s = [new(f"v_s{a}", [P, S], U8) for a in range(2)]
@@ -176,7 +171,7 @@ def tile_list_feed_slot_ranking_kernel(
                 nc.scalar.activation(tanh_b[b, jb], banks[jb][:].rearrange("j (m t) -> j t m", t=4), ACT.Tanh)
 
         def weigh(s, dst, bank):
-            b, t = s // 4, ROW_OF[s]
+            b, t = s // 4, s % 4
             for jb in range(4):
                 nc.tensor.transpose(bank[:, P * jb : P * (jb + 1)], tanh_b[b, jb][:, t, :], ident[:])
             factor[s] = dst
@@ -186,7 +181,7 @@ def tile_list_feed_slot_ranking_kernel(
             return new(name, [P, S], F32, tag=tag)[:]
 
         def gate_pass(s, a):
-            b, t = s // 4, ROW_OF[s]
+            b, t = s // 4, s % 4
             cols = slice(PASS * a + P * t, PASS * a + P * (t + 1))
             mx(banks[GATE_BANK[s]][:], wg_w[b][:, cols], wg_s[b][:, cols], v_w[a][:].bitcast(FP8X4), v_s[a][:], a == 0, a == 1)
 
@@ -204,13 +199,12 @@ def tile_list_feed_slot_ranking_kernel(
         def place(s):
             nc.vector.tensor_copy(pages[PAGE_OF[s]][:].indirect(idx2[:]), weighted[s])
 
-        def add_turned(first, tag, by_bank):
-            turned = new(f"turned{first}", [P, 8, P, 2], BF16, tag=tag)
+        def add_turned(first, by_bank):
             steps = [(step, c) for step in range(4) for c in range(8)]
             for step, c in sorted(steps, key=lambda sc: sc[1] // 2) if by_bank else steps:
                 s = first + step % 2
                 if (step < 2) == by_bank:
-                    source = slot_sb[s, c // 4][:, P * (c % 4) : P * (c % 4 + 1)]
+                    source = slot_sb[s][:, P * c : P * (c + 1)]
                 else:
                     source = pages[PAGE_OF[s]][:, P * c : P * (c + 1)]
                 column = P * (2 * (c % 2) + step % 2)
@@ -218,47 +212,26 @@ def tile_list_feed_slot_ranking_kernel(
                     banks[4 + c // 2][:, column : column + P], source, ident[:],
                     start=(step == 0 and c % 2 == 0), stop=(step == 3 and c % 2 == 1), is_transpose=True,
                 )
-            for g in range(4):
-                nc.scalar.copy(
-                    turned[:, 2 * g : 2 * g + 2], banks[4 + g][:].rearrange("m (c e p) -> m c p e", c=2, e=2)
-                )
-            return turned[:].rearrange("m c p e -> m c (p e)").bitcast(F32)
 
-        sums0 = new("sums0", [P, 4 * HALF + QUARTER], F32)
-        sums = {0: sums0[:, : 4 * HALF].rearrange("p (t m) -> p t m", t=4)}
+        def round_turned(turned, g):
+            dst = turned[g].bitcast(BF16).rearrange("m (c p e) -> m c p e", c=2, e=2)
+            nc.scalar.copy(dst, banks[4 + g][:].rearrange("m (c e p) -> m c p e", c=2, e=2))
 
-        def add_slot(engine, s, m0, m1):
-            h = m0 // HALF
-            cols = slice(m0 - HALF * h, m1 - HALF * h)
-            engine.tensor_tensor(sums[h][:, ROW_OF[s], cols], pages[PAGE_OF[s]][:, m0:m1], slot_sb[s, h][:, cols], ADD)
+        wf_bf = [new(f"wf_bf{b}", [P, 4 * N], BF16) for b in range(2)]
+        wf_w = {}
+        wf_s = [new(f"wf_s{b}", [P, N], U8) for b in range(2)]
 
-        z_bf, z_w = {}, {}
-        z_s = {(b, h): new(f"z_s{b}{h}", [P, HALF], U8) for b in range(2) for h in range(2)}
+        def weave(copy, dst, src):
+            copy(dst.rearrange("p (c i j) -> p c j i", i=4, j=4), src.rearrange("p j (c i) -> p c j i", i=4))
 
-        def round_sums(copy, h, m0, m1):
-            dst = z_bf[1, h][:, 4 * m0 : 4 * m1].rearrange("p (c i j) -> p c j i", i=4, j=4)
-            copy(dst, sums[h][:, :, m0:m1].rearrange("p j (c i) -> p c j i", i=4))
+        def round_wf(b):
+            for c in range(0, N, QUARTER):
+                weave(nc.scalar.copy, wf_bf[b][:, 4 * c : 4 * (c + QUARTER)], wf_raw[b][:, :, c : c + QUARTER])
 
-        def z_words(b, h, m0, m1):
-            if (b, h) == (0, 0):
-                q = m0 // QUARTER
-                return z_w[0, 0, q][:, m0 - QUARTER * q : m1 - QUARTER * q]
-            return z_w[b, h][:, m0:m1]
-
-        def quantize_z(b, h, m0, m1):
-            quantize(z_words(b, h, m0, m1), z_s[b, h][:, m0:m1], z_bf[b, h][:, 4 * m0 : 4 * m1])
-
-        widths = (WF_FRONT, N - WF_FRONT)
-        wf_bf = [new(f"wf_bf{part}", [P, 8 * widths[part]], BF16) for part in range(2)]
-        wf_w = []
-        wf_s = [new(f"wf_s{part}", [P, 2 * widths[part]], U8) for part in range(2)]
-
-        def round_wf(b, part):
-            width = widths[part]
-            dst = wf_bf[part][:, 4 * width * b : 4 * width * (b + 1)].rearrange("p (c i j) -> p c j i", i=4, j=4)
-            src = wf_raw[b][:, :, WF_FRONT * part : WF_FRONT * part + width].rearrange("p j (c i) -> p c j i", i=4)
-            for c in range(0, width // 4, QUARTER // 4):
-                nc.scalar.copy(dst[:, c : c + QUARTER // 4], src[:, c : c + QUARTER // 4])
+        def quantize_wf(b, pair, words):
+            wf_w[b, pair] = words
+            n0, n1 = QUARTER * pair, QUARTER * (pair + 1)
+            quantize(words, wf_s[b][:, n0:n1], wf_bf[b][:, 4 * n0 : 4 * n1])
 
         features(0)
         rounded = [new(f"wg_bf0{a}", [P, 4 * PASS], BF16) for a in range(2)]
@@ -296,119 +269,172 @@ def tile_list_feed_slot_ranking_kernel(
         place(3)
         for s in range(4, 8):
             multiply(s, gate[s])
-        for part in range(2):
-            round_wf(0, part)
-        turned0 = [add_turned(0, "wf_raw0", False)]
+        round_wf(0)
+        low = new("turned_low", [P, 4, QUARTER], F32, tag="wf_raw0")
+        turned = [[low[:, g, :] for g in range(4)]]
+        add_turned(0, False)
+        for g in range(4):
+            round_turned(turned[0], g)
         place(4)
+        wf_w[0, 0] = new("wf_w00", [P, HALF], U32, tag="gate4")[:]
+        wf_w[0, 1] = wf_w[0, 0][:, QUARTER:]
+        quantize(wf_w[0, 0], wf_s[0][:, :HALF], wf_bf[0][:, : 4 * HALF])
         place(5)
-        for part in range(2):
-            round_wf(1, part)
-        turned0.append(add_turned(2, "wf_raw1", True))
-        second = new("second", [P, 4, HALF], F32, tag="raw10")
-        load_slot(6, row("first6"), 0, HALF)
-        load_slot(7, sums[0][:, ROW_OF[7], :], 0, HALF)
-        for s in range(4, 8):
-            if s < 6:
-                load_slot(s, sums[0][:, ROW_OF[s], :] if s == 4 else row("first5"), 0, HALF)
-            load_slot(s, second[:, s - 4, :], HALF, T2)
-        z_bf0 = new("z_bf0", [P, 4 * HALF], BF16, tag="raw01")
-        woven0 = [sums0[:, 4 * HALF - QUARTER :].bitcast(BF16), sums0[:, :HALF].bitcast(BF16)]
-        woven0 += [z_bf0[:, 4 * QUARTER * q : 4 * QUARTER * (q + 1)] for q in range(2)]
+        round_wf(1)
+        add_turned(2, True)
+
+        load_scale_rows(nc.sync, w8_s, w8_scales)
+        sums_tile = new("sums", [P, 4 * STRIP], F32, tag="tab_w1")
+        sums = sums_tile[:].rearrange("p (t m) -> p t m", t=4)
+        aside = new("aside", [P, HALF + 3 * QUARTER], F32, tag="raw00")
+        late5, late6 = aside[:, :HALF], aside[:, HALF:]
+        first6 = sums[:, 1, HALF : HALF + QUARTER]
+        last4 = sums[:, 2, P : P + QUARTER]
+        late7 = sums[:, 2, P + QUARTER : P + T2]
+        load_slot(6, first6, 0, QUARTER)
+        load_slot(5, late5, HALF, T2)
+        load_slot(6, late6, QUARTER, T2)
+        load_slot(7, sums[:, 3, :QUARTER], 0, QUARTER)
+        load_slot(7, late7, QUARTER, T2)
+        load_slot(4, sums[:, 0, : 3 * QUARTER], 0, 3 * QUARTER)
+        load_slot(5, sums[:, 1, :HALF], 0, HALF)
+        load_slot(4, last4, 3 * QUARTER, T2)
+
+        def add_slot(engine, s, m0, m1, rows=None):
+            dst = sums[:, s % 4, m0:m1]
+            engine.tensor_tensor(dst, pages[PAGE_OF[s]][:, m0:m1], dst if rows is None else rows, ADD)
+
+        z_bf0 = new("z_bf0", [P, 3 * T2], BF16, tag="raw01")
+        woven0 = [sums_tile[:, 2 * STRIP - 3 * P : 2 * STRIP + P].bitcast(BF16)]
+        woven0 += [z_bf0[:, T2 * q : T2 * (q + 1)] for q in range(3)]
+        high = new("turned_high", [P, 3, QUARTER], F32, tag="wf_raw1")
+        turned.append([high[:, g, :] for g in range(3)] + [sums[:, 0, 3 * QUARTER : T2]])
+        for g in range(4):
+            round_turned(turned[1], g)
         for q in range(4):
             for u in range(2):
                 for c in range(2):
                     column = P * (2 * u + c)
-                    nc.tensor.transpose(banks[q][:, column : column + P], turned0[u][:, 2 * q + c, :], ident[:])
+                    nc.tensor.transpose(banks[q][:, column : column + P], turned[u][q][:, P * c : P * (c + 1)], ident[:])
             nc.scalar.copy(
                 woven0[q].bitcast(F32).rearrange("p (m u) -> p m u", u=2), banks[q][:].rearrange("p (u m) -> p m u", u=2)
             )
-        nc.scalar.activation(warm[:, 8:16], woven0[2][:, 4 * QUARTER - 8 :], ACT.Silu)
-        wf_w.append(new("wf_w0", [P, 2 * WF_FRONT], U32, tag="gate5")[:])
-        quantize(wf_w[0][:], wf_s[0][:], wf_bf[0][:])
-        sums1 = new("sums1", [P, 4 * HALF], F32, tag="wf_bf0")
-        sums[1] = sums1[:].rearrange("p (t m) -> p t m", t=4)
-        for s, h in ((4, 0), (4, 1)):
-            add_slot(nc.gpsimd, s, HALF * h, HALF * (h + 1))
+        nc.scalar.activation(warm[:, 8:16], woven0[3][:, T2 - 8 :], ACT.Silu)
+        for s, m0, m1 in ((4, 0, HALF), (4, HALF, 3 * QUARTER), (5, 0, HALF)):
+            add_slot(nc.gpsimd, s, m0, m1)
+        add_slot(nc.gpsimd, 4, 3 * QUARTER, T2, last4)
         place(6)
-        z_w[0, 0, 0] = new("z_w000", [P, QUARTER], U32, tag="gate6")[:]
-        quantize(z_w[0, 0, 0], z_s[0, 0][:, :QUARTER], woven0[0])
-        for m0, m1 in ((0, QUARTER), (QUARTER, HALF), (HALF, T2)):
-            add_slot(nc.gpsimd, 5, m0, m1)
+        z_s = [new(f"z_s{b}", [P, T2], U8) for b in range(2)]
+        z_w = {}
+
+        def quantize_z0(q, words):
+            z_w[0, q] = words
+            quantize(words, z_s[0][:, QUARTER * q : QUARTER * (q + 1)], woven0[q])
+
+        after6 = new("after6", [P, HALF], U32, tag="gate6")
+        quantize_z0(0, after6[:, :QUARTER])
+        quantize_wf(0, 2, after6[:, QUARTER:])
+        add_slot(nc.gpsimd, 6, 0, QUARTER, first6)
+        add_slot(nc.gpsimd, 5, HALF, T2, late5)
         place(7)
 
-        units = [(h, n) for h in range(2) for n in range(N // P)]
+        units = [(q, pair) for q in range(4) for pair in range(N // QUARTER)]
+        last = len(units) - 1
 
-        def bank_of(k, i, m0):
-            if k == len(units) - 1 and m0 >= QUARTER:
+        def bank_of(k, i, e):
+            if k == last and e == 1:
                 return banks[i]
             return banks[2 * (k % 4) + i]
 
-        def product(k, b, m0, m1, start, stop, which=(0, 1)):
-            h, n = units[k]
-            part, first = divmod(P * n, WF_FRONT)
-            wf_cols = slice(widths[part] * b + first, widths[part] * b + first + P)
-            cols = slice(P * n, P * (n + 1))
-            weights = ((wf_w[part][:, wf_cols], wf_s[part][:, wf_cols]), (w8_w[:, b, cols], w8_s[:, b, cols]))
-            for i in which:
-                mx(
-                    bank_of(k, i, m0)[:, m0:m1], weights[i][0], weights[i][1],
-                    z_words(b, h, m0, m1).bitcast(FP8X4), z_s[b, h][:, m0:m1], start, stop,
-                )
+        def product(k, b, i, e, c0, c1, start, stop):
+            q, pair = units[k]
+            cols = slice(QUARTER * pair + P * e, QUARTER * pair + P * (e + 1))
+            words, plane = ((wf_w[b, pair][:, P * e : P * (e + 1)], wf_s[b][:, cols]), (w8_w[:, b, cols], w8_s[:, b, cols]))[i]
+            mx(
+                bank_of(k, i, e)[:, QUARTER * e + c0 : QUARTER * e + c1], words, plane,
+                z_w[b, q][:, c0:c1].bitcast(FP8X4), z_s[b][:, QUARTER * q + c0 : QUARTER * q + c1], start, stop,
+            )
+
+        def passes(k, b, c0, c1, first, final):
+            for i in range(2):
+                for e in range(2):
+                    product(k, b, i, e, c0, c1, first and e == 0, final and e == 1)
 
         def finish(k):
-            h, n = units[k]
-            silu = row(f"silu{k}", f"gate{k % 4}" if k else None)
+            q, pair = units[k]
+            silu = row(f"silu{k}", f"silu_{k}" if k in (0, 1, 3, 4) else f"gate{k % 4}")
             result = row(f"result{k}", f"tanh{k // 4 % 2}{k % 4}")
-            width = QUARTER if k == len(units) - 1 else HALF
-            for c in range(0, HALF, width):
-                nc.scalar.activation(silu[:, c : c + width], bank_of(k, 0, c)[:, c : c + width], ACT.Silu)
-            for c in range(0, HALF, width):
-                cols = slice(c, c + width)
-                nc.vector.tensor_tensor(result[:, cols], bank_of(k, 1, c)[:, cols], silu[:, cols], MULT)
-                nc.sync.dma_start(out=out[P * n : P * (n + 1), HALF * h + c : HALF * h + c + width], in_=result[:, cols])
+            rows = out[QUARTER * pair : QUARTER * (pair + 1), QUARTER * q : QUARTER * (q + 1)].rearrange("(e p) m -> p e m", e=2)
+            if k < last:
+                nc.scalar.activation(silu, bank_of(k, 0, 0)[:], ACT.Silu)
+                nc.vector.tensor_tensor(result, bank_of(k, 1, 0)[:], silu, MULT)
+                nc.sync.dma_start(out=rows, in_=result.rearrange("p (e m) -> p e m", e=2))
+                return
+            halves = [slice(QUARTER * e, QUARTER * (e + 1)) for e in range(2)]
+            for e in range(2):
+                nc.scalar.activation(silu[:, halves[e]], bank_of(k, 0, e)[:, halves[e]], ACT.Silu)
+            for e in range(2):
+                nc.vector.tensor_tensor(result[:, halves[e]], bank_of(k, 1, e)[:, halves[e]], silu[:, halves[e]], MULT)
+                nc.sync.dma_start(out=rows[:, e, :], in_=result[:, halves[e]])
 
-        for k in range(4):
-            product(k, 0, 0, QUARTER, True, False)
-        z_w[0, 0, 1] = new("z_w001", [P, QUARTER], U32, tag="gate7")[:]
-        quantize(z_w[0, 0, 1], z_s[0, 0][:, QUARTER:], woven0[1])
-        for k in range(4):
-            product(k, 0, QUARTER, HALF, False, False)
-        z_bf[1, 0] = sums1[:, : 2 * HALF].bitcast(BF16)
-        z_w[1, 0] = new("z_w10", [P, HALF], U32)[:]
-        z_w[1, 1] = new("z_w11", [P, HALF], U32)[:]
-        cuts = list(zip(FIRST_CUTS, FIRST_CUTS[1:]))
-        for m0, m1 in cuts:
-            for s in (6, 7):
-                add_slot(nc.vector, s, m0, m1)
-            round_sums(nc.scalar.copy, 0, m0, m1)
-        wf_w.append(new("wf_w1", [P, 2 * widths[1]], U32, tag="first6")[:])
-        quantize(wf_w[1], wf_s[1][:], wf_bf[1][:])
-        for m0, m1 in cuts:
-            quantize_z(1, 0, m0, m1)
-            for k in range(4):
-                product(k, 1, m0, m1, False, m1 == HALF)
-        for s in (6, 7):
-            add_slot(nc.vector, s, HALF, T2)
-        z_bf[1, 1] = new("z_bf11", [P, 4 * HALF], BF16, tag="factor4")
-        round_sums(nc.vector.tensor_copy, 1, 0, QUARTER)
-        finish(0)
-        finish(1)
-        round_sums(nc.scalar.copy, 1, QUARTER, HALF)
-        z_w[0, 1] = new("z_w01", [P, HALF], U32, tag="silu0")[:]
-        quantize(z_w[0, 1], z_s[0, 1][:], z_bf0[:])
-        quantize_z(1, 1, 0, HALF)
-        for k in range(2, len(units)):
+        woven1 = {
+            0: new("woven1_0", [P, 4 * P], BF16)[:],
+            P: sums[:, 3, HALF : HALF + QUARTER].bitcast(BF16),
+            QUARTER: sums[:, 3, HALF + QUARTER :].bitcast(BF16),
+        }
+
+        def round_z(m0, m1):
+            weave(nc.scalar.copy, woven1[m0], sums[:, :, m0:m1])
+
+        def quantize_z1(m0, m1):
+            q = m0 // QUARTER
+            quantize(z_w[1, q][:, m0 - QUARTER * q : m1 - QUARTER * q], z_s[1][:, m0:m1], woven1[m0])
+
+        for q in range(4):
+            z_w[1, q] = new(f"z_w1{q}", [P, QUARTER], U32)
+        for k in range(3):
+            passes(k, 0, 0, QUARTER, True, False)
+        for m0 in range(0, QUARTER, P):
+            add_slot(nc.vector, 7, m0, m0 + P)
+            round_z(m0, m0 + P)
+        after7 = new("after7", [P, 4, QUARTER], U32, tag="gate7")
+        quantize_z0(1, after7[:, 3, :])
+        passes(3, 0, 0, QUARTER, True, False)
+        quantize_wf(1, 0, after7[:, 0, :])
+        add_slot(nc.vector, 7, QUARTER, HALF, late7[:, :QUARTER])
+        add_slot(nc.vector, 6, QUARTER, HALF, late6[:, :QUARTER])
+        round_z(QUARTER, HALF)
+        quantize_z1(0, P)
+        quantize_wf(1, 1, after7[:, 1, :])
+        quantize_wf(1, 2, after7[:, 2, :])
+        for k in range(3):
+            passes(k, 1, 0, P, False, False)
+        quantize_z1(P, QUARTER)
+        for k in range(3):
+            passes(k, 1, P, QUARTER, False, True)
+        quantize_z1(QUARTER, HALF)
+        passes(3, 1, 0, QUARTER, False, True)
+        for k in range(len(units)):
+            q, pair = units[k]
             if k >= 4:
                 for i in range(2):
-                    if k == len(units) - 1:
-                        for m0 in range(0, HALF, QUARTER):
-                            product(k, 0, m0, m0 + QUARTER, True, False, (i,))
-                            product(k, 1, m0, m0 + QUARTER, False, True, (i,))
+                    if k == last:
+                        for e in range(2):
+                            for b in range(2):
+                                product(k, b, i, e, 0, QUARTER, b == 0, b == 1)
                         continue
-                    if units[k][0] == 0:
-                        product(k, 0, 0, QUARTER, True, False, (i,))
-                        product(k, 0, QUARTER, HALF, False, False, (i,))
-                    else:
-                        product(k, 0, 0, HALF, True, False, (i,))
-                    product(k, 1, 0, HALF, False, True, (i,))
+                    for b in range(2):
+                        for e in range(2):
+                            product(k, b, i, e, 0, QUARTER, b == 0 and e == 0, b == 1 and e == 1)
             finish(k)
+            if k in (0, 3):
+                ahead = 2 + k // 3
+                m0, m1 = QUARTER * ahead, QUARTER * (ahead + 1)
+                add_slot(nc.vector, 7, m0, m1, late7[:, m0 - QUARTER : m1 - QUARTER])
+                add_slot(nc.vector, 6, m0, m1, late6[:, m0 - QUARTER : m1 - QUARTER])
+            if k in (1, 4):
+                ahead = 2 + k // 3
+                woven1[QUARTER * ahead] = new(f"woven1_{ahead}", [P, T2], BF16, tag=f"silu_{k - 1}")[:]
+                round_z(QUARTER * ahead, QUARTER * (ahead + 1))
+                quantize_z0(ahead, new(f"z_w0{ahead}", [P, QUARTER], U32, tag=f"silu_{k}")[:])
+                quantize_z1(QUARTER * ahead, QUARTER * (ahead + 1))

@@ -25,7 +25,8 @@ AL = 64
 PAGE_OF = (0, 1, 2, 3, 0, 1, 2, 0)
 HALF = T2 // 2
 QUARTER = T2 // 4
-STRIP = T2 + QUARTER
+GAP = 3 * P
+STRIP = T2 + GAP
 GATE_BANK = (6, 7, 0, 1, 5, 6, 7, 5)
 
 
@@ -217,7 +218,11 @@ def tile_list_feed_slot_ranking_kernel(
             dst = turned[g].bitcast(BF16).rearrange("m (c p e) -> m c p e", c=2, e=2)
             nc.scalar.copy(dst, banks[4 + g][:].rearrange("m (c e p) -> m c p e", c=2, e=2))
 
-        wf_bf = [new(f"wf_bf{b}", [P, 4 * N], BF16) for b in range(2)]
+        sums_tile = new("sums", [P, 4 * STRIP], F32, tag="tab_w1")
+        sums = sums_tile[:].rearrange("p (t m) -> p t m", t=4)[:, :, :T2]
+        wf_front = sums[:, 0, :T2].bitcast(BF16)
+        wf_rest = new("wf_rest", [P, 4, T2], BF16)
+        wf_bf = [[wf_front[:, :T2], wf_front[:, T2:], wf_rest[:, 0, :]], [wf_rest[:, 1 + pair, :] for pair in range(3)]]
         wf_w = {}
         wf_s = [new(f"wf_s{b}", [P, N], U8) for b in range(2)]
 
@@ -225,13 +230,13 @@ def tile_list_feed_slot_ranking_kernel(
             copy(dst.rearrange("p (c i j) -> p c j i", i=4, j=4), src.rearrange("p j (c i) -> p c j i", i=4))
 
         def round_wf(b):
-            for c in range(0, N, QUARTER):
-                weave(nc.scalar.copy, wf_bf[b][:, 4 * c : 4 * (c + QUARTER)], wf_raw[b][:, :, c : c + QUARTER])
+            for pair in range(3):
+                weave(nc.scalar.copy, wf_bf[b][pair], wf_raw[b][:, :, QUARTER * pair : QUARTER * (pair + 1)])
 
         def quantize_wf(b, pair, words):
             wf_w[b, pair] = words
             n0, n1 = QUARTER * pair, QUARTER * (pair + 1)
-            quantize(words, wf_s[b][:, n0:n1], wf_bf[b][:, 4 * n0 : 4 * n1])
+            quantize(words, wf_s[b][:, n0:n1], wf_bf[b][pair])
 
         features(0)
         rounded = [new(f"wg_bf0{a}", [P, 4 * PASS], BF16) for a in range(2)]
@@ -278,25 +283,21 @@ def tile_list_feed_slot_ranking_kernel(
         place(4)
         wf_w[0, 0] = new("wf_w00", [P, HALF], U32, tag="gate4")[:]
         wf_w[0, 1] = wf_w[0, 0][:, QUARTER:]
-        quantize(wf_w[0, 0], wf_s[0][:, :HALF], wf_bf[0][:, : 4 * HALF])
+        quantize(wf_w[0, 0], wf_s[0][:, :HALF], wf_front)
         place(5)
         round_wf(1)
         add_turned(2, True)
 
         load_scale_rows(nc.sync, w8_s, w8_scales)
-        sums_tile = new("sums", [P, 4 * STRIP], F32, tag="tab_w1")
-        sums = sums_tile[:].rearrange("p (t m) -> p t m", t=4)
-        aside = new("aside", [P, HALF + 3 * QUARTER], F32, tag="raw00")
-        late5, late6 = aside[:, :HALF], aside[:, HALF:]
-        first6 = sums[:, 1, HALF : HALF + QUARTER]
+        aside = new("aside", [P, T2 + 3 * QUARTER], F32, tag="raw00")
+        first6, late5, first4 = aside[:, :HALF], aside[:, HALF:T2], aside[:, T2:]
         last4 = sums[:, 2, P : P + QUARTER]
-        late7 = sums[:, 2, P + QUARTER : P + T2]
-        load_slot(6, first6, 0, QUARTER)
-        load_slot(5, late5, HALF, T2)
-        load_slot(6, late6, QUARTER, T2)
-        load_slot(7, sums[:, 3, :QUARTER], 0, QUARTER)
-        load_slot(7, late7, QUARTER, T2)
-        load_slot(4, sums[:, 0, : 3 * QUARTER], 0, 3 * QUARTER)
+        late = {5: late5, 6: sums[:, 1, HALF:T2], 7: sums[:, 2, HALF:T2]}
+        load_slot(6, first6, 0, HALF)
+        load_slot(7, sums[:, 3, :HALF], 0, HALF)
+        for s in late:
+            load_slot(s, late[s], HALF, T2)
+        load_slot(4, first4, 0, 3 * QUARTER)
         load_slot(5, sums[:, 1, :HALF], 0, HALF)
         load_slot(4, last4, 3 * QUARTER, T2)
 
@@ -305,7 +306,7 @@ def tile_list_feed_slot_ranking_kernel(
             engine.tensor_tensor(dst, pages[PAGE_OF[s]][:, m0:m1], dst if rows is None else rows, ADD)
 
         z_bf0 = new("z_bf0", [P, 3 * T2], BF16, tag="raw01")
-        woven0 = [sums_tile[:, 2 * STRIP - 3 * P : 2 * STRIP + P].bitcast(BF16)]
+        woven0 = [sums_tile[:, 2 * STRIP - GAP : 2 * STRIP + HALF - GAP].bitcast(BF16)]
         woven0 += [z_bf0[:, T2 * q : T2 * (q + 1)] for q in range(3)]
         high = new("turned_high", [P, 3, QUARTER], F32, tag="wf_raw1")
         turned.append([high[:, g, :] for g in range(3)] + [sums[:, 0, 3 * QUARTER : T2]])
@@ -320,8 +321,9 @@ def tile_list_feed_slot_ranking_kernel(
                 woven0[q].bitcast(F32).rearrange("p (m u) -> p m u", u=2), banks[q][:].rearrange("p (u m) -> p m u", u=2)
             )
         nc.scalar.activation(warm[:, 8:16], woven0[3][:, T2 - 8 :], ACT.Silu)
-        for s, m0, m1 in ((4, 0, HALF), (4, HALF, 3 * QUARTER), (5, 0, HALF)):
-            add_slot(nc.gpsimd, s, m0, m1)
+        for m0, m1 in ((0, HALF), (HALF, 3 * QUARTER)):
+            add_slot(nc.gpsimd, 4, m0, m1, first4[:, m0:m1])
+        add_slot(nc.gpsimd, 5, 0, HALF)
         add_slot(nc.gpsimd, 4, 3 * QUARTER, T2, last4)
         place(6)
         z_s = [new(f"z_s{b}", [P, T2], U8) for b in range(2)]
@@ -334,8 +336,7 @@ def tile_list_feed_slot_ranking_kernel(
         after6 = new("after6", [P, HALF], U32, tag="gate6")
         quantize_z0(0, after6[:, :QUARTER])
         quantize_wf(0, 2, after6[:, QUARTER:])
-        add_slot(nc.gpsimd, 6, 0, QUARTER, first6)
-        add_slot(nc.gpsimd, 5, HALF, T2, late5)
+        add_slot(nc.gpsimd, 6, 0, HALF, first6)
         place(7)
 
         units = [(q, pair) for q in range(4) for pair in range(N // QUARTER)]
@@ -377,11 +378,8 @@ def tile_list_feed_slot_ranking_kernel(
                 nc.vector.tensor_tensor(result[:, halves[e]], bank_of(k, 1, e)[:, halves[e]], silu[:, halves[e]], MULT)
                 nc.sync.dma_start(out=rows[:, e, :], in_=result[:, halves[e]])
 
-        woven1 = {
-            0: new("woven1_0", [P, 4 * P], BF16)[:],
-            P: sums[:, 3, HALF : HALF + QUARTER].bitcast(BF16),
-            QUARTER: sums[:, 3, HALF + QUARTER :].bitcast(BF16),
-        }
+        front1 = new("woven1_front", [P, 4 * HALF], BF16, tag="raw10")
+        woven1 = {m0: front1[:, 4 * m0 : 4 * m1] for m0, m1 in ((0, P), (P, QUARTER), (QUARTER, HALF))}
 
         def round_z(m0, m1):
             weave(nc.scalar.copy, woven1[m0], sums[:, :, m0:m1])
@@ -394,15 +392,14 @@ def tile_list_feed_slot_ranking_kernel(
             z_w[1, q] = new(f"z_w1{q}", [P, QUARTER], U32)
         for k in range(3):
             passes(k, 0, 0, QUARTER, True, False)
-        for m0 in range(0, QUARTER, P):
-            add_slot(nc.vector, 7, m0, m0 + P)
-            round_z(m0, m0 + P)
         after7 = new("after7", [P, 4, QUARTER], U32, tag="gate7")
         quantize_z0(1, after7[:, 3, :])
         passes(3, 0, 0, QUARTER, True, False)
+        for m0 in range(0, QUARTER, P):
+            add_slot(nc.vector, 7, m0, m0 + P)
+            round_z(m0, m0 + P)
+        add_slot(nc.vector, 7, QUARTER, HALF)
         quantize_wf(1, 0, after7[:, 0, :])
-        add_slot(nc.vector, 7, QUARTER, HALF, late7[:, :QUARTER])
-        add_slot(nc.vector, 6, QUARTER, HALF, late6[:, :QUARTER])
         round_z(QUARTER, HALF)
         quantize_z1(0, P)
         quantize_wf(1, 1, after7[:, 1, :])
@@ -430,8 +427,8 @@ def tile_list_feed_slot_ranking_kernel(
             if k in (0, 3):
                 ahead = 2 + k // 3
                 m0, m1 = QUARTER * ahead, QUARTER * (ahead + 1)
-                add_slot(nc.vector, 7, m0, m1, late7[:, m0 - QUARTER : m1 - QUARTER])
-                add_slot(nc.vector, 6, m0, m1, late6[:, m0 - QUARTER : m1 - QUARTER])
+                for s in (7, 6, 5):
+                    add_slot(nc.vector, s, m0, m1, late[s][:, m0 - HALF : m1 - HALF])
             if k in (1, 4):
                 ahead = 2 + k // 3
                 woven1[QUARTER * ahead] = new(f"woven1_{ahead}", [P, T2], BF16, tag=f"silu_{k - 1}")[:]

@@ -27,7 +27,7 @@ HALF = T2 // 2
 QUARTER = T2 // 4
 GAP = 3 * P
 STRIP = T2 + GAP
-GATE_BANK = (6, 7, 0, 1, 5, 6, 7, 5)
+GATE_BANK = (6, 7, 4, 5, 6, 7, 4, 5)
 
 
 def tile_list_feed_slot_ranking_kernel(
@@ -47,19 +47,20 @@ def tile_list_feed_slot_ranking_kernel(
         idx = lists.tile([P, S // 16], U16, name="idx")
         idx2 = lists.tile([P, S // 16], U16, name="idx2")
 
-        def load_scale_rows(queue, plane, scales):
+        def load_scale_rows(plane, scales, c0, c1):
             for q in range(4):
-                queue.dma_start(
+                nc.sync.dma_start(
                     out=plane[32 * q : 32 * q + 4].bitcast(I32),
-                    in_=scales.bitcast(I32)[:, 4 * q : 4 * q + 4, :].rearrange("a r n -> r a n"),
+                    in_=scales.bitcast(I32)[:, 4 * q : 4 * q + 4, c0 // 4 : c1 // 4].rearrange("a r n -> r a n"),
                 )
 
         tab_s = new("tab_s", [P, 2, T], U8)
-        w4_s = new("w4_s", [P, 2, H], U8)
+        w4_s = [new(f"w4_s{b}", [P, 2, PASS], U8) for b in range(2)]
         w8_s = new("w8_s", [P, 2, N], U8)
         warm = new("warm", [P, 16], F32)
         nc.vector.memset(tab_s[:].bitcast(I32), 0)
-        nc.vector.memset(w4_s[:].bitcast(I32), 0)
+        for plane in w4_s:
+            nc.vector.memset(plane[:].bitcast(I32), 0)
         nc.vector.memset(warm[:, 0:8], 0.0)
         nc.vector.memset(w8_s[:].bitcast(I32), 0)
 
@@ -88,10 +89,11 @@ def tile_list_feed_slot_ranking_kernel(
                 slot_sb[s] = new(f"slot{s}", [P, T2], F32)
                 load_slot(s, slot_sb[s][:])
 
-        def load_wf(b):
-            raw = new(f"wf_raw{b}", [P, 4, N], F32)
-            nc.sync.dma_start(out=raw[:], in_=wf[PASS * b : PASS * (b + 1), :].rearrange("(p j) c -> p j c", j=4))
-            return raw
+        def load_wf(b, n0, n1):
+            raw = new(f"wf_raw{b}_{n0}", [P, 4, n1 - n0], F32)
+            nc.sync.dma_start(out=raw[:], in_=wf[PASS * b : PASS * (b + 1), n0:n1].rearrange("(p j) c -> p j c", j=4))
+            for n in range(n0, n1, QUARTER):
+                wf_raw[b, n // QUARTER] = raw[:, :, n - n0 : n - n0 + QUARTER]
 
         def load_tab(a):
             words = new(f"tab_w{a}", [P, T], U32)
@@ -104,12 +106,12 @@ def tile_list_feed_slot_ranking_kernel(
             nc.sync.dma_start(out=words[:].bitcast(I32), in_=part.rearrange("a p n -> p a n"))
             return words
 
-        nc.sync.dma_start(idx[:], offs)
         tab_w = [load_tab(0)]
-        load_scale_rows(nc.sync, tab_s, tab_scales)
+        nc.sync.dma_start(idx[:], offs)
+        load_scale_rows(tab_s, tab_scales, 0, T)
         w4_w = [load_w4(0)]
+        load_scale_rows(w4_s[0], w4_scales, 0, PASS)
         tab_w.append(load_tab(1))
-        load_scale_rows(nc.sync, w4_s, w4_scales)
         nc.scalar.activation(warm[:, 8:16], warm[:, 0:8], ACT.Sigmoid)
         wg_raw = {(0, 0): load_wg(0, 0)}
         wg_raw[0, 1] = load_wg(0, 1)
@@ -121,12 +123,13 @@ def tile_list_feed_slot_ranking_kernel(
         wg_raw[1, 0] = load_wg(1, 0)
         wg_raw[1, 1] = load_wg(1, 1)
         w4_w.append(load_w4(1))
-        wf_raw = [load_wf(0)]
+        load_scale_rows(w4_s[1], w4_scales, PASS, H)
+        wf_raw = {}
+        load_wf(0, 0, HALF)
         load_slots(0)
-        wf_raw.append(load_wf(1))
+        load_wf(0, HALF, N)
         load_slots(2)
-        w8_w = new("w8_w", [P, 2, N], U32)
-        nc.sync.dma_start(out=w8_w[:].bitcast(I32), in_=w8_words.rearrange("a p n i -> p a (n i)").bitcast(I32))
+        load_wf(1, 0, N)
 
         v_w = [new(f"v_w{a}", [P, S], U32) for a in range(2)]
         v_s = [new(f"v_s{a}", [P, S], U8) for a in range(2)]
@@ -139,13 +142,9 @@ def tile_list_feed_slot_ranking_kernel(
             pages.append(new(f"page{len(pages)}", [P, T2], F32, tag=tag))
             nc.gpsimd.memset(pages[-1][:], 0.0)
 
-        def round_wg(raw, rounded, vector_from):
-            dst = rounded.rearrange("p (t m j) -> p m j t", t=4, j=4)
+        def round_wg(copy, raw, rounded, t0=0, t1=4):
             src = raw[:].rearrange("p j (m t) -> p m j t", t=4)
-            if vector_from > 0:
-                nc.scalar.copy(dst[:, :vector_from], src[:, :vector_from])
-            if vector_from < P:
-                nc.vector.tensor_copy(dst[:, vector_from:], src[:, vector_from:])
+            copy(rounded.rearrange("p (t m j) -> p m j t", t=t1 - t0, j=4), src[:, :, :, t0:t1])
 
         def quantize(words, plane, rounded):
             nc.vector.quantize_mx(out=words.bitcast(FP8X4), scales=plane, in_=rounded)
@@ -159,16 +158,19 @@ def tile_list_feed_slot_ranking_kernel(
         wg_s = [new(f"wg_s{b}", [P, 2 * PASS], U8) for b in range(2)]
         tanh_b, factor, gate, weighted = {}, {}, {}, {}
 
-        def features(b):
+        def features(b, first=None):
             for a in range(2):
                 for jb in range(4):
                     entries = slice(P * jb, P * (jb + 1))
                     mx(
                         banks[jb][:], v_w[a][:, entries], v_s[a][:, entries], w4_w[b][:, a, :].bitcast(FP4X4),
-                        w4_s[:, a, PASS * b : PASS * (b + 1)], a == 0, a == 1,
+                        w4_s[b][:, a, :], a == 0, a == 1,
                     )
             for jb in range(4):
-                tanh_b[b, jb] = new(f"tanh{b}{jb}", [P, 4, P], F32)[:]
+                if jb == 0 and first is not None:
+                    tanh_b[b, jb] = first.rearrange("j (t m) -> j t m", t=4)
+                else:
+                    tanh_b[b, jb] = new(f"tanh{b}{jb}", [P, 4, P], F32)[:]
                 nc.scalar.activation(tanh_b[b, jb], banks[jb][:].rearrange("j (m t) -> j t m", t=4), ACT.Tanh)
 
         def weigh(s, dst, bank):
@@ -181,13 +183,17 @@ def tile_list_feed_slot_ranking_kernel(
         def row(name, tag=None):
             return new(name, [P, S], F32, tag=tag)[:]
 
-        def gate_pass(s, a):
+        def gate_pass(s, a, bank=None, entries=slice(0, S)):
             b, t = s // 4, s % 4
             cols = slice(PASS * a + P * t, PASS * a + P * (t + 1))
-            mx(banks[GATE_BANK[s]][:], wg_w[b][:, cols], wg_s[b][:, cols], v_w[a][:].bitcast(FP8X4), v_s[a][:], a == 0, a == 1)
+            bank = banks[GATE_BANK[s]] if bank is None else bank
+            mx(
+                bank[:, entries], wg_w[b][:, cols], wg_s[b][:, cols],
+                v_w[a][:, entries].bitcast(FP8X4), v_s[a][:, entries], a == 0, a == 1,
+            )
 
-        def sigmoid(s):
-            gate[s] = row(f"gate{s}")
+        def sigmoid(s, dst=None):
+            gate[s] = row(f"gate{s}") if dst is None else dst
             nc.scalar.activation(gate[s], banks[GATE_BANK[s]][:], ACT.Sigmoid)
 
         def scatter(s):
@@ -200,105 +206,134 @@ def tile_list_feed_slot_ranking_kernel(
         def place(s):
             nc.vector.tensor_copy(pages[PAGE_OF[s]][:].indirect(idx2[:]), weighted[s])
 
-        def add_turned(first, by_bank):
-            steps = [(step, c) for step in range(4) for c in range(8)]
-            for step, c in sorted(steps, key=lambda sc: sc[1] // 2) if by_bank else steps:
+        def add_turned(first, group):
+            for c, step in [(2 * g + e, step) for g in range(4) for step in range(4) for e in range(2)]:
                 s = first + step % 2
-                if (step < 2) == by_bank:
+                if step >= 2:
                     source = slot_sb[s][:, P * c : P * (c + 1)]
                 else:
                     source = pages[PAGE_OF[s]][:, P * c : P * (c + 1)]
                 column = P * (2 * (c % 2) + step % 2)
                 nc.tensor.matmul(
-                    banks[4 + c // 2][:, column : column + P], source, ident[:],
+                    group[c // 2][:, column : column + P], source, ident[:],
                     start=(step == 0 and c % 2 == 0), stop=(step == 3 and c % 2 == 1), is_transpose=True,
                 )
 
-        def round_turned(turned, g):
-            dst = turned[g].bitcast(BF16).rearrange("m (c p e) -> m c p e", c=2, e=2)
-            nc.scalar.copy(dst, banks[4 + g][:].rearrange("m (c e p) -> m c p e", c=2, e=2))
+        def round_turned(turned, bank):
+            dst = turned.bitcast(BF16).rearrange("m (c p e) -> m c p e", c=2, e=2)
+            nc.scalar.copy(dst, bank[:].rearrange("m (c e p) -> m c p e", c=2, e=2))
 
         sums_tile = new("sums", [P, 4 * STRIP], F32, tag="tab_w1")
         sums = sums_tile[:].rearrange("p (t m) -> p t m", t=4)[:, :, :T2]
-        wf_front = sums[:, 0, :T2].bitcast(BF16)
-        wf_rest = new("wf_rest", [P, 4, T2], BF16)
-        wf_bf = [[wf_front[:, :T2], wf_front[:, T2:], wf_rest[:, 0, :]], [wf_rest[:, 1 + pair, :] for pair in range(3)]]
+        wf_front = new("wf_front", [P, 2 * T2], BF16)
+        wf_rest = new("wf_rest", [P, 3, T2], BF16)
+        wf_bf = {(0, 0): wf_front[:, :T2], (0, 1): wf_front[:, T2:], (0, 2): wf_rest[:, 0, :]}
+        wf_bf.update({(1, pair): wf_rest[:, 1 + pair, :] for pair in range(2)})
         wf_w = {}
         wf_s = [new(f"wf_s{b}", [P, N], U8) for b in range(2)]
 
         def weave(copy, dst, src):
             copy(dst.rearrange("p (c i j) -> p c j i", i=4, j=4), src.rearrange("p j (c i) -> p c j i", i=4))
 
-        def round_wf(b):
-            for pair in range(3):
-                weave(nc.scalar.copy, wf_bf[b][pair], wf_raw[b][:, :, QUARTER * pair : QUARTER * (pair + 1)])
+        def round_wf(b, pair):
+            weave(nc.scalar.copy, wf_bf[b, pair], wf_raw[b, pair])
 
         def quantize_wf(b, pair, words):
             wf_w[b, pair] = words
             n0, n1 = QUARTER * pair, QUARTER * (pair + 1)
-            quantize(words, wf_s[b][:, n0:n1], wf_bf[b][pair])
+            quantize(words, wf_s[b][:, n0:n1], wf_bf[b, pair])
+
+        def quantize_wg(a, t0, t1, rounded):
+            cols = slice(PASS * a + P * t0, PASS * a + P * t1)
+            quantize(wg_w[0][:, cols], wg_s[0][:, cols], rounded)
 
         features(0)
-        rounded = [new(f"wg_bf0{a}", [P, 4 * PASS], BF16) for a in range(2)]
-        round_wg(wg_raw[0, 0], rounded[0][:], 0)
-        quantize(wg_w[0][:, :PASS], wg_s[0][:, :PASS], rounded[0][:])
-        for s in range(4):
-            gate_pass(s, 0)
-        round_wg(wg_raw[0, 1], rounded[1][:], 32)
-        quantize(wg_w[0][:, PASS : PASS + P], wg_s[0][:, PASS : PASS + P], rounded[1][:, :PASS])
-        quantize(wg_w[0][:, PASS + P : PASS + 2 * P], wg_s[0][:, PASS + P : PASS + 2 * P], rounded[1][:, PASS : 2 * PASS])
-        quantize(wg_w[0][:, PASS + 2 * P :], wg_s[0][:, PASS + 2 * P :], rounded[1][:, 2 * PASS :])
-        for s in range(4):
-            gate_pass(s, 1)
-            sigmoid(s)
-        early = new("early", [P, 2 * S], F32, tag="wg_bf01")
-        weigh(0, early[:, :S], banks[4])
-        weigh(1, early[:, S:], banks[5])
-        scatter(0)
+        pairs = {(a, u): new(f"wg_bf0{a}{u}", [P, 2 * PASS], BF16) for a in range(2) for u in range(2)}
+        for u in range(2):
+            round_wg(nc.vector.tensor_copy, wg_raw[0, 0], pairs[0, u][:], 2 * u, 2 * u + 2)
+        for u in range(2):
+            quantize_wg(0, 2 * u, 2 * u + 2, pairs[0, u][:])
+        first_halves = [(banks[3], slice(0, S // 2)), (banks[GATE_BANK[0]], slice(S // 2, S))]
+        for bank, entries in first_halves:
+            gate_pass(0, 0, bank, entries)
+        gate_pass(1, 0)
+        round_wg(nc.vector.tensor_copy, wg_raw[0, 1], pairs[1, 0][:], 0, 2)
+        round_wg(nc.scalar.copy, wg_raw[0, 1], pairs[1, 1][:], 2, 4)
+        for s in range(2):
+            quantize_wg(1, s, s + 1, pairs[1, 0][:, PASS * s : PASS * (s + 1)])
+        gate[0] = row("gate0")
+        for bank, entries in first_halves:
+            gate_pass(0, 1, bank, entries)
+            nc.scalar.activation(gate[0][:, entries], bank[:, entries], ACT.Sigmoid)
+        gate_pass(1, 1)
+        sigmoid(1)
+        for s in range(2):
+            weigh(s, row(f"factor{s}"), banks[4 + s])
+        quantize_wg(1, 2, 4, pairs[1, 1][:])
+        for s in range(2, 4):
+            for a in range(2):
+                gate_pass(s, a)
+        for h in range(2):
+            entries = first_halves[h][1]
+            places = pages[0][:].indirect(idx2[:, S // 32 * h : S // 32 * (h + 1)])
+            nc.vector.tensor_tensor(places, gate[0][:, entries], factor[0][:, entries], MULT)
+        for s in range(2, 4):
+            weigh(s, row(f"factor{s}", f"wg_bf01{s - 2}"), banks[4 + s])
         scatter(1)
         rounded1 = new("wg_bf1", [P, 8 * PASS], BF16)
         for a in range(2):
-            round_wg(wg_raw[1, a], rounded1[:, 4 * PASS * a : 4 * PASS * (a + 1)], P)
+            round_wg(nc.scalar.copy, wg_raw[1, a], rounded1[:, 4 * PASS * a : 4 * PASS * (a + 1)])
         quantize(wg_w[1][:], wg_s[1][:], rounded1[:])
-        weigh(2, row("factor2", "wg_bf1"), banks[4])
+        late_gates = new("late_gates", [P, 3, S], F32, tag="raw11")
+        for s in range(2, 4):
+            sigmoid(s, late_gates[:, s - 2, :])
         scatter(2)
-        weigh(3, gate[2], banks[4])
-        features(1)
+        features(1, late_gates[:, 2, :])
+        for pair in range(2):
+            round_wf(0, pair)
+        wf_w[0, 0] = new("wf_w00", [P, HALF], U32)[:]
+        wf_w[0, 1] = wf_w[0, 0][:, QUARTER:]
+        quantize(wf_w[0, 0], wf_s[0][:, :HALF], wf_front[:])
+        last_gates = new("last_gates", [P, 4, S], F32, tag="wf_raw0_0")
         for s in range(4, 8):
             for a in range(2):
                 gate_pass(s, a)
-            sigmoid(s)
+            sigmoid(s, last_gates[:, s - 4, :])
+        nc.scalar.activation(warm[:, 8:16], gate[7][:, :8], ACT.Silu)
+        behind = new("behind_wf", [P, 5, S], F32, tag="wf_front")
         for s in range(4, 8):
-            weigh(s, row(f"factor{s}"), banks[7 - s])
-        multiply(3, row("weighted3", "tanh10"))
+            weigh(s, behind[:, s - 4, :], banks[7 - s])
+        multiply(3, behind[:, 4, :])
         place(3)
         for s in range(4, 8):
-            multiply(s, gate[s])
-        round_wf(0)
-        low = new("turned_low", [P, 4, QUARTER], F32, tag="wf_raw0")
+            multiply(s, gate[s] if s < 6 else row(f"weighted{s}"))
+        gate_banks = [banks[GATE_BANK[s]] for s in range(4, 8)]
+        factor_banks = [banks[7 - s] for s in range(4, 8)]
+        low = new("turned_low", [P, 4, QUARTER], F32, tag="wg_bf1")
         turned = [[low[:, g, :] for g in range(4)]]
-        add_turned(0, False)
+        add_turned(0, gate_banks)
         for g in range(4):
-            round_turned(turned[0], g)
+            round_turned(turned[0][g], gate_banks[g])
+            if g == 0:
+                round_wf(0, 2)
         place(4)
-        wf_w[0, 0] = new("wf_w00", [P, HALF], U32, tag="gate4")[:]
-        wf_w[0, 1] = wf_w[0, 0][:, QUARTER:]
-        quantize(wf_w[0, 0], wf_s[0][:, :HALF], wf_front)
         place(5)
-        round_wf(1)
-        add_turned(2, True)
+        round_wf(1, 0)
+        add_turned(2, factor_banks)
 
-        load_scale_rows(nc.sync, w8_s, w8_scales)
-        aside = new("aside", [P, T2 + 3 * QUARTER], F32, tag="raw00")
-        first6, late5, first4 = aside[:, :HALF], aside[:, HALF:T2], aside[:, T2:]
+        aside = new("aside", [P, T2], F32, tag="raw00")
+        first6, late5 = aside[:, :HALF], aside[:, HALF:]
         last4 = sums[:, 2, P : P + QUARTER]
         late = {5: late5, 6: sums[:, 1, HALF:T2], 7: sums[:, 2, HALF:T2]}
+        load_slot(4, sums[:, 0, : 3 * QUARTER], 0, 3 * QUARTER)
+        load_slot(5, sums[:, 1, :HALF], 0, HALF)
+        w8_w = new("w8_w", [P, 2, N], U32)
+        nc.sync.dma_start(out=w8_w[:].bitcast(I32), in_=w8_words.rearrange("a p n i -> p a (n i)").bitcast(I32))
+        load_scale_rows(w8_s, w8_scales, 0, N)
         load_slot(6, first6, 0, HALF)
         load_slot(7, sums[:, 3, :HALF], 0, HALF)
         for s in late:
             load_slot(s, late[s], HALF, T2)
-        load_slot(4, first4, 0, 3 * QUARTER)
-        load_slot(5, sums[:, 1, :HALF], 0, HALF)
         load_slot(4, last4, 3 * QUARTER, T2)
 
         def add_slot(engine, s, m0, m1, rows=None):
@@ -308,21 +343,25 @@ def tile_list_feed_slot_ranking_kernel(
         z_bf0 = new("z_bf0", [P, 3 * T2], BF16, tag="raw01")
         woven0 = [sums_tile[:, 2 * STRIP - GAP : 2 * STRIP + HALF - GAP].bitcast(BF16)]
         woven0 += [z_bf0[:, T2 * q : T2 * (q + 1)] for q in range(3)]
-        high = new("turned_high", [P, 3, QUARTER], F32, tag="wf_raw1")
+        high = new("turned_high", [P, 3, QUARTER], F32, tag="wf_raw0_512")
         turned.append([high[:, g, :] for g in range(3)] + [sums[:, 0, 3 * QUARTER : T2]])
         for g in range(4):
-            round_turned(turned[1], g)
+            round_turned(turned[1][g], factor_banks[g])
+            if g == 1:
+                round_wf(1, 1)
         for q in range(4):
+            bank = gate_banks[q % 3]
             for u in range(2):
                 for c in range(2):
                     column = P * (2 * u + c)
-                    nc.tensor.transpose(banks[q][:, column : column + P], turned[u][q][:, P * c : P * (c + 1)], ident[:])
+                    nc.tensor.transpose(bank[:, column : column + P], turned[u][q][:, P * c : P * (c + 1)], ident[:])
             nc.scalar.copy(
-                woven0[q].bitcast(F32).rearrange("p (m u) -> p m u", u=2), banks[q][:].rearrange("p (u m) -> p m u", u=2)
+                woven0[q].bitcast(F32).rearrange("p (m u) -> p m u", u=2), bank[:].rearrange("p (u m) -> p m u", u=2)
             )
-        nc.scalar.activation(warm[:, 8:16], woven0[3][:, T2 - 8 :], ACT.Silu)
+        wf_bf[1, 2] = new("wf_last", [P, T2], BF16, tag="wg_bf1")[:]
+        round_wf(1, 2)
         for m0, m1 in ((0, HALF), (HALF, 3 * QUARTER)):
-            add_slot(nc.gpsimd, 4, m0, m1, first4[:, m0:m1])
+            add_slot(nc.gpsimd, 4, m0, m1)
         add_slot(nc.gpsimd, 5, 0, HALF)
         add_slot(nc.gpsimd, 4, 3 * QUARTER, T2, last4)
         place(6)
@@ -333,7 +372,7 @@ def tile_list_feed_slot_ranking_kernel(
             z_w[0, q] = words
             quantize(words, z_s[0][:, QUARTER * q : QUARTER * (q + 1)], woven0[q])
 
-        after6 = new("after6", [P, HALF], U32, tag="gate6")
+        after6 = new("after6", [P, HALF], U32, tag="weighted6")
         quantize_z0(0, after6[:, :QUARTER])
         quantize_wf(0, 2, after6[:, QUARTER:])
         add_slot(nc.gpsimd, 6, 0, HALF, first6)
@@ -392,7 +431,7 @@ def tile_list_feed_slot_ranking_kernel(
             z_w[1, q] = new(f"z_w1{q}", [P, QUARTER], U32)
         for k in range(3):
             passes(k, 0, 0, QUARTER, True, False)
-        after7 = new("after7", [P, 4, QUARTER], U32, tag="gate7")
+        after7 = new("after7", [P, 4, QUARTER], U32, tag="weighted7")
         quantize_z0(1, after7[:, 3, :])
         passes(3, 0, 0, QUARTER, True, False)
         for m0 in range(0, QUARTER, P):

@@ -27,6 +27,7 @@ HALF = T2 // 2
 QUARTER = T2 // 4
 GAP = 3 * P
 STRIP = T2 + GAP
+VECTOR_SHARE = 88
 GATE_BANK = (6, 7, 4, 5, 6, 7, 4, 5)
 
 
@@ -257,7 +258,10 @@ def tile_list_feed_slot_ranking_kernel(
         for bank, entries in first_halves:
             gate_pass(0, 0, bank, entries)
         gate_pass(1, 0)
-        round_wg(nc.vector.tensor_copy, wg_raw[0, 1], pairs[1, 0][:], 0, 2)
+        first = pairs[1, 0][:].rearrange("p (t m j) -> p m j t", t=2, j=4)
+        source = wg_raw[0, 1][:].rearrange("p j (m t) -> p m j t", t=4)[:, :, :, :2]
+        nc.vector.tensor_copy(first[:, :VECTOR_SHARE], source[:, :VECTOR_SHARE])
+        nc.scalar.copy(first[:, VECTOR_SHARE:], source[:, VECTOR_SHARE:])
         round_wg(nc.scalar.copy, wg_raw[0, 1], pairs[1, 1][:], 2, 4)
         for s in range(2):
             quantize_wg(1, s, s + 1, pairs[1, 0][:, PASS * s : PASS * (s + 1)])
@@ -309,8 +313,8 @@ def tile_list_feed_slot_ranking_kernel(
             multiply(s, gate[s] if s < 6 else row(f"weighted{s}"))
         gate_banks = [banks[GATE_BANK[s]] for s in range(4, 8)]
         factor_banks = [banks[7 - s] for s in range(4, 8)]
-        low = new("turned_low", [P, 4, QUARTER], F32, tag="wg_bf1")
-        turned = [[low[:, g, :] for g in range(4)]]
+        low = new("turned_low", [P, 3, QUARTER], F32, tag="wg_bf1")
+        turned = [[low[:, g, :] for g in range(3)] + [sums[:, 0, 3 * QUARTER :]]]
         add_turned(0, gate_banks)
         for g in range(4):
             round_turned(turned[0][g], gate_banks[g])
@@ -343,14 +347,14 @@ def tile_list_feed_slot_ranking_kernel(
         z_bf0 = new("z_bf0", [P, 3 * T2], BF16, tag="raw01")
         woven0 = [sums_tile[:, 2 * STRIP - GAP : 2 * STRIP + HALF - GAP].bitcast(BF16)]
         woven0 += [z_bf0[:, T2 * q : T2 * (q + 1)] for q in range(3)]
-        high = new("turned_high", [P, 3, QUARTER], F32, tag="wf_raw0_512")
-        turned.append([high[:, g, :] for g in range(3)] + [sums[:, 0, 3 * QUARTER : T2]])
+        high = new("turned_high", [P, 4, QUARTER], F32, tag="wf_raw0_512")
+        turned.append([high[:, g, :] for g in range(4)])
         for g in range(4):
             round_turned(turned[1][g], factor_banks[g])
             if g == 1:
                 round_wf(1, 1)
         for q in range(4):
-            bank = gate_banks[q % 3]
+            bank = gate_banks[q]
             for u in range(2):
                 for c in range(2):
                     column = P * (2 * u + c)

@@ -436,11 +436,11 @@ def tile_list_feed_slot_ranking_kernel(
         for k in range(3):
             passes(k, 0, 0, QUARTER, True, False)
         after7 = new("after7", [P, 4, QUARTER], U32, tag="weighted7")
-        quantize_z0(1, after7[:, 3, :])
-        passes(3, 0, 0, QUARTER, True, False)
         for m0 in range(0, QUARTER, P):
             add_slot(nc.vector, 7, m0, m0 + P)
             round_z(m0, m0 + P)
+        quantize_z0(1, after7[:, 3, :])
+        passes(3, 0, 0, QUARTER, True, False)
         add_slot(nc.vector, 7, QUARTER, HALF)
         quantize_wf(1, 0, after7[:, 0, :])
         round_z(QUARTER, HALF)

@@ -27,7 +27,6 @@ HALF = T2 // 2
 QUARTER = T2 // 4
 GAP = 3 * P
 STRIP = T2 + GAP
-VECTOR_SHARE = 88
 GATE_BANK = (6, 7, 4, 5, 6, 7, 4, 5)
 
 
@@ -49,20 +48,22 @@ def tile_list_feed_slot_ranking_kernel(
         idx2 = lists.tile([P, S // 16], U16, name="idx2")
 
         def load_scale_rows(plane, scales, c0, c1):
-            for q in range(4):
+            for r in range(4):
                 nc.sync.dma_start(
-                    out=plane[32 * q : 32 * q + 4].bitcast(I32),
-                    in_=scales.bitcast(I32)[:, 4 * q : 4 * q + 4, c0 // 4 : c1 // 4].rearrange("a r n -> r a n"),
+                    out=plane[r:P:32].bitcast(I32),
+                    in_=scales.bitcast(I32)[:, r:16:4, c0 // 4 : c1 // 4].rearrange("a q n -> q a n"),
                 )
 
         tab_s = new("tab_s", [P, 2, T], U8)
         w4_s = [new(f"w4_s{b}", [P, 2, PASS], U8) for b in range(2)]
         w8_s = new("w8_s", [P, 2, N], U8)
         warm = new("warm", [P, 16], F32)
+        v_planes = new("v_planes", [P, 2, S], U8)
         nc.vector.memset(tab_s[:].bitcast(I32), 0)
         for plane in w4_s:
             nc.vector.memset(plane[:].bitcast(I32), 0)
         nc.vector.memset(warm[:, 0:8], 0.0)
+        nc.vector.memset(v_planes[:].bitcast(I32), 0)
         nc.vector.memset(w8_s[:].bitcast(I32), 0)
 
         ident = new("ident", [P, P], F32)
@@ -107,19 +108,28 @@ def tile_list_feed_slot_ranking_kernel(
             nc.sync.dma_start(out=words[:].bitcast(I32), in_=part.rearrange("a p n -> p a n"))
             return words
 
-        tab_w = [load_tab(0)]
         nc.sync.dma_start(idx[:], offs)
-        load_scale_rows(tab_s, tab_scales, 0, T)
-        w4_w = [load_w4(0)]
+        tab_w = [load_tab(0)]
+        nc.scalar.dma_start(out=tab_s[0:P:8].bitcast(I32), in_=tab_scales.bitcast(I32).rearrange("a q n -> q a n"))
         load_scale_rows(w4_s[0], w4_scales, 0, PASS)
+        w4_w = [load_w4(0)]
         tab_w.append(load_tab(1))
+        picked_s = new("picked_s", [P, 2, S], U8)
+        for a in range(2):
+            nc.vector.tensor_copy(picked_s[:, a, :], tab_s[:, a, :].indirect(idx[:]))
         nc.scalar.activation(warm[:, 8:16], warm[:, 0:8], ACT.Sigmoid)
-        wg_raw = {(0, 0): load_wg(0, 0)}
-        wg_raw[0, 1] = load_wg(0, 1)
         wgs_sb = new("wgs_sb", [P, S], F32)
         nc.sync.dma_start(out=wgs_sb[:], in_=wgs)
         gain_sb = new("gain_sb", [P, 2, 4], F32)
         nc.sync.dma_start(out=gain_sb[:], in_=gain.rearrange("(b p i) -> p b i", b=2, i=4))
+        for r in range(4):
+            nc.sync.dma_start(out=v_planes[r:P:32].bitcast(I32), in_=picked_s[8 * r : P : 32].bitcast(I32))
+        wg_raw = {(0, 0): load_wg(0, 0)}
+        wg_last = []
+        for h, tag in enumerate(("raw01", "raw01b")):
+            wg_last.append(new(f"wg_raw01{h}", [P, 4, PASS // 2], F32, tag=tag))
+            part = wg[PASS:, PASS // 2 * h : PASS // 2 * (h + 1)]
+            nc.sync.dma_start(out=wg_last[h][:], in_=part.rearrange("(p j) c -> p j c", j=4))
         nc.sync.dma_start(idx2[:], offs2)
         wg_raw[1, 0] = load_wg(1, 0)
         wg_raw[1, 1] = load_wg(1, 1)
@@ -133,15 +143,9 @@ def tile_list_feed_slot_ranking_kernel(
         load_wf(1, 0, N)
 
         v_w = [new(f"v_w{a}", [P, S], U32) for a in range(2)]
-        v_s = [new(f"v_s{a}", [P, S], U8) for a in range(2)]
-        nc.vector.tensor_copy(v_w[0][:], tab_w[0][:].indirect(idx[:]))
+        v_s = [v_planes[:, a, :] for a in range(2)]
         for a in range(2):
-            nc.vector.tensor_copy(v_s[a][:], tab_s[:, a, :].indirect(idx[:]))
-        nc.vector.tensor_copy(v_w[1][:], tab_w[1][:].indirect(idx[:]))
-
-        for tag in ("tab_w0", "tab_s"):
-            pages.append(new(f"page{len(pages)}", [P, T2], F32, tag=tag))
-            nc.gpsimd.memset(pages[-1][:], 0.0)
+            nc.vector.tensor_copy(v_w[a][:], tab_w[a][:].indirect(idx[:]))
 
         def round_wg(copy, raw, rounded, t0=0, t1=4):
             src = raw[:].rearrange("p j (m t) -> p m j t", t=4)
@@ -186,7 +190,8 @@ def tile_list_feed_slot_ranking_kernel(
 
         def gate_pass(s, a, bank=None, entries=slice(0, S)):
             b, t = s // 4, s % 4
-            cols = slice(PASS * a + P * t, PASS * a + P * (t + 1))
+            c0 = PASS * a + P * t if b == 1 else PASS * (t // 2) + 2 * P * a + P * (t % 2)
+            cols = slice(c0, c0 + P)
             bank = banks[GATE_BANK[s]] if bank is None else bank
             mx(
                 bank[:, entries], wg_w[b][:, cols], wg_s[b][:, cols],
@@ -244,36 +249,66 @@ def tile_list_feed_slot_ranking_kernel(
             n0, n1 = QUARTER * pair, QUARTER * (pair + 1)
             quantize(words, wf_s[b][:, n0:n1], wf_bf[b, pair])
 
-        def quantize_wg(a, t0, t1, rounded):
-            cols = slice(PASS * a + P * t0, PASS * a + P * t1)
-            quantize(wg_w[0][:, cols], wg_s[0][:, cols], rounded)
+        def quantize_wg(c0, c1, rounded):
+            quantize(wg_w[0][:, c0:c1], wg_s[0][:, c0:c1], rounded)
 
-        features(0)
-        pairs = {(a, u): new(f"wg_bf0{a}{u}", [P, 2 * PASS], BF16) for a in range(2) for u in range(2)}
-        for u in range(2):
-            round_wg(nc.vector.tensor_copy, wg_raw[0, 0], pairs[0, u][:], 2 * u, 2 * u + 2)
-        for u in range(2):
-            quantize_wg(0, 2 * u, 2 * u + 2, pairs[0, u][:])
+        w4_sorted = new("w4_sorted", [P, 2, 2 * PASS], U8)
+        w4_sorted_s = new("w4_sorted_s", [P, 2, PASS], U8)
+        for a in range(2):
+            nc.scalar.copy(
+                w4_sorted[:, a, :].bitcast(U16).rearrange("p (t m) -> p t m", t=4),
+                w4_w[0][:, a, :].bitcast(U16).rearrange("p (m t) -> p t m", t=4),
+            )
+            nc.gpsimd.tensor_copy(
+                w4_sorted_s[:, a, :].rearrange("p (t m) -> p t m", t=4),
+                w4_s[0][:, a, :].rearrange("p (m t) -> p t m", t=4),
+            )
+        for tag in ("tab_s", "w4_s0"):
+            pages.append(new(f"page{len(pages)}", [P, T2], F32, tag=tag))
+            nc.gpsimd.memset(pages[-1][:], 0.0)
+        for t in range(4):
+            for a in range(2):
+                nc.tensor.matmul_mx(
+                    out=banks[t][:], lhsT=w4_sorted[:, a, 2 * P * t : 2 * P * (t + 1)].bitcast(FP4X4),
+                    lhsT_scale=w4_sorted_s[:, a, P * t : P * (t + 1)], rhs=v_w[a][:].bitcast(FP8X4), rhs_scale=v_s[a][:],
+                    start=a == 0, stop=a == 1,
+                )
+        tanh_rows = [row(f"tanh0{t}") for t in range(4)]
+        for t in range(4):
+            nc.scalar.activation(tanh_rows[t], banks[t][:], ACT.Tanh)
+
+        def weigh_rows(t, dst):
+            factor[t] = dst
+            nc.vector.scalar_tensor_tensor(dst, tanh_rows[t], gain_sb[:, 0, t : t + 1], wgs_sb[:], MULT, MULT)
+
+        for t in range(2):
+            weigh_rows(t, row(f"factor{t}"))
+        pairs = {(a, 0): new(f"wg_bf0{a}0", [P, 2 * PASS], BF16) for a in range(2)}
+        late_pairs = new("wg_bf0_late", [P, 4 * PASS], BF16, tag="tab_w0")
+        round_wg(nc.vector.tensor_copy, wg_raw[0, 0], pairs[0, 0][:], 0, 2)
+        round_wg(nc.scalar.copy, wg_raw[0, 0], late_pairs[:, : 2 * PASS], 2, 4)
+        quantize_wg(0, 2 * P, pairs[0, 0][:])
+        weigh_rows(2, row("factor2", "wg_bf000"))
         first_halves = [(banks[3], slice(0, S // 2)), (banks[GATE_BANK[0]], slice(S // 2, S))]
         for bank, entries in first_halves:
             gate_pass(0, 0, bank, entries)
         gate_pass(1, 0)
         first = pairs[1, 0][:].rearrange("p (t m j) -> p m j t", t=2, j=4)
-        source = wg_raw[0, 1][:].rearrange("p j (m t) -> p m j t", t=4)[:, :, :, :2]
-        nc.vector.tensor_copy(first[:, :VECTOR_SHARE], source[:, :VECTOR_SHARE])
-        nc.scalar.copy(first[:, VECTOR_SHARE:], source[:, VECTOR_SHARE:])
-        round_wg(nc.scalar.copy, wg_raw[0, 1], pairs[1, 1][:], 2, 4)
+        second = late_pairs[:, 2 * PASS :].rearrange("p (t m j) -> p m j t", t=2, j=4)
+        for h in range(2):
+            source = wg_last[h][:].rearrange("p j (m t) -> p m j t", t=4)
+            nc.vector.tensor_copy(first[:, P // 2 * h : P // 2 * (h + 1)], source[:, :, :, :2])
+            nc.scalar.copy(second[:, P // 2 * h : P // 2 * (h + 1)], source[:, :, :, 2:])
         for s in range(2):
-            quantize_wg(1, s, s + 1, pairs[1, 0][:, PASS * s : PASS * (s + 1)])
+            quantize_wg(P * (2 + s), P * (3 + s), pairs[1, 0][:, PASS * s : PASS * (s + 1)])
         gate[0] = row("gate0")
         for bank, entries in first_halves:
             gate_pass(0, 1, bank, entries)
             nc.scalar.activation(gate[0][:, entries], bank[:, entries], ACT.Sigmoid)
         gate_pass(1, 1)
         sigmoid(1)
-        for s in range(2):
-            weigh(s, row(f"factor{s}"), banks[4 + s])
-        quantize_wg(1, 2, 4, pairs[1, 1][:])
+        weigh_rows(3, row("factor3", "wg_bf010"))
+        quantize_wg(PASS, 2 * PASS, late_pairs[:])
         for s in range(2, 4):
             for a in range(2):
                 gate_pass(s, a)
@@ -281,8 +316,6 @@ def tile_list_feed_slot_ranking_kernel(
             entries = first_halves[h][1]
             places = pages[0][:].indirect(idx2[:, S // 32 * h : S // 32 * (h + 1)])
             nc.vector.tensor_tensor(places, gate[0][:, entries], factor[0][:, entries], MULT)
-        for s in range(2, 4):
-            weigh(s, row(f"factor{s}", f"wg_bf01{s - 2}"), banks[4 + s])
         scatter(1)
         rounded1 = new("wg_bf1", [P, 8 * PASS], BF16)
         for a in range(2):

@@ -59,7 +59,7 @@ def tile_list_feed_slot_ranking_kernel(
         w8_s = new("w8_s", [P, 2, N], U8)
         warm = new("warm", [P, 16], F32)
         v_planes = new("v_planes", [P, 2, S], U8)
-        nc.vector.memset(tab_s[:].bitcast(I32), 0)
+        nc.gpsimd.memset(tab_s[:].bitcast(I32), 0)
         for plane in w4_s:
             nc.vector.memset(plane[:].bitcast(I32), 0)
         nc.vector.memset(warm[:, 0:8], 0.0)
@@ -68,9 +68,9 @@ def tile_list_feed_slot_ranking_kernel(
 
         ident = new("ident", [P, P], F32)
         make_identity(nc, ident[:])
-        pages = [new(f"page{i}", [P, T2], F32) for i in range(2)]
-        for page in pages:
-            nc.vector.memset(page[:], 0.0)
+        pages = [new(f"page{i}", [P, T2], F32) for i in range(4)]
+        for i, page in enumerate(pages):
+            (nc.vector if i < 2 else nc.gpsimd).memset(page[:], 0.0)
 
         def load_wg(b, a):
             raw = new(f"wg_raw{b}{a}", [P, 4, PASS], F32, tag=f"raw{b}{a}")
@@ -97,10 +97,12 @@ def tile_list_feed_slot_ranking_kernel(
             for n in range(n0, n1, QUARTER):
                 wf_raw[b, n // QUARTER] = raw[:, :, n - n0 : n - n0 + QUARTER]
 
-        def load_tab(a):
-            words = new(f"tab_w{a}", [P, T], U32)
-            nc.sync.dma_start(out=words[:].bitcast(I32), in_=tab_words[a].rearrange("p t i -> p (t i)").bitcast(I32))
-            return words
+        table = new("table", [P, 2, T], U32, tag="tab_w1")
+        tab_w = [table[:, a, :] for a in range(2)]
+
+        def load_tab(t0, t1):
+            words = tab_words.rearrange("a p t i -> p a (t i)").bitcast(I32)
+            nc.sync.dma_start(out=table[:, :, t0:t1].bitcast(I32), in_=words[:, :, t0:t1])
 
         def load_w4(b):
             words = new(f"w4_w{b}", [P, 2, 2 * PASS], U8)
@@ -109,27 +111,36 @@ def tile_list_feed_slot_ranking_kernel(
             return words
 
         nc.sync.dma_start(idx[:], offs)
-        tab_w = [load_tab(0)]
-        nc.scalar.dma_start(out=tab_s[0:P:8].bitcast(I32), in_=tab_scales.bitcast(I32).rearrange("a q n -> q a n"))
+        load_tab(0, T // 4)
+        nc.sync.dma_start(out=tab_s[0:P:8].bitcast(I32), in_=tab_scales.bitcast(I32).rearrange("a q n -> q a n"))
         load_scale_rows(w4_s[0], w4_scales, 0, PASS)
+        load_tab(T // 4, T)
         w4_w = [load_w4(0)]
-        tab_w.append(load_tab(1))
         picked_s = new("picked_s", [P, 2, S], U8)
         for a in range(2):
             nc.vector.tensor_copy(picked_s[:, a, :], tab_s[:, a, :].indirect(idx[:]))
-        nc.scalar.activation(warm[:, 8:16], warm[:, 0:8], ACT.Sigmoid)
-        wgs_sb = new("wgs_sb", [P, S], F32)
-        nc.sync.dma_start(out=wgs_sb[:], in_=wgs)
-        gain_sb = new("gain_sb", [P, 2, 4], F32)
-        nc.sync.dma_start(out=gain_sb[:], in_=gain.rearrange("(b p i) -> p b i", b=2, i=4))
+        wg_first = []
+
+        def load_wg_half(h, tag):
+            wg_first.append(new(f"wg_raw00{h}", [P, 4, PASS // 2], F32, tag=tag))
+            part = wg[:PASS, PASS // 2 * h : PASS // 2 * (h + 1)]
+            nc.sync.dma_start(out=wg_first[h][:], in_=part.rearrange("(p j) c -> p j c", j=4))
+
+        load_wg_half(0, "raw00")
+        load_wg_half(1, "raw00b")
         for r in range(4):
             nc.sync.dma_start(out=v_planes[r:P:32].bitcast(I32), in_=picked_s[8 * r : P : 32].bitcast(I32))
-        wg_raw = {(0, 0): load_wg(0, 0)}
+        nc.scalar.activation(warm[:, 8:16], warm[:, 0:8], ACT.Sigmoid)
+        wg_raw = {}
         wg_last = []
         for h, tag in enumerate(("raw01", "raw01b")):
             wg_last.append(new(f"wg_raw01{h}", [P, 4, PASS // 2], F32, tag=tag))
             part = wg[PASS:, PASS // 2 * h : PASS // 2 * (h + 1)]
             nc.sync.dma_start(out=wg_last[h][:], in_=part.rearrange("(p j) c -> p j c", j=4))
+        wgs_sb = new("wgs_sb", [P, S], F32)
+        nc.sync.dma_start(out=wgs_sb[:], in_=wgs)
+        gain_sb = new("gain_sb", [P, 2, 4], F32)
+        nc.sync.dma_start(out=gain_sb[:], in_=gain.rearrange("(b p i) -> p b i", b=2, i=4))
         nc.sync.dma_start(idx2[:], offs2)
         wg_raw[1, 0] = load_wg(1, 0)
         wg_raw[1, 1] = load_wg(1, 1)
@@ -145,7 +156,7 @@ def tile_list_feed_slot_ranking_kernel(
         v_w = [new(f"v_w{a}", [P, S], U32) for a in range(2)]
         v_s = [v_planes[:, a, :] for a in range(2)]
         for a in range(2):
-            nc.vector.tensor_copy(v_w[a][:], tab_w[a][:].indirect(idx[:]))
+            nc.vector.tensor_copy(v_w[a][:], tab_w[a].indirect(idx[:]))
 
         def round_wg(copy, raw, rounded, t0=0, t1=4):
             src = raw[:].rearrange("p j (m t) -> p m j t", t=4)
@@ -190,8 +201,7 @@ def tile_list_feed_slot_ranking_kernel(
 
         def gate_pass(s, a, bank=None, entries=slice(0, S)):
             b, t = s // 4, s % 4
-            c0 = PASS * a + P * t if b == 1 else PASS * (t // 2) + 2 * P * a + P * (t % 2)
-            cols = slice(c0, c0 + P)
+            cols = slice(PASS * a + P * t, PASS * a + P * (t + 1))
             bank = banks[GATE_BANK[s]] if bank is None else bank
             mx(
                 bank[:, entries], wg_w[b][:, cols], wg_s[b][:, cols],
@@ -253,74 +263,81 @@ def tile_list_feed_slot_ranking_kernel(
             quantize(wg_w[0][:, c0:c1], wg_s[0][:, c0:c1], rounded)
 
         w4_sorted = new("w4_sorted", [P, 2, 2 * PASS], U8)
-        w4_sorted_s = new("w4_sorted_s", [P, 2, PASS], U8)
+        w4_sorted_s = new("w4_sorted_s", [P, 2, PASS], U8, tag="tab_s")
         for a in range(2):
             nc.scalar.copy(
                 w4_sorted[:, a, :].bitcast(U16).rearrange("p (t m) -> p t m", t=4),
                 w4_w[0][:, a, :].bitcast(U16).rearrange("p (m t) -> p t m", t=4),
             )
-            nc.gpsimd.tensor_copy(
-                w4_sorted_s[:, a, :].rearrange("p (t m) -> p t m", t=4),
-                w4_s[0][:, a, :].rearrange("p (m t) -> p t m", t=4),
+            nc.vector.tensor_copy(
+                w4_sorted_s[:, a, :].rearrange("p (t m) -> p m t", t=4),
+                w4_s[0][:, a, :].rearrange("p (m t) -> p m t", t=4),
             )
-        for tag in ("tab_s", "w4_s0"):
-            pages.append(new(f"page{len(pages)}", [P, T2], F32, tag=tag))
-            nc.gpsimd.memset(pages[-1][:], 0.0)
-        for t in range(4):
+        tanh_rows = [row(f"tanh0{t}") for t in range(4)]
+
+        def feature_rows(t):
             for a in range(2):
                 nc.tensor.matmul_mx(
                     out=banks[t][:], lhsT=w4_sorted[:, a, 2 * P * t : 2 * P * (t + 1)].bitcast(FP4X4),
                     lhsT_scale=w4_sorted_s[:, a, P * t : P * (t + 1)], rhs=v_w[a][:].bitcast(FP8X4), rhs_scale=v_s[a][:],
                     start=a == 0, stop=a == 1,
                 )
-        tanh_rows = [row(f"tanh0{t}") for t in range(4)]
-        for t in range(4):
             nc.scalar.activation(tanh_rows[t], banks[t][:], ACT.Tanh)
 
         def weigh_rows(t, dst):
             factor[t] = dst
             nc.vector.scalar_tensor_tensor(dst, tanh_rows[t], gain_sb[:, 0, t : t + 1], wgs_sb[:], MULT, MULT)
 
-        for t in range(2):
-            weigh_rows(t, row(f"factor{t}"))
-        pairs = {(a, 0): new(f"wg_bf0{a}0", [P, 2 * PASS], BF16) for a in range(2)}
-        late_pairs = new("wg_bf0_late", [P, 4 * PASS], BF16, tag="tab_w0")
-        round_wg(nc.vector.tensor_copy, wg_raw[0, 0], pairs[0, 0][:], 0, 2)
-        round_wg(nc.scalar.copy, wg_raw[0, 0], late_pairs[:, : 2 * PASS], 2, 4)
-        quantize_wg(0, 2 * P, pairs[0, 0][:])
-        weigh_rows(2, row("factor2", "wg_bf000"))
-        first_halves = [(banks[3], slice(0, S // 2)), (banks[GATE_BANK[0]], slice(S // 2, S))]
-        for bank, entries in first_halves:
-            gate_pass(0, 0, bank, entries)
-        gate_pass(1, 0)
-        first = pairs[1, 0][:].rearrange("p (t m j) -> p m j t", t=2, j=4)
-        second = late_pairs[:, 2 * PASS :].rearrange("p (t m j) -> p m j t", t=2, j=4)
+        pairs = {(a, u): new(f"wg_bf0{a}{u}", [P, 2 * PASS], BF16) for a in range(2) for u in range(2)}
+
+        def round_half(copy, a, h, u):
+            dst = pairs[a, u][:].rearrange("p (t m j) -> p m j t", t=2, j=4)[:, P // 2 * h : P // 2 * (h + 1)]
+            raw = (wg_first, wg_last)[a][h]
+            copy(dst, raw[:].rearrange("p j (m t) -> p m j t", t=4)[:, :, :, 2 * u : 2 * u + 2])
+
+        for t in (0, 2):
+            feature_rows(t)
         for h in range(2):
-            source = wg_last[h][:].rearrange("p j (m t) -> p m j t", t=4)
-            nc.vector.tensor_copy(first[:, P // 2 * h : P // 2 * (h + 1)], source[:, :, :, :2])
-            nc.scalar.copy(second[:, P // 2 * h : P // 2 * (h + 1)], source[:, :, :, 2:])
+            round_half(nc.vector.tensor_copy, 0, h, 0)
+            round_half(nc.scalar.copy, 0, h, 1)
+        for u in range(2):
+            quantize_wg(2 * P * u, 2 * P * (u + 1), pairs[0, u][:])
+        for h in range(2):
+            round_half(nc.vector.tensor_copy, 1, h, 0)
         for s in range(2):
-            quantize_wg(P * (2 + s), P * (3 + s), pairs[1, 0][:, PASS * s : PASS * (s + 1)])
+            quantize_wg(PASS + P * s, PASS + P * (s + 1), pairs[1, 0][:, PASS * s : PASS * (s + 1)])
+        first_halves = [(banks[4], slice(0, S // 2)), (banks[GATE_BANK[0]], slice(S // 2, S))]
         gate[0] = row("gate0")
         for bank, entries in first_halves:
-            gate_pass(0, 1, bank, entries)
-            nc.scalar.activation(gate[0][:, entries], bank[:, entries], ACT.Sigmoid)
-        gate_pass(1, 1)
-        sigmoid(1)
-        weigh_rows(3, row("factor3", "wg_bf010"))
-        quantize_wg(PASS, 2 * PASS, late_pairs[:])
-        for s in range(2, 4):
             for a in range(2):
-                gate_pass(s, a)
+                gate_pass(0, a, bank, entries)
+            nc.scalar.activation(gate[0][:, entries], bank[:, entries], ACT.Sigmoid)
+        for t in (0, 2):
+            weigh_rows(t, row(f"factor{t}"))
+        for h in range(2):
+            round_half(nc.vector.tensor_copy, 1, h, 1)
+        for t in (1, 3):
+            feature_rows(t)
+        for a in range(2):
+            gate_pass(1, a)
+        sigmoid(1)
         for h in range(2):
             entries = first_halves[h][1]
             places = pages[0][:].indirect(idx2[:, S // 32 * h : S // 32 * (h + 1)])
             nc.vector.tensor_tensor(places, gate[0][:, entries], factor[0][:, entries], MULT)
-        scatter(1)
-        rounded1 = new("wg_bf1", [P, 8 * PASS], BF16)
+        quantize_wg(PASS + 2 * P, 2 * PASS, pairs[1, 1][:])
+        for s in range(2, 4):
+            for a in range(2):
+                gate_pass(s, a)
+        rounded1 = [new(name, [P, 4 * PASS], BF16) for name in ("wg_bf10", "wg_bf1")]
         for a in range(2):
-            round_wg(nc.scalar.copy, wg_raw[1, a], rounded1[:, 4 * PASS * a : 4 * PASS * (a + 1)])
-        quantize(wg_w[1][:], wg_s[1][:], rounded1[:])
+            round_wg(nc.scalar.copy, wg_raw[1, a], rounded1[a][:])
+        quantize(wg_w[1][:, :PASS], wg_s[1][:, :PASS], rounded1[0][:])
+        odd_factors = new("odd_factors", [P, 2, S], F32, tag="wg_bf10")
+        for t in (1, 3):
+            weigh_rows(t, odd_factors[:, t // 2, :])
+        scatter(1)
+        quantize(wg_w[1][:, PASS:], wg_s[1][:, PASS:], rounded1[1][:])
         late_gates = new("late_gates", [P, 3, S], F32, tag="raw11")
         for s in range(2, 4):
             sigmoid(s, late_gates[:, s - 2, :])

@@ -270,8 +270,8 @@ def tile_list_feed_slot_ranking_kernel(
                 w4_w[0][:, a, :].bitcast(U16).rearrange("p (m t) -> p t m", t=4),
             )
             nc.vector.tensor_copy(
-                w4_sorted_s[:, a, :].rearrange("p (t m) -> p m t", t=4),
-                w4_s[0][:, a, :].rearrange("p (m t) -> p m t", t=4),
+                w4_sorted_s[:, a, :].rearrange("p (t m) -> p t m", t=4),
+                w4_s[0][:, a, :].rearrange("p (m t) -> p t m", t=4),
             )
         tanh_rows = [row(f"tanh0{t}") for t in range(4)]
 

@@ -27,6 +27,7 @@ HALF = T2 // 2
 QUARTER = T2 // 4
 GAP = 3 * P
 STRIP = T2 + GAP
+TABLE_FRONT = 640
 GATE_BANK = (6, 7, 4, 5, 6, 7, 4, 5)
 
 
@@ -59,7 +60,7 @@ def tile_list_feed_slot_ranking_kernel(
         w8_s = new("w8_s", [P, 2, N], U8)
         warm = new("warm", [P, 16], F32)
         v_planes = new("v_planes", [P, 2, S], U8)
-        nc.gpsimd.memset(tab_s[:].bitcast(I32), 0)
+        nc.vector.memset(tab_s[:].bitcast(I32), 0)
         for plane in w4_s:
             nc.vector.memset(plane[:].bitcast(I32), 0)
         nc.vector.memset(warm[:, 0:8], 0.0)
@@ -68,9 +69,9 @@ def tile_list_feed_slot_ranking_kernel(
 
         ident = new("ident", [P, P], F32)
         make_identity(nc, ident[:])
-        pages = [new(f"page{i}", [P, T2], F32) for i in range(4)]
-        for i, page in enumerate(pages):
-            (nc.vector if i < 2 else nc.gpsimd).memset(page[:], 0.0)
+        pages = [new(f"page{i}", [P, T2], F32) for i in range(2)]
+        for page in pages:
+            nc.vector.memset(page[:], 0.0)
 
         def load_wg(b, a):
             raw = new(f"wg_raw{b}{a}", [P, 4, PASS], F32, tag=f"raw{b}{a}")
@@ -111,10 +112,10 @@ def tile_list_feed_slot_ranking_kernel(
             return words
 
         nc.sync.dma_start(idx[:], offs)
-        load_tab(0, T // 4)
+        load_tab(0, TABLE_FRONT)
         nc.sync.dma_start(out=tab_s[0:P:8].bitcast(I32), in_=tab_scales.bitcast(I32).rearrange("a q n -> q a n"))
         load_scale_rows(w4_s[0], w4_scales, 0, PASS)
-        load_tab(T // 4, T)
+        load_tab(TABLE_FRONT, T)
         w4_w = [load_w4(0)]
         picked_s = new("picked_s", [P, 2, S], U8)
         for a in range(2):
@@ -336,6 +337,8 @@ def tile_list_feed_slot_ranking_kernel(
         odd_factors = new("odd_factors", [P, 2, S], F32, tag="wg_bf10")
         for t in (1, 3):
             weigh_rows(t, odd_factors[:, t // 2, :])
+            pages.append(new(f"page{len(pages)}", [P, T2], F32, tag=f"tanh0{t}"))
+            nc.gpsimd.memset(pages[-1][:], 0.0)
         scatter(1)
         quantize(wg_w[1][:, PASS:], wg_s[1][:, PASS:], rounded1[1][:])
         late_gates = new("late_gates", [P, 3, S], F32, tag="raw11")
@@ -457,7 +460,7 @@ def tile_list_feed_slot_ranking_kernel(
         def finish(k):
             q, pair = units[k]
             silu = row(f"silu{k}", f"silu_{k}" if k in (0, 1, 3, 4) else f"gate{k % 4}")
-            result = row(f"result{k}", f"tanh{k // 4 % 2}{k % 4}")
+            result = row(f"result{k}", "result1" if k % 8 == 1 else f"tanh{k // 4 % 2}{k % 4}")
             rows = out[QUARTER * pair : QUARTER * (pair + 1), QUARTER * q : QUARTER * (q + 1)].rearrange("(e p) m -> p e m", e=2)
             if k < last:
                 nc.scalar.activation(silu, bank_of(k, 0, 0)[:], ACT.Silu)

from contextlib import ExitStack

import concourse.mybir as mybir
from concourse.masks import make_identity

K, T, S, H, T2, N = 1024, 2048, 512, 1024, 1024, 768
FLOPS = 2 * (2 * K * H * S + 2 * H * N * T2)

F32 = mybir.dt.float32
BF16 = mybir.dt.bfloat16
I32 = mybir.dt.int32
U32 = mybir.dt.uint32
U16 = mybir.dt.uint16
U8 = mybir.dt.uint8
FP8X4 = mybir.dt.float8_e4m3fn_x4
FP4X4 = mybir.dt.float4_e2m1fn_x4
ACT = mybir.ActivationFunctionType
MULT = mybir.AluOpType.mult
ADD = mybir.AluOpType.add

P = 128
PASS = 512
BANK = 512
AL = 64
PAGE_OF = (0, 1, 2, 3, 0, 1, 2, 0)
HALF = T2 // 2
QUARTER = T2 // 4
GAP = 3 * P
STRIP = T2 + GAP
TABLE_FRONT = 640
GATE_BANK = (6, 7, 4, 5, 6, 7, 4, 5)


def tile_list_feed_slot_ranking_kernel(
    tc, tab_words, tab_scales, offs, wg, w4_words, w4_scales, gain, wgs, offs2, slot, w8_words, w8_scales, wf, out
):
    nc = tc.nc
    with ExitStack() as ctx:
        lists = ctx.enter_context(tc.tile_pool(name="lists", bufs=1))
        sb = ctx.enter_context(tc.tile_pool(name="sb", bufs=1))
        psum = ctx.enter_context(tc.psum_pool(name="psum", bufs=1))

        def new(name, shape, dtype, tag=None):
            return sb.tile(shape, dtype, name=name, tag=tag or name, align_bytes=AL)

        banks = [psum.tile([P, BANK], F32, name=f"bank{i}") for i in range(8)]

        idx = lists.tile([P, S // 16], U16, name="idx")
        idx2 = lists.tile([P, S // 16], U16, name="idx2")

        def load_scale_rows(plane, scales, c0, c1):
            for r in range(4):
                nc.sync.dma_start(
                    out=plane[r:P:32].bitcast(I32),
                    in_=scales.bitcast(I32)[:, r:16:4, c0 // 4 : c1 // 4].rearrange("a q n -> q a n"),
                )

        tab_s = new("tab_s", [P, 2, T], U8)
        w4_s = [new(f"w4_s{b}", [P, 2, PASS], U8) for b in range(2)]
        w8_s = new("w8_s", [P, 2, N], U8)
        warm = new("warm", [P, 16], F32)
        v_planes = new("v_planes", [P, 2, S], U8)
        nc.vector.memset(tab_s[:].bitcast(I32), 0)
        for plane in w4_s:
            nc.vector.memset(plane[:].bitcast(I32), 0)
        nc.vector.memset(warm[:, 0:8], 0.0)
        nc.vector.memset(v_planes[:].bitcast(I32), 0)
        nc.vector.memset(w8_s[:].bitcast(I32), 0)

        ident = new("ident", [P, P], F32)
        make_identity(nc, ident[:])
        pages = [new(f"page{i}", [P, T2], F32) for i in range(2)]
        for page in pages:
            nc.vector.memset(page[:], 0.0)

        def load_wg(b, a):
            raw = new(f"wg_raw{b}{a}", [P, 4, PASS], F32, tag=f"raw{b}{a}")
            nc.sync.dma_start(
                out=raw[:],
                in_=wg[PASS * a : PASS * (a + 1), PASS * b : PASS * (b + 1)].rearrange("(p j) c -> p j c", j=4),
            )
            return raw

        def load_slot(s, dst, m0=0, m1=T2):
            rows = slot[PASS * (s // 4) : PASS * (s // 4 + 1), m0:m1].rearrange("(p i) m -> p i m", i=4)
            nc.sync.dma_start(out=dst, in_=rows[:, s % 4, :])

        slot_sb = {}

        def load_slots(first):
            for s in range(first, first + 2):
                slot_sb[s] = new(f"slot{s}", [P, T2], F32)
                load_slot(s, slot_sb[s][:])

        def load_wf(b, n0, n1):
            raw = new(f"wf_raw{b}_{n0}", [P, 4, n1 - n0], F32)
            nc.sync.dma_start(out=raw[:], in_=wf[PASS * b : PASS * (b + 1), n0:n1].rearrange("(p j) c -> p j c", j=4))
            for n in range(n0, n1, QUARTER):
                wf_raw[b, n // QUARTER] = raw[:, :, n - n0 : n - n0 + QUARTER]

        table = new("table", [P, 2, T], U32, tag="tab_w1")
        tab_w = [table[:, a, :] for a in range(2)]

        def load_tab(t0, t1):
            words = tab_words.rearrange("a p t i -> p a (t i)").bitcast(I32)
            nc.sync.dma_start(out=table[:, :, t0:t1].bitcast(I32), in_=words[:, :, t0:t1])

        def load_w4(b):
            words = new(f"w4_w{b}", [P, 2, 2 * PASS], U8)
            part = w4_words.bitcast(I32)[:, :, PASS // 2 * b : PASS // 2 * (b + 1)]
            nc.sync.dma_start(out=words[:].bitcast(I32), in_=part.rearrange("a p n -> p a n"))
            return words

        nc.sync.dma_start(idx[:], offs)
        load_tab(0, TABLE_FRONT)
        nc.sync.dma_start(out=tab_s[0:P:8].bitcast(I32), in_=tab_scales.bitcast(I32).rearrange("a q n -> q a n"))
        load_scale_rows(w4_s[0], w4_scales, 0, PASS)
        load_tab(TABLE_FRONT, T)
        w4_w = [load_w4(0)]
        picked_s = new("picked_s", [P, 2, S], U8)
        for a in range(2):
            nc.vector.tensor_copy(picked_s[:, a, :], tab_s[:, a, :].indirect(idx[:]))
        wg_first = []

        def load_wg_half(h, tag):
            wg_first.append(new(f"wg_raw00{h}", [P, 4, PASS // 2], F32, tag=tag))
            part = wg[:PASS, PASS // 2 * h : PASS // 2 * (h + 1)]
            nc.sync.dma_start(out=wg_first[h][:], in_=part.rearrange("(p j) c -> p j c", j=4))

        load_wg_half(0, "raw00")
        load_wg_half(1, "raw00b")
        for r in range(4):
            nc.sync.dma_start(out=v_planes[r:P:32].bitcast(I32), in_=picked_s[8 * r : P : 32].bitcast(I32))
        nc.scalar.activation(warm[:, 8:16], warm[:, 0:8], ACT.Sigmoid)
        wg_raw = {}
        wg_last = []
        for h, tag in enumerate(("raw01", "raw01b")):
            wg_last.append(new(f"wg_raw01{h}", [P, 4, PASS // 2], F32, tag=tag))
            part = wg[PASS:, PASS // 2 * h : PASS // 2 * (h + 1)]
            nc.sync.dma_start(out=wg_last[h][:], in_=part.rearrange("(p j) c -> p j c", j=4))
        wgs_sb = new("wgs_sb", [P, S], F32)
        nc.sync.dma_start(out=wgs_sb[:], in_=wgs)
        gain_sb = new("gain_sb", [P, 2, 4], F32)
        nc.sync.dma_start(out=gain_sb[:], in_=gain.rearrange("(b p i) -> p b i", b=2, i=4))
        nc.sync.dma_start(idx2[:], offs2)
        wg_raw[1, 0] = load_wg(1, 0)
        wg_raw[1, 1] = load_wg(1, 1)
        w4_w.append(load_w4(1))
        load_scale_rows(w4_s[1], w4_scales, PASS, H)
        wf_raw = {}
        load_wf(0, 0, HALF)
        load_slots(0)
        load_wf(0, HALF, N)
        load_slots(2)
        load_wf(1, 0, N)

        v_w = [new(f"v_w{a}", [P, S], U32) for a in range(2)]
        v_s = [v_planes[:, a, :] for a in range(2)]
        for a in range(2):
            nc.vector.tensor_copy(v_w[a][:], tab_w[a].indirect(idx[:]))

        def round_wg(copy, raw, rounded, t0=0, t1=4):
            src = raw[:].rearrange("p j (m t) -> p m j t", t=4)
            copy(rounded.rearrange("p (t m j) -> p m j t", t=t1 - t0, j=4), src[:, :, :, t0:t1])

        def quantize(words, plane, rounded):
            nc.vector.quantize_mx(out=words.bitcast(FP8X4), scales=plane, in_=rounded)

        def mx(bank, lhs_w, lhs_s, rhs, rhs_s, start, stop):
            nc.tensor.matmul_mx(
                out=bank, lhsT=lhs_w.bitcast(FP8X4), lhsT_scale=lhs_s, rhs=rhs, rhs_scale=rhs_s, start=start, stop=stop
            )

        wg_w = [new(f"wg_w{b}", [P, 2 * PASS], U32) for b in range(2)]
        wg_s = [new(f"wg_s{b}", [P, 2 * PASS], U8) for b in range(2)]
        tanh_b, factor, gate, weighted = {}, {}, {}, {}

        def features(b, first=None):
            for a in range(2):
                for jb in range(4):
                    entries = slice(P * jb, P * (jb + 1))
                    mx(
                        banks[jb][:], v_w[a][:, entries], v_s[a][:, entries], w4_w[b][:, a, :].bitcast(FP4X4),
                        w4_s[b][:, a, :], a == 0, a == 1,
                    )
            for jb in range(4):
                if jb == 0 and first is not None:
                    tanh_b[b, jb] = first.rearrange("j (t m) -> j t m", t=4)
                else:
                    tanh_b[b, jb] = new(f"tanh{b}{jb}", [P, 4, P], F32)[:]
                nc.scalar.activation(tanh_b[b, jb], banks[jb][:].rearrange("j (m t) -> j t m", t=4), ACT.Tanh)

        def weigh(s, dst, bank):
            b, t = s // 4, s % 4
            for jb in range(4):
                nc.tensor.transpose(bank[:, P * jb : P * (jb + 1)], tanh_b[b, jb][:, t, :], ident[:])
            factor[s] = dst
            nc.vector.scalar_tensor_tensor(dst, bank[:], gain_sb[:, b, t : t + 1], wgs_sb[:], MULT, MULT)

        def row(name, tag=None):
            return new(name, [P, S], F32, tag=tag)[:]

        def gate_pass(s, a, bank=None, entries=slice(0, S)):
            b, t = s // 4, s % 4
            cols = slice(PASS * a + P * t, PASS * a + P * (t + 1))
            bank = banks[GATE_BANK[s]] if bank is None else bank
            mx(
                bank[:, entries], wg_w[b][:, cols], wg_s[b][:, cols],
                v_w[a][:, entries].bitcast(FP8X4), v_s[a][:, entries], a == 0, a == 1,
            )

        def sigmoid(s, dst=None):
            gate[s] = row(f"gate{s}") if dst is None else dst
            nc.scalar.activation(gate[s], banks[GATE_BANK[s]][:], ACT.Sigmoid)

        def scatter(s):
            nc.vector.tensor_tensor(pages[PAGE_OF[s]][:].indirect(idx2[:]), gate[s], factor[s], MULT)

        def multiply(s, dst):
            weighted[s] = dst
            nc.gpsimd.tensor_tensor(dst, gate[s], factor[s], MULT)

        def place(s):
            nc.vector.tensor_copy(pages[PAGE_OF[s]][:].indirect(idx2[:]), weighted[s])

        def add_turned(first, group):
            for c, step in [(2 * g + e, step) for g in range(4) for step in range(4) for e in range(2)]:
                s = first + step % 2
                if step >= 2:
                    source = slot_sb[s][:, P * c : P * (c + 1)]
                else:
                    source = pages[PAGE_OF[s]][:, P * c : P * (c + 1)]
                column = P * (2 * (c % 2) + step % 2)
                nc.tensor.matmul(
                    group[c // 2][:, column : column + P], source, ident[:],
                    start=(step == 0 and c % 2 == 0), stop=(step == 3 and c % 2 == 1), is_transpose=True,
                )

        def round_turned(turned, bank):
            dst = turned.bitcast(BF16).rearrange("m (c p e) -> m c p e", c=2, e=2)
            nc.scalar.copy(dst, bank[:].rearrange("m (c e p) -> m c p e", c=2, e=2))

        sums_tile = new("sums", [P, 4 * STRIP], F32, tag="tab_w1")
        sums = sums_tile[:].rearrange("p (t m) -> p t m", t=4)[:, :, :T2]
        wf_front = new("wf_front", [P, 2 * T2], BF16)
        wf_rest = new("wf_rest", [P, 3, T2], BF16)
        wf_bf = {(0, 0): wf_front[:, :T2], (0, 1): wf_front[:, T2:], (0, 2): wf_rest[:, 0, :]}
        wf_bf.update({(1, pair): wf_rest[:, 1 + pair, :] for pair in range(2)})
        wf_w = {}
        wf_s = [new(f"wf_s{b}", [P, N], U8) for b in range(2)]

        def weave(copy, dst, src):
            copy(dst.rearrange("p (c i j) -> p c j i", i=4, j=4), src.rearrange("p j (c i) -> p c j i", i=4))

        def round_wf(b, pair):
            weave(nc.scalar.copy, wf_bf[b, pair], wf_raw[b, pair])

        def quantize_wf(b, pair, words):
            wf_w[b, pair] = words
            n0, n1 = QUARTER * pair, QUARTER * (pair + 1)
            quantize(words, wf_s[b][:, n0:n1], wf_bf[b, pair])

        def quantize_wg(c0, c1, rounded):
            quantize(wg_w[0][:, c0:c1], wg_s[0][:, c0:c1], rounded)

        w4_sorted = new("w4_sorted", [P, 2, 2 * PASS], U8)
        w4_sorted_s = new("w4_sorted_s", [P, 2, PASS], U8, tag="tab_s")
        for a in range(2):
            nc.scalar.copy(
                w4_sorted[:, a, :].bitcast(U16).rearrange("p (t m) -> p t m", t=4),
                w4_w[0][:, a, :].bitcast(U16).rearrange("p (m t) -> p t m", t=4),
            )
            nc.vector.tensor_copy(
                w4_sorted_s[:, a, :].rearrange("p (t m) -> p t m", t=4),
                w4_s[0][:, a, :].rearrange("p (m t) -> p t m", t=4),
            )
        tanh_rows = [row(f"tanh0{t}") for t in range(4)]

        def feature_rows(t):
            for a in range(2):
                nc.tensor.matmul_mx(
                    out=banks[t][:], lhsT=w4_sorted[:, a, 2 * P * t : 2 * P * (t + 1)].bitcast(FP4X4),
                    lhsT_scale=w4_sorted_s[:, a, P * t : P * (t + 1)], rhs=v_w[a][:].bitcast(FP8X4), rhs_scale=v_s[a][:],
                    start=a == 0, stop=a == 1,
                )
            nc.scalar.activation(tanh_rows[t], banks[t][:], ACT.Tanh)

        def weigh_rows(t, dst):
            factor[t] = dst
            nc.vector.scalar_tensor_tensor(dst, tanh_rows[t], gain_sb[:, 0, t : t + 1], wgs_sb[:], MULT, MULT)

        pairs = {(a, u): new(f"wg_bf0{a}{u}", [P, 2 * PASS], BF16) for a in range(2) for u in range(2)}

        def round_half(copy, a, h, u):
            dst = pairs[a, u][:].rearrange("p (t m j) -> p m j t", t=2, j=4)[:, P // 2 * h : P // 2 * (h + 1)]
            raw = (wg_first, wg_last)[a][h]
            copy(dst, raw[:].rearrange("p j (m t) -> p m j t", t=4)[:, :, :, 2 * u : 2 * u + 2])

        for t in (0, 2):
            feature_rows(t)
        for h in range(2):
            round_half(nc.vector.tensor_copy, 0, h, 0)
            round_half(nc.scalar.copy, 0, h, 1)
        for u in range(2):
            quantize_wg(2 * P * u, 2 * P * (u + 1), pairs[0, u][:])
        for h in range(2):
            round_half(nc.vector.tensor_copy, 1, h, 0)
        for s in range(2):
            quantize_wg(PASS + P * s, PASS + P * (s + 1), pairs[1, 0][:, PASS * s : PASS * (s + 1)])
        first_halves = [(banks[4], slice(0, S // 2)), (banks[GATE_BANK[0]], slice(S // 2, S))]
        gate[0] = row("gate0")
        for bank, entries in first_halves:
            for a in range(2):
                gate_pass(0, a, bank, entries)
            nc.scalar.activation(gate[0][:, entries], bank[:, entries], ACT.Sigmoid)
        for t in (0, 2):
            weigh_rows(t, row(f"factor{t}"))
        for h in range(2):
            round_half(nc.vector.tensor_copy, 1, h, 1)
        for t in (1, 3):
            feature_rows(t)
        for a in range(2):
            gate_pass(1, a)
        sigmoid(1)
        for h in range(2):
            entries = first_halves[h][1]
            places = pages[0][:].indirect(idx2[:, S // 32 * h : S // 32 * (h + 1)])
            nc.vector.tensor_tensor(places, gate[0][:, entries], factor[0][:, entries], MULT)
        quantize_wg(PASS + 2 * P, 2 * PASS, pairs[1, 1][:])
        for s in range(2, 4):
            for a in range(2):
                gate_pass(s, a)
        rounded1 = [new(name, [P, 4 * PASS], BF16) for name in ("wg_bf10", "wg_bf1")]
        for a in range(2):
            round_wg(nc.scalar.copy, wg_raw[1, a], rounded1[a][:])
        quantize(wg_w[1][:, :PASS], wg_s[1][:, :PASS], rounded1[0][:])
        odd_factors = new("odd_factors", [P, 2, S], F32, tag="wg_bf10")
        for t in (1, 3):
            weigh_rows(t, odd_factors[:, t // 2, :])
            pages.append(new(f"page{len(pages)}", [P, T2], F32, tag=f"tanh0{t}"))
            nc.gpsimd.memset(pages[-1][:], 0.0)
        scatter(1)
        quantize(wg_w[1][:, PASS:], wg_s[1][:, PASS:], rounded1[1][:])
        late_gates = new("late_gates", [P, 3, S], F32, tag="raw11")
        for s in range(2, 4):
            sigmoid(s, late_gates[:, s - 2, :])
        scatter(2)
        features(1, late_gates[:, 2, :])
        for pair in range(2):
            round_wf(0, pair)
        wf_w[0, 0] = new("wf_w00", [P, HALF], U32)[:]
        wf_w[0, 1] = wf_w[0, 0][:, QUARTER:]
        quantize(wf_w[0, 0], wf_s[0][:, :HALF], wf_front[:])
        last_gates = new("last_gates", [P, 4, S], F32, tag="wf_raw0_0")
        for s in range(4, 8):
            for a in range(2):
                gate_pass(s, a)
            sigmoid(s, last_gates[:, s - 4, :])
        nc.scalar.activation(warm[:, 8:16], gate[7][:, :8], ACT.Silu)
        behind = new("behind_wf", [P, 5, S], F32, tag="wf_front")
        for s in range(4, 8):
            weigh(s, behind[:, s - 4, :], banks[7 - s])
        multiply(3, behind[:, 4, :])
        place(3)
        for s in range(4, 8):
            multiply(s, gate[s] if s < 6 else row(f"weighted{s}"))
        gate_banks = [banks[GATE_BANK[s]] for s in range(4, 8)]
        factor_banks = [banks[7 - s] for s in range(4, 8)]
        low = new("turned_low", [P, 3, QUARTER], F32, tag="wg_bf1")
        turned = [[low[:, g, :] for g in range(3)] + [sums[:, 0, 3 * QUARTER :]]]
        add_turned(0, gate_banks)
        for g in range(4):
            round_turned(turned[0][g], gate_banks[g])
            if g == 0:
                round_wf(0, 2)
        place(4)
        place(5)
        round_wf(1, 0)
        add_turned(2, factor_banks)

        aside = new("aside", [P, T2], F32, tag="raw00")
        first6, late5 = aside[:, :HALF], aside[:, HALF:]
        last4 = sums[:, 2, P : P + QUARTER]
        late = {5: late5, 6: sums[:, 1, HALF:T2], 7: sums[:, 2, HALF:T2]}
        load_slot(4, sums[:, 0, : 3 * QUARTER], 0, 3 * QUARTER)
        load_slot(5, sums[:, 1, :HALF], 0, HALF)
        w8_w = new("w8_w", [P, 2, N], U32)
        nc.sync.dma_start(out=w8_w[:].bitcast(I32), in_=w8_words.rearrange("a p n i -> p a (n i)").bitcast(I32))
        load_scale_rows(w8_s, w8_scales, 0, N)
        load_slot(6, first6, 0, HALF)
        load_slot(7, sums[:, 3, :HALF], 0, HALF)
        for s in late:
            load_slot(s, late[s], HALF, T2)
        load_slot(4, last4, 3 * QUARTER, T2)

        def add_slot(engine, s, m0, m1, rows=None):
            dst = sums[:, s % 4, m0:m1]
            engine.tensor_tensor(dst, pages[PAGE_OF[s]][:, m0:m1], dst if rows is None else rows, ADD)

        z_bf0 = new("z_bf0", [P, 3 * T2], BF16, tag="raw01")
        woven0 = [sums_tile[:, 2 * STRIP - GAP : 2 * STRIP + HALF - GAP].bitcast(BF16)]
        woven0 += [z_bf0[:, T2 * q : T2 * (q + 1)] for q in range(3)]
        high = new("turned_high", [P, 4, QUARTER], F32, tag="wf_raw0_512")
        turned.append([high[:, g, :] for g in range(4)])
        for g in range(4):
            round_turned(turned[1][g], factor_banks[g])
            if g == 1:
                round_wf(1, 1)
        for q in range(4):
            bank = gate_banks[q]
            for u in range(2):
                for c in range(2):
                    column = P * (2 * u + c)
                    nc.tensor.transpose(bank[:, column : column + P], turned[u][q][:, P * c : P * (c + 1)], ident[:])
            nc.scalar.copy(
                woven0[q].bitcast(F32).rearrange("p (m u) -> p m u", u=2), bank[:].rearrange("p (u m) -> p m u", u=2)
            )
        wf_bf[1, 2] = new("wf_last", [P, T2], BF16, tag="wg_bf1")[:]
        round_wf(1, 2)
        for m0, m1 in ((0, HALF), (HALF, 3 * QUARTER)):
            add_slot(nc.gpsimd, 4, m0, m1)
        add_slot(nc.gpsimd, 5, 0, HALF)
        add_slot(nc.gpsimd, 4, 3 * QUARTER, T2, last4)
        place(6)
        z_s = [new(f"z_s{b}", [P, T2], U8) for b in range(2)]
        z_w = {}

        def quantize_z0(q, words):
            z_w[0, q] = words
            quantize(words, z_s[0][:, QUARTER * q : QUARTER * (q + 1)], woven0[q])

        after6 = new("after6", [P, HALF], U32, tag="weighted6")
        quantize_z0(0, after6[:, :QUARTER])
        quantize_wf(0, 2, after6[:, QUARTER:])
        add_slot(nc.gpsimd, 6, 0, HALF, first6)
        place(7)

        units = [(q, pair) for q in range(4) for pair in range(N // QUARTER)]
        last = len(units) - 1

        def bank_of(k, i, e):
            if k == last and e == 1:
                return banks[i]
            return banks[2 * (k % 4) + i]

        def product(k, b, i, e, c0, c1, start, stop):
            q, pair = units[k]
            cols = slice(QUARTER * pair + P * e, QUARTER * pair + P * (e + 1))
            words, plane = ((wf_w[b, pair][:, P * e : P * (e + 1)], wf_s[b][:, cols]), (w8_w[:, b, cols], w8_s[:, b, cols]))[i]
            mx(
                bank_of(k, i, e)[:, QUARTER * e + c0 : QUARTER * e + c1], words, plane,
                z_w[b, q][:, c0:c1].bitcast(FP8X4), z_s[b][:, QUARTER * q + c0 : QUARTER * q + c1], start, stop,
            )

        def passes(k, b, c0, c1, first, final):
            for i in range(2):
                for e in range(2):
                    product(k, b, i, e, c0, c1, first and e == 0, final and e == 1)

        def finish(k):
            q, pair = units[k]
            silu = row(f"silu{k}", f"silu_{k}" if k in (0, 1, 3, 4) else f"gate{k % 4}")
            result = row(f"result{k}", "result1" if k % 8 == 1 else f"tanh{k // 4 % 2}{k % 4}")
            rows = out[QUARTER * pair : QUARTER * (pair + 1), QUARTER * q : QUARTER * (q + 1)].rearrange("(e p) m -> p e m", e=2)
            if k < last:
                nc.scalar.activation(silu, bank_of(k, 0, 0)[:], ACT.Silu)
                nc.vector.tensor_tensor(result, bank_of(k, 1, 0)[:], silu, MULT)
                nc.sync.dma_start(out=rows, in_=result.rearrange("p (e m) -> p e m", e=2))
                return
            halves = [slice(QUARTER * e, QUARTER * (e + 1)) for e in range(2)]
            for e in range(2):
                nc.scalar.activation(silu[:, halves[e]], bank_of(k, 0, e)[:, halves[e]], ACT.Silu)
            for e in range(2):
                nc.vector.tensor_tensor(result[:, halves[e]], bank_of(k, 1, e)[:, halves[e]], silu[:, halves[e]], MULT)
                nc.sync.dma_start(out=rows[:, e, :], in_=result[:, halves[e]])

        front1 = new("woven1_front", [P, 4 * HALF], BF16, tag="raw10")
        woven1 = {m0: front1[:, 4 * m0 : 4 * m1] for m0, m1 in ((0, P), (P, QUARTER), (QUARTER, HALF))}

        def round_z(m0, m1):
            weave(nc.scalar.copy, woven1[m0], sums[:, :, m0:m1])

        def quantize_z1(m0, m1):
            q = m0 // QUARTER
            quantize(z_w[1, q][:, m0 - QUARTER * q : m1 - QUARTER * q], z_s[1][:, m0:m1], woven1[m0])

        for q in range(4):
            z_w[1, q] = new(f"z_w1{q}", [P, QUARTER], U32)
        for k in range(3):
            passes(k, 0, 0, QUARTER, True, False)
        after7 = new("after7", [P, 4, QUARTER], U32, tag="weighted7")
        for m0 in range(0, QUARTER, P):
            add_slot(nc.vector, 7, m0, m0 + P)
            round_z(m0, m0 + P)
        quantize_z0(1, after7[:, 3, :])
        passes(3, 0, 0, QUARTER, True, False)
        add_slot(nc.vector, 7, QUARTER, HALF)
        quantize_wf(1, 0, after7[:, 0, :])
        round_z(QUARTER, HALF)
        quantize_z1(0, P)
        quantize_wf(1, 1, after7[:, 1, :])
        quantize_wf(1, 2, after7[:, 2, :])
        for k in range(3):
            passes(k, 1, 0, P, False, False)
        quantize_z1(P, QUARTER)
        for k in range(3):
            passes(k, 1, P, QUARTER, False, True)
        quantize_z1(QUARTER, HALF)
        passes(3, 1, 0, QUARTER, False, True)
        for k in range(len(units)):
            q, pair = units[k]
            if k >= 4:
                for i in range(2):
                    if k == last:
                        for e in range(2):
                            for b in range(2):
                                product(k, b, i, e, 0, QUARTER, b == 0, b == 1)
                        continue
                    for b in range(2):
                        for e in range(2):
                            product(k, b, i, e, 0, QUARTER, b == 0 and e == 0, b == 1 and e == 1)
            finish(k)
            if k in (0, 3):
                ahead = 2 + k // 3
                m0, m1 = QUARTER * ahead, QUARTER * (ahead + 1)
                for s in (7, 6, 5):
                    add_slot(nc.vector, s, m0, m1, late[s][:, m0 - HALF : m1 - HALF])
            if k in (1, 4):
                ahead = 2 + k // 3
                woven1[QUARTER * ahead] = new(f"woven1_{ahead}", [P, T2], BF16, tag=f"silu_{k - 1}")[:]
                round_z(QUARTER * ahead, QUARTER * (ahead + 1))
                quantize_z0(ahead, new(f"z_w0{ahead}", [P, QUARTER], U32, tag=f"silu_{k}")[:])
                quantize_z1(QUARTER * ahead, QUARTER * (ahead + 1))
